import numpy as np
import ml_dtypes


def mxq(x, axis, fmt="e4m3"):
    dtype, down = {"e4m3": (ml_dtypes.float8_e4m3fn, 7), "e5m2": (ml_dtypes.float8_e5m2, 14)}[fmt]
    v = np.moveaxis(np.asarray(x, np.float32).astype(ml_dtypes.bfloat16).astype(np.float64), axis, -1)
    blocks = v.reshape(v.shape[:-1] + (-1, 32))
    amax = np.abs(blocks).max(-1, keepdims=True)
    byte = np.maximum(np.where(amax > 0, np.frexp(amax)[1] - 1 + 127, 0) - down, 1)
    scale = np.exp2(byte - 127.0)
    codes = (blocks / scale).astype(np.float32).astype(dtype).astype(np.float64)
    return np.moveaxis((codes * scale).reshape(v.shape), -1, axis)


WIDE = False


def mx_kscale(k):
    if not WIDE:
        return np.ones(k)
    levels = np.array([10, -10, 5, -5, 0])
    if k % 512:
        return np.exp2(np.random.permutation(np.resize(levels, k // 32))).repeat(32)
    a = np.empty((k // 512, 16))
    for p in range(k // 512):
        a[p, :8] = np.random.permutation(np.resize(levels, 8))
        for g in range(8):
            far = levels[np.abs(levels - a[p, g]) >= 10]
            a[p, g + 8] = far[np.random.randint(len(far))]
    return np.exp2(a.ravel()).repeat(32)


BF16 = ml_dtypes.bfloat16


def bf(x):
    return np.asarray(x, np.float32).astype(BF16)


def f64(x):
    return np.asarray(x).astype(np.float64)


E2M1 = np.array([0.0, 0.5, 1.0, 1.5, 2.0, 3.0, 4.0, 6.0, -0.0, -0.5, -1.0, -1.5, -2.0, -3.0, -4.0, -6.0])


def pack_weight(w, fmt):
    k, n = w.shape
    w = f64(bf(w)).reshape(k // 32, 32, n)
    amax = np.abs(w).max(1)
    if fmt == "e4m3":
        byte = np.frexp(amax)[1] - 1 + 127 - 7
    else:
        mant, ex = np.frexp(amax / 6.0)
        byte = np.where(mant > 0.5, ex, ex - 1) + 127
    byte = np.clip(np.where(amax > 0, byte, 1), 1, 254)
    scaled = (w * np.exp2(127.0 - byte)[:, None, :]).reshape(k, n).astype(np.float32)
    by_word = np.ascontiguousarray(scaled.reshape(k // 512, 128, 4, n).transpose(0, 1, 3, 2))
    if fmt == "e4m3":
        words = by_word.astype(ml_dtypes.float8_e4m3fn).view(np.uint8)
    else:
        c = by_word.astype(ml_dtypes.float4_e2m1fn).view(np.uint8) & 0xF
        words = c[..., 0::2] | (c[..., 1::2] << 4)
    return np.ascontiguousarray(words), np.ascontiguousarray(byte.astype(np.uint8).reshape(k // 512, 16, n))


def unpack_weight(words, scales, fmt):
    g, p, n, _ = words.shape
    if fmt == "e4m3":
        vals = np.ascontiguousarray(words).view(ml_dtypes.float8_e4m3fn).astype(np.float64)
    else:
        nib = np.empty((g, p, n, 4), np.uint8)
        nib[..., 0::2] = words & 0xF
        nib[..., 1::2] = words >> 4
        vals = E2M1[nib]
    vals = vals * np.repeat(np.exp2(scales.astype(np.float64) - 127.0), 8, axis=1)[..., None]
    return vals.transpose(0, 1, 3, 2).reshape(g * 512, n)
def pack4(w):
    words, scales = pack_weight(w, "e2m1")
    return words.reshape(words.shape[0], 128, -1), scales


def unpack4(words, scales):
    return unpack_weight(words.reshape(words.shape[0], 128, -1, 2), scales, "e2m1")


E4M3FN = np.array([(-1.0 if i & 128 else 1.0) * ((1.0 + (i & 7) / 8.0) * 2.0 ** (((i >> 3) & 15) - 7) if i & 120 else (i & 7) * 2.0 ** -9) for i in range(256)])


def e4m3fn_bytes(y):
    return np.clip(np.asarray(y, np.float64), -448.0, 448.0).astype(np.float32).astype(ml_dtypes.float8_e4m3fn).view(np.uint8)


def e4m3fn_values(b):
    return E4M3FN[b]


T, K, F, B = 512, 1024, 4096, 128


def setup_inputs():
    s, t = mx_kscale(K), mx_kscale(F)
    x = np.random.standard_normal((T, K)) * s
    x_scale = (np.abs(x).reshape(T, K // B, B).max(axis=2) / 448.0).astype(np.float32)
    x_bytes = e4m3fn_bytes(x / np.repeat(f64(x_scale), B, axis=1))
    w_enc = np.random.standard_normal((F, K)) / np.sqrt(K) / s * t[:, None]
    w_dec = np.random.standard_normal((F, K)) / np.sqrt(F) / t[:, None]
    dec_words, dec_scales = pack4(w_dec)
    return {"x_bytes": x_bytes,
            "x_scale": x_scale,
            "w_enc": bf(w_enc),
            "b_enc": bf(0.5 * np.random.standard_normal(F) * t),
            "dec_words": dec_words,
            "dec_scales": dec_scales,
            "b_dec": bf(0.3 * np.random.standard_normal(K))}


def reference(x_bytes, x_scale, w_enc, b_enc, dec_words, dec_scales, b_dec):
    x = e4m3fn_values(x_bytes) * np.repeat(f64(x_scale), B, axis=1)
    pre = mxq(x, 1, "e4m3") @ mxq(f64(w_enc), 1, "e4m3").T
    z = np.maximum(pre + f64(b_enc), 0.0)
    rec = mxq(z, 1, "e4m3") @ unpack4(dec_words, dec_scales)
    return rec + f64(b_dec)

@@ -1,0 +1,341 @@
+from contextlib import ExitStack
+
+import concourse.mybir as mybir
+from concourse.masks import make_identity
+
+T, K, F, B = 512, 1024, 4096, 128
+FLOPS = 2 * 2 * T * K * F
+
+F32 = mybir.dt.float32
+BF16 = mybir.dt.bfloat16
+I32 = mybir.dt.int32
+U32 = mybir.dt.uint32
+U8 = mybir.dt.uint8
+FP8 = mybir.dt.float8_e4m3fn
+FP8X4 = mybir.dt.float8_e4m3fn_x4
+FP4X4 = mybir.dt.float4_e2m1fn_x4
+ALU = mybir.AluOpType
+ACT = mybir.ActivationFunctionType
+
+P = 128
+GROUPS = F // 512
+PAIRS = F // 256
+CHUNK = 2
+ZB = 2
+PA = 1
+EARLY = 8 - CHUNK - ZB
+TB = CHUNK
+XV = 6
+DIRECT = 2
+
+
+def tile_sae_encode_decode_fp8_d4_kernel(tc, x_bytes, x_scale, w_enc, b_enc, dec_words, dec_scales, b_dec, out):
+    nc = tc.nc
+    with ExitStack() as ctx:
+        keep = ctx.enter_context(tc.tile_pool(name="keep", bufs=1))
+        wraw = ctx.enter_context(tc.tile_pool(name="wraw", bufs=PAIRS))
+        work = ctx.enter_context(tc.tile_pool(name="work", bufs=3))
+        outp = ctx.enter_context(tc.tile_pool(name="outp", bufs=4))
+        psum = ctx.enter_context(tc.psum_pool(name="psum", bufs=2))
+
+        ident = keep.tile([P, P], F32, name="ident")
+        dsc = keep.tile([P, GROUPS, K], U8, name="dsc", align_bytes=64)
+        dw = keep.tile([P, GROUPS, 2 * K], U8, name="dw", align_bytes=64)
+        zc = keep.tile([P, GROUPS, T], U32, name="zc", align_bytes=64)
+        zs = keep.tile([P, GROUPS, T], U8, name="zs", align_bytes=64)
+        xc = keep.tile([P, 2, T], U32, name="xc", align_bytes=64)
+        xs = keep.tile([P, 2, T], U8, name="xs", align_bytes=64)
+        xsc = keep.tile([P, 4, 8], F32, name="xsc")
+        b_bf = keep.tile([P, GROUPS, 4], BF16, name="b_bf")
+        b_f = keep.tile([P, GROUPS, 4], F32, name="b_f")
+        bd = keep.tile([P, K], BF16, name="bd")
+        xin = [keep.tile([P, 2, K], U8, name="xin%d" % i) for i in range(2)]
+
+        ctx.enter_context(tc.manual_schedule())
+
+        make_identity(nc, ident[:])
+        warm = keep.tile([P, 512], BF16, name="warm")
+        nc.vector.memset(warm[:], 0.0)
+
+        def warm_up(n):
+            for i in range(n):
+                wp = psum.tile([P, T], F32, name="wp", tag="zp", bufs=ZB)
+                nc.tensor.matmul(wp[:], lhsT=warm[:, 0:P], rhs=warm[:], start=True, stop=True)
+
+        nc.vector.memset(dsc[:].rearrange("p g n -> p (g n)").bitcast(I32), 0)
+
+        nc.sync.dma_start(out=xsc[:], in_=x_scale.rearrange("(p n) b -> p n b", p=P))
+
+        xr = x_bytes.rearrange("(p i n) k -> i p n k", p=P, n=2)
+        wr = w_enc.rearrange("(g m t) k -> g m t k", m=P, t=4)
+        raws = []
+
+        def load_w(j):
+            raw = wraw.tile([P, 2, K], BF16, name="raw")
+            t0 = 2 * (j % 2)
+            nc.sync.dma_start(out=raw[:], in_=wr[j // 2][:, t0 : t0 + 2, :])
+            raws.append(raw)
+
+        def load_dec(g):
+            nc.sync.dma_start(out=dw[:, g, :].bitcast(I32), in_=dec_words[g].bitcast(I32))
+
+        for i in range(2):
+            nc.sync.dma_start(out=xin[i][:], in_=xr[i])
+            if i == 0:
+                load_w(0)
+        for j in range(1, 6):
+            load_w(j)
+        for q in range(4):
+            nc.sync.dma_start(
+                out=dsc[32 * q : 32 * q + 4, :, :].bitcast(I32),
+                in_=dec_scales[:, 4 * q : 4 * q + 4, :].rearrange("g q n -> q g n").bitcast(I32),
+            )
+        load_dec(0)
+        for j in range(6, PAIRS):
+            load_w(j)
+            if j - 5 < GROUPS:
+                load_dec(j - 5)
+        nc.sync.dma_start(out=bd[:], in_=b_dec.partition_broadcast(P))
+
+
+        xw, xg = {}, {}
+
+        def x_widen(n, xv=6):
+            xw[n] = work.tile([P, K], BF16, name="xw", bufs=4)
+            for b in range(K // B):
+                src = xin[n // 2][:, n % 2, B * b : B * (b + 1)].bitcast(FP8)
+                dst = xw[n][:, B * b : B * (b + 1)]
+                s = xsc[:, n, b : b + 1]
+                if b < xv:
+                    nc.vector.tensor_scalar(out=dst, in0=src, scalar1=s, scalar2=None, op0=ALU.mult)
+                else:
+                    nc.scalar.activation(out=dst, in_=src, func=ACT.Copy, scale=s)
+
+        def words_out(dst, bank, eng="s"):
+            if eng == "s":
+                nc.scalar.copy(out=dst, in_=bank)
+            else:
+                nc.vector.tensor_copy(out=dst, in_=bank)
+
+        def x_turn(n, eng="s"):
+            tp = psum.tile([P, 2, 2, P], F32, name="xp", tag="rp", bufs=EARLY)
+            words = xw[n][:].bitcast(F32)
+            for c in range(2):
+                for u in range(2):
+                    nc.tensor.transpose(tp[:, c, u, :], words[:, 256 * c + u : 256 * (c + 1) : 2], ident[:])
+            xg[n] = work.tile([P, 2, P, 4], BF16, name="xg", bufs=4, align_bytes=64)
+            dst = xg[n][:].rearrange("p c r t -> p (c r t)").bitcast(F32).rearrange("p (c r u) -> p c r u", c=2, u=2)
+            words_out(dst, tp[:].rearrange("p c u r -> p c r u"), eng)
+
+        def x_quant(n):
+            for c in range(2):
+                nc.vector.quantize_mx(
+                    out=xc[:, c, P * n : P * (n + 1)].bitcast(FP8X4),
+                    scales=xs[:, c, P * n : P * (n + 1)],
+                    in_=xg[n][:, c, :, :].rearrange("p r t -> p (r t)"),
+                )
+
+        perm, wg, wc, ws = {}, {}, {}, {}
+
+        def raw_words(f):
+            return raws[f // 2][:, f % 2, :].bitcast(F32)
+
+        def w_perm(f):
+            perm[f] = work.tile([P, 2, 2, P], F32, name="perm", bufs=6)
+            nc.vector.tensor_copy(out=perm[f][:], in_=raw_words(f).rearrange("p (c m u) -> p c u m", m=P, u=2))
+
+        def w_turn(f, direct=False, eng="s", tag="tp", bufs=TB):
+            wg[f] = work.tile([P, 2, P, 4], BF16, name="wg", align_bytes=64, bufs=8)
+            tp = psum.tile([P, 2, 2, P], F32, name="tp", tag=tag, bufs=bufs)
+            for c in range(2):
+                for u in range(2):
+                    src = raw_words(f)[:, 256 * c + u : 256 * (c + 1) : 2] if direct else perm[f][:, c, u, :]
+                    nc.tensor.transpose(tp[:, c, u, :], src, ident[:])
+            dst = wg[f][:].rearrange("p c r t -> p (c r t)").bitcast(F32).rearrange("p (c r u) -> p c r u", c=2, u=2)
+            words_out(dst, tp[:].rearrange("p c u r -> p c r u"), eng)
+
+        def w_quant(f):
+            wc[f] = work.tile([P, 2, P], U32, name="wc", align_bytes=64, bufs=8)
+            ws[f] = work.tile([P, 2, P], U8, name="ws", align_bytes=64, bufs=8)
+            nc.vector.quantize_mx(
+                out=wc[f][:].rearrange("p x r -> p (x r)").bitcast(FP8X4),
+                scales=ws[f][:].rearrange("p x r -> p (x r)"),
+                in_=wg[f][:].rearrange("p c r t -> p (c r t)"),
+            )
+
+        zt, zi = {}, {}
+        zp = {}
+
+        def encode(f, lo=0, hi=T, eng="s"):
+            g, t = f // 4, f % 4
+            if t == 0 and lo == 0:
+                zt[g] = work.tile([P, 4, T], BF16, name="zt")
+            if lo == 0:
+                zp[f] = psum.tile([P, T], F32, name="zp", bufs=ZB)
+            for c in range(2):
+                nc.tensor.matmul_mx(
+                    out=zp[f][:, lo:hi],
+                    lhsT=wc[f][:, c, :].bitcast(FP8X4),
+                    lhsT_scale=ws[f][:, c, :],
+                    rhs=xc[:, c, lo:hi].bitcast(FP8X4),
+                    rhs_scale=xs[:, c, lo:hi],
+                    start=(c == 0),
+                    stop=(c == 1),
+                )
+            if hi == T:
+                if eng == "s":
+                    nc.scalar.activation(out=zt[g][:, t, :], in_=zp[f][:], func=ACT.Relu, bias=b_f[:, g, t : t + 1], scale=1.0)
+                else:
+                    nc.vector.tensor_scalar(out=zt[g][:, t, :], in0=zp[f][:], scalar1=b_f[:, g, t : t + 1], scalar2=0.0, op0=ALU.add, op1=ALU.max)
+
+        def z_lace(g, h):
+            zi[g, h] = work.tile([P, 256, 4], BF16, name="zi", align_bytes=64, bufs=4)
+            nc.vector.tensor_copy(
+                out=zi[g, h][:].rearrange("p (c i) t -> p c t i", i=4),
+                in_=zt[g][:, :, 256 * h : 256 * (h + 1)].rearrange("p t (c i) -> p c t i", i=4),
+            )
+
+        def z_quant(g, h):
+            nc.vector.quantize_mx(
+                out=zc[:, g, 256 * h : 256 * (h + 1)].bitcast(FP8X4),
+                scales=zs[:, g, 256 * h : 256 * (h + 1)],
+                in_=zi[g, h][:].rearrange("p n t -> p (n t)"),
+            )
+
+        acc = {}
+        orows = out.rearrange("(p n) k -> n p k", p=P)
+
+        def decode(g, b):
+            n, h = b // 2, b % 2
+            if g == 0:
+                name, bufs = ("rp", EARLY) if b < EARLY else (("tp", TB) if b < EARLY + TB else ("zp", ZB))
+                acc[b] = psum.tile([P, 512], F32, name="acc", tag=name, bufs=bufs)
+            nc.tensor.matmul_mx(
+                out=acc[b][:],
+                lhsT=zc[:, g, P * n : P * (n + 1)].bitcast(FP8X4),
+                lhsT_scale=zs[:, g, P * n : P * (n + 1)],
+                rhs=dw[:, g, 1024 * h : 1024 * (h + 1)].bitcast(FP4X4),
+                rhs_scale=dsc[:, g, 512 * h : 512 * (h + 1)],
+                start=(g == 0),
+                stop=(g == GROUPS - 1),
+            )
+
+        def store(b, cuts):
+            n, h = b // 2, b % 2
+            w = 512 // cuts
+            for i in range(cuts):
+                o = outp.tile([P, 512], F32, name="o")
+                nc.vector.tensor_tensor(
+                    out=o[:, 0:w], in0=acc[b][:, w * i : w * (i + 1)], in1=bd[:, 512 * h + w * i : 512 * h + w * (i + 1)], op=ALU.add
+                )
+                nc.sync.dma_start(out=orows[n][:, 512 * h + w * i : 512 * h + w * (i + 1)], in_=o[:, 0:w])
+
+        warm_up(5)
+        x_widen(0, 5)
+        nc.scalar.dma_start(out=b_bf[:], in_=b_enc.rearrange("(g p t) -> p g t", p=P, t=4))
+        x_turn(0, "s")
+        x_widen(1, 8)
+        x_widen(2, 7)
+        w_turn(0, True, "s")
+        x_widen(3, 8)
+        x_turn(1, "v")
+        w_turn(1, True, "s")
+        warm_up(1)
+        x_turn(2, "s")
+        x_turn(3, "s")
+        warm_up(1)
+        x_quant(0)
+        x_quant(1)
+        w_quant(0)
+        w_turn(2, True, "s")
+        nc.scalar.copy(out=b_f[:], in_=b_bf[:])
+        w_quant(1)
+        x_quant(2)
+        x_quant(3)
+        w_quant(2)
+        w_turn(3, True, "s")
+        warm_up(1)
+        encode(0)
+        w_perm(4)
+        encode(1)
+        w_perm(5)
+        w_quant(3)
+        w_perm(6)
+        START, FED = 4, 2
+        chunks = [list(range(a, min(a + CHUNK, 32))) for a in range(START, 32, CHUNK)]
+        prev = list(range(FED, START))
+        permed = 7
+        laces, quants, decs = [], [], []
+        for s in range(len(chunks) + 3):
+            now = chunks[s] if s < len(chunks) else []
+            nxt = chunks[s + 1] if s + 1 < len(chunks) else []
+            for f in now:
+                w_turn(f)
+            ready = decs[:]
+            quota = (len(ready) + 1) // 2 if len(ready) <= 2 * EARLY else len(ready)
+            done = []
+            for k in range(0, len(prev), 2):
+                for f in prev[k : k + 2]:
+                    encode(f)
+                for q in range(2):
+                    if ready:
+                        decode(*ready.pop(0))
+                        decs.pop(0)
+            if not prev:
+                while ready:
+                    decode(*ready.pop(0))
+                    decs.pop(0)
+            pre = []
+            for (g, h) in laces:
+                pre.append(("l", g, h))
+            laces = []
+            pm = []
+            while permed < 32 and nxt and permed <= nxt[-1] + PA:
+                pm.append(permed)
+                permed += 1
+            seq = []
+            a, b, c = [("p", f) for f in pm], pre, [("q", f) for f in now]
+            while a or b or c:
+                if a:
+                    seq.append(a.pop(0))
+                if b:
+                    seq.append(b.pop(0))
+                if c and (len(seq) >= 2 or not (a or b)):
+                    seq.append(c.pop(0))
+            zq = quants
+            quants = []
+            for it in seq:
+                if it[0] == "p":
+                    w_perm(it[1])
+                elif it[0] == "l":
+                    z_lace(it[1], it[2])
+                    quants.append((it[1], it[2]))
+                else:
+                    w_quant(it[1])
+                    if zq:
+                        g, h = zq.pop(0)
+                        z_quant(g, h)
+                        if h == 0 and g < GROUPS - 1:
+                            decs += [(g, b) for b in range(EARLY)]
+            for g, h in zq:
+                z_quant(g, h)
+                if h == 0 and g < GROUPS - 1:
+                    decs += [(g, b) for b in range(EARLY)]
+            for f in prev:
+                if f % 4 == 3:
+                    laces += [(f // 4, 0), (f // 4, 1)]
+            prev = now
+        for g, h in quants:
+            z_quant(g, h)
+        for g, b in decs:
+            decode(g, b)
+        for b in range(EARLY, EARLY + TB):
+            for g in range(GROUPS - 1):
+                decode(g, b)
+        for b in range(EARLY + TB):
+            decode(GROUPS - 1, b)
+            store(b, 1)
+        for b in range(EARLY + TB, 8):
+            for g in range(GROUPS):
+                decode(g, b)
+            store(b, 2 if b == 7 else 1)

@@ -19,24 +19,18 @@ ACT = mybir.ActivationFunctionType
 
 P = 128
 GROUPS = F // 512
-PAIRS = F // 256
-CHUNK = 2
-ZB = 2
-PA = 1
-EARLY = 8 - CHUNK - ZB
-TB = CHUNK
-XV = 6
-DIRECT = 2
+TILES = F // P
+HALF = T // 2
+DIRECT = 4
+WIDEN_V = 5
 
 
 def tile_sae_encode_decode_fp8_d4_kernel(tc, x_bytes, x_scale, w_enc, b_enc, dec_words, dec_scales, b_dec, out):
     nc = tc.nc
     with ExitStack() as ctx:
         keep = ctx.enter_context(tc.tile_pool(name="keep", bufs=1))
-        wraw = ctx.enter_context(tc.tile_pool(name="wraw", bufs=PAIRS))
         work = ctx.enter_context(tc.tile_pool(name="work", bufs=3))
-        outp = ctx.enter_context(tc.tile_pool(name="outp", bufs=4))
-        psum = ctx.enter_context(tc.psum_pool(name="psum", bufs=2))
+        psum = ctx.enter_context(tc.psum_pool(name="psum", bufs=4))
 
         ident = keep.tile([P, P], F32, name="ident")
         dsc = keep.tile([P, GROUPS, K], U8, name="dsc", align_bytes=64)
@@ -45,6 +39,8 @@ def tile_sae_encode_decode_fp8_d4_kernel(tc, x_bytes, x_scale, w_enc, b_enc, dec
         zs = keep.tile([P, GROUPS, T], U8, name="zs", align_bytes=64)
         xc = keep.tile([P, 2, T], U32, name="xc", align_bytes=64)
         xs = keep.tile([P, 2, T], U8, name="xs", align_bytes=64)
+        wc = keep.tile([P, TILES, 2, P], U32, name="wc", align_bytes=64)
+        ws = keep.tile([P, TILES, 2, P], U8, name="ws", align_bytes=64)
         xsc = keep.tile([P, 4, 8], F32, name="xsc")
         b_bf = keep.tile([P, GROUPS, 4], BF16, name="b_bf")
         b_f = keep.tile([P, GROUPS, 4], F32, name="b_f")
@@ -54,78 +50,67 @@ def tile_sae_encode_decode_fp8_d4_kernel(tc, x_bytes, x_scale, w_enc, b_enc, dec
         ctx.enter_context(tc.manual_schedule())
 
         make_identity(nc, ident[:])
-        warm = keep.tile([P, 512], BF16, name="warm")
-        nc.vector.memset(warm[:], 0.0)
-
-        def warm_up(n):
-            for i in range(n):
-                wp = psum.tile([P, T], F32, name="wp", tag="zp", bufs=ZB)
-                nc.tensor.matmul(wp[:], lhsT=warm[:, 0:P], rhs=warm[:], start=True, stop=True)
-
         nc.vector.memset(dsc[:].rearrange("p g n -> p (g n)").bitcast(I32), 0)
-
-        nc.sync.dma_start(out=xsc[:], in_=x_scale.rearrange("(p n) b -> p n b", p=P))
 
         xr = x_bytes.rearrange("(p i n) k -> i p n k", p=P, n=2)
         wr = w_enc.rearrange("(g m t) k -> g m t k", m=P, t=4)
-        raws = []
+        raw = {}
 
-        def load_w(j):
-            raw = wraw.tile([P, 2, K], BF16, name="raw")
-            t0 = 2 * (j % 2)
-            nc.sync.dma_start(out=raw[:], in_=wr[j // 2][:, t0 : t0 + 2, :])
-            raws.append(raw)
+        def load_w(f, count):
+            tile = work.tile([P, count, K], BF16, name="raw%d" % count, bufs=4 if count == 1 else 14)
+            nc.sync.dma_start(out=tile[:], in_=wr[f // 4][:, f % 4 : f % 4 + count, :])
+            for i in range(count):
+                raw[f + i] = tile[:, i, :].bitcast(F32)
 
         def load_dec(g):
             nc.sync.dma_start(out=dw[:, g, :].bitcast(I32), in_=dec_words[g].bitcast(I32))
 
-        for i in range(2):
-            nc.sync.dma_start(out=xin[i][:], in_=xr[i])
-            if i == 0:
-                load_w(0)
-        for j in range(1, 6):
-            load_w(j)
-        for q in range(4):
-            nc.sync.dma_start(
-                out=dsc[32 * q : 32 * q + 4, :, :].bitcast(I32),
-                in_=dec_scales[:, 4 * q : 4 * q + 4, :].rearrange("g q n -> q g n").bitcast(I32),
-            )
-        load_dec(0)
-        for j in range(6, PAIRS):
-            load_w(j)
-            if j - 5 < GROUPS:
-                load_dec(j - 5)
-        nc.sync.dma_start(out=bd[:], in_=b_dec.partition_broadcast(P))
+        def load_dec_scales():
+            for q in range(4):
+                nc.sync.dma_start(
+                    out=dsc[32 * q : 32 * q + 4, :, :].bitcast(I32),
+                    in_=dec_scales[:, 4 * q : 4 * q + 4, :].rearrange("g q n -> q g n").bitcast(I32),
+                )
 
+        xw, xg, sorted_words = {}, {}, {}
 
-        xw, xg = {}, {}
-
-        def x_widen(n, xv=6):
-            xw[n] = work.tile([P, K], BF16, name="xw", bufs=4)
-            for b in range(K // B):
-                src = xin[n // 2][:, n % 2, B * b : B * (b + 1)].bitcast(FP8)
-                dst = xw[n][:, B * b : B * (b + 1)]
-                s = xsc[:, n, b : b + 1]
-                if b < xv:
+        def x_widen(n, c, on_vector):
+            if n not in xw:
+                xw[n] = work.tile([P, 2, 512], BF16, name="xw", bufs=4)
+            sorted_words[n, c] = on_vector
+            for q in range(4):
+                src = xin[n // 2][:, n % 2, 512 * c + B * q : 512 * c + B * (q + 1)].bitcast(FP8)
+                s = xsc[:, n, 4 * c + q : 4 * c + q + 1]
+                if on_vector:
+                    dst = xw[n][:, c, :].rearrange("p (u m e) -> p m u e", u=2, e=2)[:, 32 * q : 32 * (q + 1), :, :]
                     nc.vector.tensor_scalar(out=dst, in0=src, scalar1=s, scalar2=None, op0=ALU.mult)
                 else:
-                    nc.scalar.activation(out=dst, in_=src, func=ACT.Copy, scale=s)
+                    nc.scalar.activation(out=xw[n][:, c, B * q : B * (q + 1)], in_=src, func=ACT.Copy, scale=s)
 
-        def words_out(dst, bank, eng="s"):
-            if eng == "s":
-                nc.scalar.copy(out=dst, in_=bank)
-            else:
-                nc.vector.tensor_copy(out=dst, in_=bank)
-
-        def x_turn(n, eng="s"):
-            tp = psum.tile([P, 2, 2, P], F32, name="xp", tag="rp", bufs=EARLY)
-            words = xw[n][:].bitcast(F32)
+        def turn(words, in_order, tag):
+            bank = psum.tile([P, 2, 2, P], F32, name="turned", tag=tag)
             for c in range(2):
                 for u in range(2):
-                    nc.tensor.transpose(tp[:, c, u, :], words[:, 256 * c + u : 256 * (c + 1) : 2], ident[:])
+                    src = words[:, c, P * u : P * (u + 1)] if in_order[c] else words[:, c, u : 2 * P : 2]
+                    nc.tensor.transpose(bank[:, c, u, :], src, ident[:])
+            return bank
+
+        def words_out(dst, bank, on_vector):
+            words = dst[:].rearrange("p c r t -> p (c r t)").bitcast(F32).rearrange("p (c r u) -> p c r u", c=2, u=2)
+            src = bank[:].rearrange("p c u r -> p c r u")
+            if on_vector:
+                nc.vector.tensor_copy(out=words, in_=src)
+            else:
+                nc.scalar.copy(out=words, in_=src)
+
+        xbank = {}
+
+        def x_turn(n, tag):
+            xbank[n] = turn(xw[n][:].bitcast(F32), [sorted_words[n, c] for c in range(2)], tag)
+
+        def x_out(n, on_vector):
             xg[n] = work.tile([P, 2, P, 4], BF16, name="xg", bufs=4, align_bytes=64)
-            dst = xg[n][:].rearrange("p c r t -> p (c r t)").bitcast(F32).rearrange("p (c r u) -> p c r u", c=2, u=2)
-            words_out(dst, tp[:].rearrange("p c u r -> p c r u"), eng)
+            words_out(xg[n], xbank[n], on_vector)
 
         def x_quant(n):
             for c in range(2):
@@ -135,83 +120,89 @@ def tile_sae_encode_decode_fp8_d4_kernel(tc, x_bytes, x_scale, w_enc, b_enc, dec
                     in_=xg[n][:, c, :, :].rearrange("p r t -> p (r t)"),
                 )
 
-        perm, wg, wc, ws = {}, {}, {}, {}
-
-        def raw_words(f):
-            return raws[f // 2][:, f % 2, :].bitcast(F32)
+        perm, wbank, wg = {}, {}, {}
 
         def w_perm(f):
-            perm[f] = work.tile([P, 2, 2, P], F32, name="perm", bufs=6)
-            nc.vector.tensor_copy(out=perm[f][:], in_=raw_words(f).rearrange("p (c m u) -> p c u m", m=P, u=2))
+            if DIRECT <= f < TILES:
+                perm[f] = work.tile([P, 2, 2, P], F32, name="perm", bufs=8)
+                nc.vector.tensor_copy(out=perm[f][:], in_=raw[f].rearrange("p (c m u) -> p c u m", m=P, u=2))
 
-        def w_turn(f, direct=False, eng="s", tag="tp", bufs=TB):
-            wg[f] = work.tile([P, 2, P, 4], BF16, name="wg", align_bytes=64, bufs=8)
-            tp = psum.tile([P, 2, 2, P], F32, name="tp", tag=tag, bufs=bufs)
-            for c in range(2):
-                for u in range(2):
-                    src = raw_words(f)[:, 256 * c + u : 256 * (c + 1) : 2] if direct else perm[f][:, c, u, :]
-                    nc.tensor.transpose(tp[:, c, u, :], src, ident[:])
-            dst = wg[f][:].rearrange("p c r t -> p (c r t)").bitcast(F32).rearrange("p (c r u) -> p c r u", c=2, u=2)
-            words_out(dst, tp[:].rearrange("p c u r -> p c r u"), eng)
+        def w_turn(f, tag="step"):
+            if f in perm:
+                wbank[f] = turn(perm[f][:].rearrange("p c u m -> p c (u m)"), [True, True], tag)
+            else:
+                wbank[f] = turn(raw[f].rearrange("p (c w) -> p c w", c=2), [False, False], tag)
+
+        def w_out(f, on_vector=False):
+            wg[f] = work.tile([P, 2, P, 4], BF16, name="wg", align_bytes=64, bufs=4)
+            words_out(wg[f], wbank[f], on_vector)
 
         def w_quant(f):
-            wc[f] = work.tile([P, 2, P], U32, name="wc", align_bytes=64, bufs=8)
-            ws[f] = work.tile([P, 2, P], U8, name="ws", align_bytes=64, bufs=8)
             nc.vector.quantize_mx(
-                out=wc[f][:].rearrange("p x r -> p (x r)").bitcast(FP8X4),
-                scales=ws[f][:].rearrange("p x r -> p (x r)"),
+                out=wc[:, f, :, :].rearrange("p c r -> p (c r)").bitcast(FP8X4),
+                scales=ws[:, f, :, :].rearrange("p c r -> p (c r)"),
                 in_=wg[f][:].rearrange("p c r t -> p (c r t)"),
             )
 
         zt, zi = {}, {}
-        zp = {}
 
-        def encode(f, lo=0, hi=T, eng="s"):
-            g, t = f // 4, f % 4
-            if t == 0 and lo == 0:
-                zt[g] = work.tile([P, 4, T], BF16, name="zt")
-            if lo == 0:
-                zp[f] = psum.tile([P, T], F32, name="zp", bufs=ZB)
+        def passes(dst, f, cols):
             for c in range(2):
                 nc.tensor.matmul_mx(
-                    out=zp[f][:, lo:hi],
-                    lhsT=wc[f][:, c, :].bitcast(FP8X4),
-                    lhsT_scale=ws[f][:, c, :],
-                    rhs=xc[:, c, lo:hi].bitcast(FP8X4),
-                    rhs_scale=xs[:, c, lo:hi],
+                    out=dst,
+                    lhsT=wc[:, f, c, :].bitcast(FP8X4),
+                    lhsT_scale=ws[:, f, c, :],
+                    rhs=xc[:, c, cols].bitcast(FP8X4),
+                    rhs_scale=xs[:, c, cols],
                     start=(c == 0),
                     stop=(c == 1),
                 )
-            if hi == T:
-                if eng == "s":
-                    nc.scalar.activation(out=zt[g][:, t, :], in_=zp[f][:], func=ACT.Relu, bias=b_f[:, g, t : t + 1], scale=1.0)
-                else:
-                    nc.vector.tensor_scalar(out=zt[g][:, t, :], in0=zp[f][:], scalar1=b_f[:, g, t : t + 1], scalar2=0.0, op0=ALU.add, op1=ALU.max)
 
-        def z_lace(g, h):
-            zi[g, h] = work.tile([P, 256, 4], BF16, name="zi", align_bytes=64, bufs=4)
+        def z_out(f, cols, src):
+            g, t = f // 4, f % 4
+            if g not in zt:
+                zt[g] = work.tile([P, 4, T], BF16, name="zt", bufs=2)
+            nc.scalar.activation(out=zt[g][:, t, cols], in_=src, func=ACT.Relu, bias=b_f[:, g, t : t + 1], scale=1.0)
+
+        pre = {}
+
+        def encode(f, tag="step"):
+            pre[f] = psum.tile([P, T], F32, name="pre", tag=tag)
+            passes(pre[f][:], f, slice(0, T))
+
+        def encode_half(f, half, tag="step"):
+            cols = slice(HALF * half, HALF * (half + 1))
+            if half == 0:
+                pre[f] = psum.tile([P, T], F32, name="pre", tag=tag)
+            passes(pre[f][:, cols], f, cols)
+
+        def relu_out(f):
+            z_out(f, slice(0, T), pre[f][:])
+
+        def z_lace(half, g):
+            zi[half, g] = work.tile([P, HALF, 4], BF16, name="zi", align_bytes=64, bufs=3)
             nc.vector.tensor_copy(
-                out=zi[g, h][:].rearrange("p (c i) t -> p c t i", i=4),
-                in_=zt[g][:, :, 256 * h : 256 * (h + 1)].rearrange("p t (c i) -> p c t i", i=4),
+                out=zi[half, g][:].rearrange("p (c i) t -> p c t i", i=4),
+                in_=zt[g][:, :, HALF * half : HALF * (half + 1)].rearrange("p t (c i) -> p c t i", i=4),
             )
 
-        def z_quant(g, h):
+        def z_quant(half, g):
+            cols = slice(HALF * half, HALF * (half + 1))
             nc.vector.quantize_mx(
-                out=zc[:, g, 256 * h : 256 * (h + 1)].bitcast(FP8X4),
-                scales=zs[:, g, 256 * h : 256 * (h + 1)],
-                in_=zi[g, h][:].rearrange("p n t -> p (n t)"),
+                out=zc[:, g, cols].bitcast(FP8X4),
+                scales=zs[:, g, cols],
+                in_=zi[half, g][:].rearrange("p n t -> p (n t)"),
             )
 
         acc = {}
         orows = out.rearrange("(p n) k -> n p k", p=P)
 
-        def decode(g, b):
-            n, h = b // 2, b % 2
+        def decode(half, g, b):
+            n, h = 2 * half + b // 2, b % 2
             if g == 0:
-                name, bufs = ("rp", EARLY) if b < EARLY else (("tp", TB) if b < EARLY + TB else ("zp", ZB))
-                acc[b] = psum.tile([P, 512], F32, name="acc", tag=name, bufs=bufs)
+                acc[half, b] = psum.tile([P, 512], F32, name="acc", tag="step" if half else "acc")
             nc.tensor.matmul_mx(
-                out=acc[b][:],
+                out=acc[half, b][:],
                 lhsT=zc[:, g, P * n : P * (n + 1)].bitcast(FP8X4),
                 lhsT_scale=zs[:, g, P * n : P * (n + 1)],
                 rhs=dw[:, g, 1024 * h : 1024 * (h + 1)].bitcast(FP4X4),
@@ -220,122 +211,125 @@ def tile_sae_encode_decode_fp8_d4_kernel(tc, x_bytes, x_scale, w_enc, b_enc, dec
                 stop=(g == GROUPS - 1),
             )
 
-        def store(b, cuts):
-            n, h = b // 2, b % 2
+        def store(half, b, cuts=1):
+            n, h = 2 * half + b // 2, b % 2
             w = 512 // cuts
             for i in range(cuts):
-                o = outp.tile([P, 512], F32, name="o")
-                nc.vector.tensor_tensor(
-                    out=o[:, 0:w], in0=acc[b][:, w * i : w * (i + 1)], in1=bd[:, 512 * h + w * i : 512 * h + w * (i + 1)], op=ALU.add
-                )
-                nc.sync.dma_start(out=orows[n][:, 512 * h + w * i : 512 * h + w * (i + 1)], in_=o[:, 0:w])
+                o = work.tile([P, 512], F32, name="o", bufs=5)
+                cols = slice(512 * h + w * i, 512 * h + w * (i + 1))
+                nc.vector.tensor_tensor(out=o[:, 0:w], in0=acc[half, b][:, w * i : w * (i + 1)], in1=bd[:, cols], op=ALU.add)
+                nc.sync.dma_start(out=orows[n][:, cols], in_=o[:, 0:w])
 
-        warm_up(5)
-        x_widen(0, 5)
+        nc.scalar.dma_start(out=xsc[:], in_=x_scale.rearrange("(p n) b -> p n b", p=P))
         nc.scalar.dma_start(out=b_bf[:], in_=b_enc.rearrange("(g p t) -> p g t", p=P, t=4))
-        x_turn(0, "s")
-        x_widen(1, 8)
-        x_widen(2, 7)
-        w_turn(0, True, "s")
-        x_widen(3, 8)
-        x_turn(1, "v")
-        w_turn(1, True, "s")
-        warm_up(1)
-        x_turn(2, "s")
-        x_turn(3, "s")
-        warm_up(1)
-        x_quant(0)
-        x_quant(1)
-        w_quant(0)
-        w_turn(2, True, "s")
-        nc.scalar.copy(out=b_f[:], in_=b_bf[:])
-        w_quant(1)
-        x_quant(2)
+        nc.sync.dma_start(out=xin[0][:], in_=xr[0])
+        nc.sync.dma_start(out=xin[1][:], in_=xr[1])
+        load_w(0, 1)
+        load_w(1, 1)
+        load_w(2, 1)
+        load_w(3, 1)
+        for f in range(4, 14, 2):
+            load_w(f, 2)
+        load_dec(0)
+        load_dec_scales()
+        load_w(14, 2)
+        load_dec(1)
+        for g in range(4, GROUPS):
+            load_w(4 * g, 2)
+            load_w(4 * g + 2, 2)
+            load_dec(g - 2)
+        load_dec(GROUPS - 2)
+        load_dec(GROUPS - 1)
+        nc.sync.dma_start(out=bd[:], in_=b_dec.partition_broadcast(P))
+
+        for n in range(4):
+            x_widen(n, 0, True)
+            x_widen(n, 1, n >= 2)
+            x_turn(n, "acc")
+        for f in range(4):
+            w_turn(f)
+        for n in range(3):
+            x_out(n, False)
+            x_quant(n)
+        x_out(3, False)
+        w_out(0, True)
         x_quant(3)
-        w_quant(2)
-        w_turn(3, True, "s")
-        warm_up(1)
-        encode(0)
+        w_out(1)
+        nc.scalar.copy(out=b_f[:], in_=b_bf[:])
+        w_quant(0)
+        w_out(2)
         w_perm(4)
-        encode(1)
+        w_quant(1)
+        encode(0, "acc")
+        encode(1, "acc")
+        w_out(3)
         w_perm(5)
-        w_quant(3)
+        w_quant(2)
         w_perm(6)
-        START, FED = 4, 2
-        chunks = [list(range(a, min(a + CHUNK, 32))) for a in range(START, 32, CHUNK)]
-        prev = list(range(FED, START))
-        permed = 7
-        laces, quants, decs = [], [], []
-        for s in range(len(chunks) + 3):
-            now = chunks[s] if s < len(chunks) else []
-            nxt = chunks[s + 1] if s + 1 < len(chunks) else []
-            for f in now:
-                w_turn(f)
-            ready = decs[:]
-            quota = (len(ready) + 1) // 2 if len(ready) <= 2 * EARLY else len(ready)
-            done = []
-            for k in range(0, len(prev), 2):
-                for f in prev[k : k + 2]:
-                    encode(f)
-                for q in range(2):
-                    if ready:
-                        decode(*ready.pop(0))
-                        decs.pop(0)
-            if not prev:
-                while ready:
-                    decode(*ready.pop(0))
-                    decs.pop(0)
-            pre = []
-            for (g, h) in laces:
-                pre.append(("l", g, h))
-            laces = []
-            pm = []
-            while permed < 32 and nxt and permed <= nxt[-1] + PA:
-                pm.append(permed)
-                permed += 1
-            seq = []
-            a, b, c = [("p", f) for f in pm], pre, [("q", f) for f in now]
-            while a or b or c:
-                if a:
-                    seq.append(a.pop(0))
-                if b:
-                    seq.append(b.pop(0))
-                if c and (len(seq) >= 2 or not (a or b)):
-                    seq.append(c.pop(0))
-            zq = quants
-            quants = []
-            for it in seq:
-                if it[0] == "p":
-                    w_perm(it[1])
-                elif it[0] == "l":
-                    z_lace(it[1], it[2])
-                    quants.append((it[1], it[2]))
-                else:
-                    w_quant(it[1])
-                    if zq:
-                        g, h = zq.pop(0)
-                        z_quant(g, h)
-                        if h == 0 and g < GROUPS - 1:
-                            decs += [(g, b) for b in range(EARLY)]
-            for g, h in zq:
-                z_quant(g, h)
-                if h == 0 and g < GROUPS - 1:
-                    decs += [(g, b) for b in range(EARLY)]
-            for f in prev:
-                if f % 4 == 3:
-                    laces += [(f // 4, 0), (f // 4, 1)]
-            prev = now
-        for g, h in quants:
-            z_quant(g, h)
-        for g, b in decs:
-            decode(g, b)
-        for b in range(EARLY, EARLY + TB):
-            for g in range(GROUPS - 1):
-                decode(g, b)
-        for b in range(EARLY + TB):
-            decode(GROUPS - 1, b)
-            store(b, 1)
-        for b in range(EARLY + TB, 8):
+        w_perm(7)
+        w_quant(3)
+        w_turn(4, "acc")
+        w_turn(5, "acc")
+        w_turn(6)
+        w_turn(7)
+        relu_out(0)
+        relu_out(1)
+        encode(2)
+        encode(3)
+        w_perm(8)
+        w_out(4, True)
+        w_out(5)
+        w_perm(9)
+        w_out(6)
+        w_quant(4)
+        w_perm(10)
+        w_out(7)
+        w_quant(5)
+        relu_out(2)
+        relu_out(3)
+        w_perm(11)
+        w_quant(6)
+        w_quant(7)
+
+        for g in range(1, GROUPS):
+            nxt = [f for f in range(4 * g + 4, 4 * g + 8) if f < TILES]
+            for f in nxt:
+                w_turn(f, "acc" if g == 1 else "step")
+                w_out(f)
+            if g >= 2:
+                decode(0, g - 2, 3)
+            for f in range(4 * g, 4 * g + 4):
+                encode(f)
+                relu_out(f)
+            z_lace(0, g - 1)
+            w_perm(4 * g + 8)
+            z_quant(0, g - 1)
+            for i in range(4):
+                if nxt:
+                    w_quant(nxt[i])
+                if i == 0:
+                    z_lace(1, g - 1)
+                if i == 2:
+                    z_quant(1, g - 1)
+                if i < 3:
+                    w_perm(4 * g + 9 + i)
+            for b in range(3):
+                decode(0, g - 1, b)
+
+        last = GROUPS - 1
+        z_lace(0, last)
+        z_lace(1, last)
+        z_quant(0, last)
+        z_quant(1, last)
+        decode(0, last - 1, 3)
+        for g in range(last):
+            decode(1, g, 0)
+        for b in range(4):
+            decode(0, last, b)
+            store(0, b)
+        decode(1, last, 0)
+        store(1, 0)
+        for b in range(1, 4):
             for g in range(GROUPS):
-                decode(g, b)
-            store(b, 2 if b == 7 else 1)
+                decode(1, g, b)
+            store(1, b, 2 if b == 3 else 1)

@@ -39,8 +39,6 @@ def tile_sae_encode_decode_fp8_d4_kernel(tc, x_bytes, x_scale, w_enc, b_enc, dec
         zs = keep.tile([P, GROUPS, T], U8, name="zs", align_bytes=64)
         xc = keep.tile([P, 2, T], U32, name="xc", align_bytes=64)
         xs = keep.tile([P, 2, T], U8, name="xs", align_bytes=64)
-        wc = keep.tile([P, TILES, 2, P], U32, name="wc", align_bytes=64)
-        ws = keep.tile([P, TILES, 2, P], U8, name="ws", align_bytes=64)
         xsc = keep.tile([P, 4, 8], F32, name="xsc")
         b_bf = keep.tile([P, GROUPS, 4], BF16, name="b_bf")
         b_f = keep.tile([P, GROUPS, 4], F32, name="b_f")
@@ -109,7 +107,7 @@ def tile_sae_encode_decode_fp8_d4_kernel(tc, x_bytes, x_scale, w_enc, b_enc, dec
             xbank[n] = turn(xw[n][:].bitcast(F32), [sorted_words[n, c] for c in range(2)], tag)
 
         def x_out(n, on_vector):
-            xg[n] = work.tile([P, 2, P, 4], BF16, name="xg", bufs=4, align_bytes=64)
+            xg[n] = work.tile([P, 2, P, 4], BF16, name="xg", tag="wg", bufs=8, align_bytes=64)
             words_out(xg[n], xbank[n], on_vector)
 
         def x_quant(n):
@@ -120,7 +118,7 @@ def tile_sae_encode_decode_fp8_d4_kernel(tc, x_bytes, x_scale, w_enc, b_enc, dec
                     in_=xg[n][:, c, :, :].rearrange("p r t -> p (r t)"),
                 )
 
-        perm, wbank, wg = {}, {}, {}
+        perm, wbank, wg, wc, ws = {}, {}, {}, {}, {}
 
         def w_perm(f):
             if DIRECT <= f < TILES:
@@ -134,13 +132,15 @@ def tile_sae_encode_decode_fp8_d4_kernel(tc, x_bytes, x_scale, w_enc, b_enc, dec
                 wbank[f] = turn(raw[f].rearrange("p (c w) -> p c w", c=2), [False, False], tag)
 
         def w_out(f, on_vector=False):
-            wg[f] = work.tile([P, 2, P, 4], BF16, name="wg", align_bytes=64, bufs=4)
+            wg[f] = work.tile([P, 2, P, 4], BF16, name="wg", align_bytes=64, bufs=8)
             words_out(wg[f], wbank[f], on_vector)
 
         def w_quant(f):
+            wc[f] = work.tile([P, 2, P], U32, name="wc", align_bytes=64, bufs=12)
+            ws[f] = work.tile([P, 2, P], U8, name="ws", align_bytes=64, bufs=12)
             nc.vector.quantize_mx(
-                out=wc[:, f, :, :].rearrange("p c r -> p (c r)").bitcast(FP8X4),
-                scales=ws[:, f, :, :].rearrange("p c r -> p (c r)"),
+                out=wc[f][:].rearrange("p c r -> p (c r)").bitcast(FP8X4),
+                scales=ws[f][:].rearrange("p c r -> p (c r)"),
                 in_=wg[f][:].rearrange("p c r t -> p (c r t)"),
             )
 
@@ -150,8 +150,8 @@ def tile_sae_encode_decode_fp8_d4_kernel(tc, x_bytes, x_scale, w_enc, b_enc, dec
             for c in range(2):
                 nc.tensor.matmul_mx(
                     out=dst,
-                    lhsT=wc[:, f, c, :].bitcast(FP8X4),
-                    lhsT_scale=ws[:, f, c, :],
+                    lhsT=wc[f][:, c, :].bitcast(FP8X4),
+                    lhsT_scale=ws[f][:, c, :],
                     rhs=xc[:, c, cols].bitcast(FP8X4),
                     rhs_scale=xs[:, c, cols],
                     start=(c == 0),
@@ -161,7 +161,7 @@ def tile_sae_encode_decode_fp8_d4_kernel(tc, x_bytes, x_scale, w_enc, b_enc, dec
         def z_out(f, cols, src):
             g, t = f // 4, f % 4
             if g not in zt:
-                zt[g] = work.tile([P, 4, T], BF16, name="zt", bufs=2)
+                zt[g] = work.tile([P, 4, T], BF16, name="zt", bufs=GROUPS)
             nc.scalar.activation(out=zt[g][:, t, cols], in_=src, func=ACT.Relu, bias=b_f[:, g, t : t + 1], scale=1.0)
 
         pre = {}
@@ -170,17 +170,11 @@ def tile_sae_encode_decode_fp8_d4_kernel(tc, x_bytes, x_scale, w_enc, b_enc, dec
             pre[f] = psum.tile([P, T], F32, name="pre", tag=tag)
             passes(pre[f][:], f, slice(0, T))
 
-        def encode_half(f, half, tag="step"):
-            cols = slice(HALF * half, HALF * (half + 1))
-            if half == 0:
-                pre[f] = psum.tile([P, T], F32, name="pre", tag=tag)
-            passes(pre[f][:, cols], f, cols)
-
         def relu_out(f):
             z_out(f, slice(0, T), pre[f][:])
 
         def z_lace(half, g):
-            zi[half, g] = work.tile([P, HALF, 4], BF16, name="zi", align_bytes=64, bufs=3)
+            zi[half, g] = work.tile([P, HALF, 4], BF16, name="zi", align_bytes=64, bufs=4)
             nc.vector.tensor_copy(
                 out=zi[half, g][:].rearrange("p (c i) t -> p c t i", i=4),
                 in_=zt[g][:, :, HALF * half : HALF * (half + 1)].rearrange("p t (c i) -> p c t i", i=4),
@@ -228,16 +222,15 @@ def tile_sae_encode_decode_fp8_d4_kernel(tc, x_bytes, x_scale, w_enc, b_enc, dec
         load_w(1, 1)
         load_w(2, 1)
         load_w(3, 1)
-        for f in range(4, 14, 2):
+        for f in range(4, 16, 2):
             load_w(f, 2)
         load_dec(0)
         load_dec_scales()
-        load_w(14, 2)
-        load_dec(1)
         for g in range(4, GROUPS):
             load_w(4 * g, 2)
             load_w(4 * g + 2, 2)
-            load_dec(g - 2)
+            load_dec(g - 3)
+        load_dec(GROUPS - 3)
         load_dec(GROUPS - 2)
         load_dec(GROUPS - 1)
         nc.sync.dma_start(out=bd[:], in_=b_dec.partition_broadcast(P))
@@ -291,45 +284,62 @@ def tile_sae_encode_decode_fp8_d4_kernel(tc, x_bytes, x_scale, w_enc, b_enc, dec
         w_quant(6)
         w_quant(7)
 
+        last = GROUPS - 1
+        late = []
+        for g in range(GROUPS):
+            late.append((z_lace, g))
+            if g >= 1:
+                late.append((z_quant, g - 1))
+        late.append((z_quant, last))
+
+        def late_work(count):
+            for i in range(count):
+                step, g = late.pop(0)
+                step(1, g)
+
         for g in range(1, GROUPS):
             nxt = [f for f in range(4 * g + 4, 4 * g + 8) if f < TILES]
-            for f in nxt:
+            z_lace(0, g - 1)
+            for i, f in enumerate(nxt):
                 w_turn(f, "acc" if g == 1 else "step")
-                w_out(f)
+                w_out(f, i == 1)
             if g >= 2:
-                decode(0, g - 2, 3)
+                decode(0, g - 2, 0)
             for f in range(4 * g, 4 * g + 4):
                 encode(f)
                 relu_out(f)
-            z_lace(0, g - 1)
-            w_perm(4 * g + 8)
-            z_quant(0, g - 1)
+            if g >= 2:
+                for b in range(1, 4):
+                    decode(0, g - 2, b)
+            if g == last:
+                late_work(1)
             for i in range(4):
+                w_perm(4 * g + 8 + i)
                 if nxt:
                     w_quant(nxt[i])
                 if i == 0:
-                    z_lace(1, g - 1)
-                if i == 2:
-                    z_quant(1, g - 1)
-                if i < 3:
-                    w_perm(4 * g + 9 + i)
-            for b in range(3):
-                decode(0, g - 1, b)
+                    z_quant(0, g - 1)
+            late_work({last: 5, last - 1: 3}.get(g, 1 if g >= 3 else 0))
 
-        last = GROUPS - 1
         z_lace(0, last)
-        z_lace(1, last)
+        late_work(1)
         z_quant(0, last)
-        z_quant(1, last)
-        decode(0, last - 1, 3)
-        for g in range(last):
-            decode(1, g, 0)
+        late_work(2)
+        for b in range(4):
+            decode(0, last - 1, b)
+        for g in range(2):
+            for b in range(4):
+                decode(1, g, b)
         for b in range(4):
             decode(0, last, b)
-            store(0, b)
-        decode(1, last, 0)
-        store(1, 0)
+        store(0, 0)
+        late_work(1)
+        for g in range(2, 4):
+            for b in range(4):
+                decode(1, g, b)
         for b in range(1, 4):
-            for g in range(GROUPS):
+            store(0, b)
+        for b in range(4):
+            for g in range(4, GROUPS):
                 decode(1, g, b)
             store(1, b, 2 if b == 3 else 1)

@@ -21,7 +21,7 @@ P = 128
 GROUPS = F // 512
 TILES = F // P
 HALF = T // 2
-DIRECT = 4
+DIRECT = 0
 WIDEN_V = 5
 
 
@@ -52,13 +52,14 @@ def tile_sae_encode_decode_fp8_d4_kernel(tc, x_bytes, x_scale, w_enc, b_enc, dec
 
         xr = x_bytes.rearrange("(p i n) k -> i p n k", p=P, n=2)
         wr = w_enc.rearrange("(g m t) k -> g m t k", m=P, t=4)
-        raw = {}
+        raw, pair_raw = {}, {}
 
         def load_w(f, count):
-            tile = work.tile([P, count, K], BF16, name="raw%d" % count, bufs=4 if count == 1 else 14)
+            tile = work.tile([P, count, K], BF16, name="raw%d" % count, bufs=16)
             nc.sync.dma_start(out=tile[:], in_=wr[f // 4][:, f % 4 : f % 4 + count, :])
             for i in range(count):
                 raw[f + i] = tile[:, i, :].bitcast(F32)
+            pair_raw[f] = tile[:].bitcast(F32)
 
         def load_dec(g):
             nc.sync.dma_start(out=dw[:, g, :].bitcast(I32), in_=dec_words[g].bitcast(I32))
@@ -94,7 +95,7 @@ def tile_sae_encode_decode_fp8_d4_kernel(tc, x_bytes, x_scale, w_enc, b_enc, dec
             return bank
 
         def words_out(dst, bank, on_vector):
-            words = dst[:].rearrange("p c r t -> p (c r t)").bitcast(F32).rearrange("p (c r u) -> p c r u", c=2, u=2)
+            words = dst.rearrange("p c r t -> p (c r t)").bitcast(F32).rearrange("p (c r u) -> p c r u", c=2, u=2)
             src = bank[:].rearrange("p c u r -> p c r u")
             if on_vector:
                 nc.vector.tensor_copy(out=words, in_=src)
@@ -107,8 +108,8 @@ def tile_sae_encode_decode_fp8_d4_kernel(tc, x_bytes, x_scale, w_enc, b_enc, dec
             xbank[n] = turn(xw[n][:].bitcast(F32), [sorted_words[n, c] for c in range(2)], tag)
 
         def x_out(n, on_vector):
-            xg[n] = work.tile([P, 2, P, 4], BF16, name="xg", tag="wg", bufs=8, align_bytes=64)
-            words_out(xg[n], xbank[n], on_vector)
+            xg[n] = work.tile([P, 2, P, 4], BF16, name="xg", bufs=4, align_bytes=64)
+            words_out(xg[n][:], xbank[n], on_vector)
 
         def x_quant(n):
             for c in range(2):
@@ -122,26 +123,35 @@ def tile_sae_encode_decode_fp8_d4_kernel(tc, x_bytes, x_scale, w_enc, b_enc, dec
 
         def w_perm(f):
             if DIRECT <= f < TILES:
-                perm[f] = work.tile([P, 2, 2, P], F32, name="perm", bufs=8)
-                nc.vector.tensor_copy(out=perm[f][:], in_=raw[f].rearrange("p (c m u) -> p c u m", m=P, u=2))
+                both = work.tile([P, 2, 2, 2, P], F32, name="perm", bufs=3)
+                nc.vector.tensor_copy(
+                    out=both[:].rearrange("p i c u m -> p (i c) u m"),
+                    in_=pair_raw[f].rearrange("p i (c m u) -> p (i c) u m", m=P, u=2),
+                )
+                for i in range(2):
+                    perm[f + i] = both[:, i, :, :, :]
 
         def w_turn(f, tag="step"):
             if f in perm:
-                wbank[f] = turn(perm[f][:].rearrange("p c u m -> p c (u m)"), [True, True], tag)
+                wbank[f] = turn(perm[f].rearrange("p c u m -> p c (u m)"), [True, True], tag)
             else:
                 wbank[f] = turn(raw[f].rearrange("p (c w) -> p c w", c=2), [False, False], tag)
 
         def w_out(f, on_vector=False):
-            wg[f] = work.tile([P, 2, P, 4], BF16, name="wg", align_bytes=64, bufs=8)
-            words_out(wg[f], wbank[f], on_vector)
+            if f % 2 == 0:
+                wg[f // 2] = work.tile([P, 2, 2, P, 4], BF16, name="wg", align_bytes=64, bufs=4)
+            words_out(wg[f // 2][:, f % 2, :, :, :], wbank[f], on_vector)
 
-        def w_quant(f):
-            wc[f] = work.tile([P, 2, P], U32, name="wc", align_bytes=64, bufs=12)
-            ws[f] = work.tile([P, 2, P], U8, name="ws", align_bytes=64, bufs=12)
+        def w_quant(f, count):
+            j = f // 2
+            if f % 2 == 0:
+                wc[j] = work.tile([P, 2, 2, P], U32, name="wc", align_bytes=64, bufs=4)
+                ws[j] = work.tile([P, 2, 2, P], U8, name="ws", align_bytes=64, bufs=4)
+            part = slice(f % 2, f % 2 + count)
             nc.vector.quantize_mx(
-                out=wc[f][:].rearrange("p c r -> p (c r)").bitcast(FP8X4),
-                scales=ws[f][:].rearrange("p c r -> p (c r)"),
-                in_=wg[f][:].rearrange("p c r t -> p (c r t)"),
+                out=wc[j][:, part, :, :].rearrange("p i c r -> p (i c r)").bitcast(FP8X4),
+                scales=ws[j][:, part, :, :].rearrange("p i c r -> p (i c r)"),
+                in_=wg[j][:, part, :, :, :].rearrange("p i c r t -> p (i c r t)"),
             )
 
         zt, zi = {}, {}
@@ -150,8 +160,8 @@ def tile_sae_encode_decode_fp8_d4_kernel(tc, x_bytes, x_scale, w_enc, b_enc, dec
             for c in range(2):
                 nc.tensor.matmul_mx(
                     out=dst,
-                    lhsT=wc[f][:, c, :].bitcast(FP8X4),
-                    lhsT_scale=ws[f][:, c, :],
+                    lhsT=wc[f // 2][:, f % 2, c, :].bitcast(FP8X4),
+                    lhsT_scale=ws[f // 2][:, f % 2, c, :],
                     rhs=xc[:, c, cols].bitcast(FP8X4),
                     rhs_scale=xs[:, c, cols],
                     start=(c == 0),
@@ -169,6 +179,16 @@ def tile_sae_encode_decode_fp8_d4_kernel(tc, x_bytes, x_scale, w_enc, b_enc, dec
         def encode(f, tag="step"):
             pre[f] = psum.tile([P, T], F32, name="pre", tag=tag)
             passes(pre[f][:], f, slice(0, T))
+
+        def encode_pair(f, half, tag="step"):
+            cols = slice(HALF * half, HALF * (half + 1))
+            pre[f, half] = psum.tile([P, 2, HALF], F32, name="pre2", tag=tag)
+            for i in range(2):
+                passes(pre[f, half][:, i, :], f + i, cols)
+
+        def relu_pair(f, half):
+            for i in range(2):
+                z_out(f + i, slice(HALF * half, HALF * (half + 1)), pre[f, half][:, i, :])
 
         def relu_out(f):
             z_out(f, slice(0, T), pre[f][:])
@@ -215,74 +235,52 @@ def tile_sae_encode_decode_fp8_d4_kernel(tc, x_bytes, x_scale, w_enc, b_enc, dec
                 nc.sync.dma_start(out=orows[n][:, cols], in_=o[:, 0:w])
 
         nc.scalar.dma_start(out=xsc[:], in_=x_scale.rearrange("(p n) b -> p n b", p=P))
-        nc.scalar.dma_start(out=b_bf[:], in_=b_enc.rearrange("(g p t) -> p g t", p=P, t=4))
         nc.sync.dma_start(out=xin[0][:], in_=xr[0])
         nc.sync.dma_start(out=xin[1][:], in_=xr[1])
-        load_w(0, 1)
-        load_w(1, 1)
-        load_w(2, 1)
-        load_w(3, 1)
-        for f in range(4, 16, 2):
+        load_w(0, 2)
+        load_w(2, 2)
+        nc.sync.dma_start(out=b_bf[:], in_=b_enc.rearrange("(g p t) -> p g t", p=P, t=4))
+        for f in range(4, 14, 2):
             load_w(f, 2)
         load_dec(0)
         load_dec_scales()
+        load_w(14, 2)
         for g in range(4, GROUPS):
             load_w(4 * g, 2)
             load_w(4 * g + 2, 2)
             load_dec(g - 3)
-        load_dec(GROUPS - 3)
-        load_dec(GROUPS - 2)
-        load_dec(GROUPS - 1)
+        for g in range(GROUPS - 3, GROUPS):
+            load_dec(g)
         nc.sync.dma_start(out=bd[:], in_=b_dec.partition_broadcast(P))
 
         for n in range(4):
             x_widen(n, 0, True)
             x_widen(n, 1, n >= 2)
+        for n in range(4):
             x_turn(n, "acc")
+            x_out(n, False)
+        w_perm(0)
+        x_quant(0)
+        x_quant(1)
+        w_perm(2)
         for f in range(4):
             w_turn(f)
-        for n in range(3):
-            x_out(n, False)
-            x_quant(n)
-        x_out(3, False)
-        w_out(0, True)
+        x_quant(2)
+        w_out(0)
         x_quant(3)
-        w_out(1)
+        w_out(1, True)
         nc.scalar.copy(out=b_f[:], in_=b_bf[:])
-        w_quant(0)
+        w_quant(0, 1)
         w_out(2)
         w_perm(4)
-        w_quant(1)
-        encode(0, "acc")
-        encode(1, "acc")
+        w_quant(1, 1)
         w_out(3)
-        w_perm(5)
-        w_quant(2)
+        encode(0)
+        encode(1)
         w_perm(6)
-        w_perm(7)
-        w_quant(3)
-        w_turn(4, "acc")
-        w_turn(5, "acc")
-        w_turn(6)
-        w_turn(7)
+        w_quant(2, 2)
         relu_out(0)
         relu_out(1)
-        encode(2)
-        encode(3)
-        w_perm(8)
-        w_out(4, True)
-        w_out(5)
-        w_perm(9)
-        w_out(6)
-        w_quant(4)
-        w_perm(10)
-        w_out(7)
-        w_quant(5)
-        relu_out(2)
-        relu_out(3)
-        w_perm(11)
-        w_quant(6)
-        w_quant(7)
 
         last = GROUPS - 1
         late = []
@@ -298,33 +296,38 @@ def tile_sae_encode_decode_fp8_d4_kernel(tc, x_bytes, x_scale, w_enc, b_enc, dec
                 step(1, g)
 
         for g in range(1, GROUPS):
-            nxt = [f for f in range(4 * g + 4, 4 * g + 8) if f < TILES]
-            z_lace(0, g - 1)
-            for i, f in enumerate(nxt):
-                w_turn(f, "acc" if g == 1 else "step")
-                w_out(f, i == 1)
+            first = 4 * g
+            for f in range(first, first + 4):
+                w_turn(f, "acc" if g <= 2 else "step")
+                w_out(f, f == first + 1)
             if g >= 2:
-                decode(0, g - 2, 0)
-            for f in range(4 * g, 4 * g + 4):
+                z_quant(0, g - 2)
+            w_quant(first, 2)
+            if g >= 3:
+                decode(0, g - 3, 3)
+            for f in range(first - 2, first + 2):
                 encode(f)
                 relu_out(f)
+            w_perm(first + 4)
             if g >= 2:
-                for b in range(1, 4):
+                for b in range(3):
                     decode(0, g - 2, b)
+            w_quant(first + 2, 2)
+            w_perm(first + 6)
             if g == last:
-                late_work(1)
-            for i in range(4):
-                w_perm(4 * g + 8 + i)
-                if nxt:
-                    w_quant(nxt[i])
-                if i == 0:
-                    z_quant(0, g - 1)
-            late_work({last: 5, last - 1: 3}.get(g, 1 if g >= 3 else 0))
+                late_work(2)
+            z_lace(0, g - 1)
+            late_work(1 if g >= 3 else 0)
+        z_quant(0, last - 1)
 
+        decode(0, last - 2, 3)
+        for f in range(TILES - 2, TILES):
+            encode(f)
+            relu_out(f)
+        late_work(3)
         z_lace(0, last)
         late_work(1)
         z_quant(0, last)
-        late_work(2)
         for b in range(4):
             decode(0, last - 1, b)
         for g in range(2):
@@ -332,6 +335,7 @@ def tile_sae_encode_decode_fp8_d4_kernel(tc, x_bytes, x_scale, w_enc, b_enc, dec
                 decode(1, g, b)
         for b in range(4):
             decode(0, last, b)
+        late_work(4)
         store(0, 0)
         late_work(1)
         for g in range(2, 4):

@@ -21,7 +21,7 @@ P = 128
 GROUPS = F // 512
 TILES = F // P
 HALF = T // 2
-DIRECT = 0
+DIRECT = 4
 WIDEN_V = 5
 
 
@@ -40,7 +40,8 @@ def tile_sae_encode_decode_fp8_d4_kernel(tc, x_bytes, x_scale, w_enc, b_enc, dec
         xc = keep.tile([P, 2, T], U32, name="xc", align_bytes=64)
         xs = keep.tile([P, 2, T], U8, name="xs", align_bytes=64)
         xsc = keep.tile([P, 4, 8], F32, name="xsc")
-        b_bf = keep.tile([P, GROUPS, 4], BF16, name="b_bf")
+        b_first = keep.tile([P, 1, 4], BF16, name="b_first")
+        b_rest = keep.tile([P, GROUPS - 1, 4], BF16, name="b_rest")
         b_f = keep.tile([P, GROUPS, 4], F32, name="b_f")
         bd = keep.tile([P, K], BF16, name="bd")
         xin = [keep.tile([P, 2, K], U8, name="xin%d" % i) for i in range(2)]
@@ -193,9 +194,10 @@ def tile_sae_encode_decode_fp8_d4_kernel(tc, x_bytes, x_scale, w_enc, b_enc, dec
         def relu_out(f):
             z_out(f, slice(0, T), pre[f][:])
 
-        def z_lace(half, g):
-            zi[half, g] = work.tile([P, HALF, 4], BF16, name="zi", align_bytes=64, bufs=4)
-            nc.vector.tensor_copy(
+        def z_lace(half, g, on_vector=True):
+            zi[half, g] = work.tile([P, HALF, 4], BF16, name="zi", align_bytes=64, bufs=5)
+            copy = nc.vector.tensor_copy if on_vector else nc.scalar.copy
+            copy(
                 out=zi[half, g][:].rearrange("p (c i) t -> p c t i", i=4),
                 in_=zt[g][:, :, HALF * half : HALF * (half + 1)].rearrange("p t (c i) -> p c t i", i=4),
             )
@@ -211,37 +213,43 @@ def tile_sae_encode_decode_fp8_d4_kernel(tc, x_bytes, x_scale, w_enc, b_enc, dec
         acc = {}
         orows = out.rearrange("(p n) k -> n p k", p=P)
 
-        def decode(half, g, b):
-            n, h = 2 * half + b // 2, b % 2
-            if g == 0:
-                acc[half, b] = psum.tile([P, 512], F32, name="acc", tag="step" if half else "acc")
+        def decode_cols(bank, n, g, lo, width):
             nc.tensor.matmul_mx(
-                out=acc[half, b][:],
+                out=bank[:, 0:width],
                 lhsT=zc[:, g, P * n : P * (n + 1)].bitcast(FP8X4),
                 lhsT_scale=zs[:, g, P * n : P * (n + 1)],
-                rhs=dw[:, g, 1024 * h : 1024 * (h + 1)].bitcast(FP4X4),
-                rhs_scale=dsc[:, g, 512 * h : 512 * (h + 1)],
+                rhs=dw[:, g, 2 * lo : 2 * (lo + width)].bitcast(FP4X4),
+                rhs_scale=dsc[:, g, lo : lo + width],
                 start=(g == 0),
                 stop=(g == GROUPS - 1),
             )
 
-        def store(half, b, cuts=1):
-            n, h = 2 * half + b // 2, b % 2
-            w = 512 // cuts
-            for i in range(cuts):
-                o = work.tile([P, 512], F32, name="o", bufs=5)
-                cols = slice(512 * h + w * i, 512 * h + w * (i + 1))
-                nc.vector.tensor_tensor(out=o[:, 0:w], in0=acc[half, b][:, w * i : w * (i + 1)], in1=bd[:, cols], op=ALU.add)
-                nc.sync.dma_start(out=orows[n][:, cols], in_=o[:, 0:w])
+        def store_cols(bank, n, lo, width):
+            o = work.tile([P, 512], F32, name="o", bufs=5)
+            cols = slice(lo, lo + width)
+            nc.vector.tensor_tensor(out=o[:, 0:width], in0=bank[:, 0:width], in1=bd[:, cols], op=ALU.add)
+            nc.sync.dma_start(out=orows[n][:, cols], in_=o[:, 0:width])
 
+        def decode(half, g, b):
+            if g == 0:
+                acc[half, b] = psum.tile([P, 512], F32, name="acc", tag="step" if half else "acc")
+            decode_cols(acc[half, b], 2 * half + b // 2, g, 512 * (b % 2), 512)
+
+        def store(half, b):
+            store_cols(acc[half, b], 2 * half + b // 2, 512 * (b % 2), 512)
+
+        b_rows = b_enc.rearrange("(g p t) -> p g t", p=P, t=4)
         nc.scalar.dma_start(out=xsc[:], in_=x_scale.rearrange("(p n) b -> p n b", p=P))
         nc.sync.dma_start(out=xin[0][:], in_=xr[0])
         nc.sync.dma_start(out=xin[1][:], in_=xr[1])
         load_w(0, 2)
         load_w(2, 2)
-        nc.sync.dma_start(out=b_bf[:], in_=b_enc.rearrange("(g p t) -> p g t", p=P, t=4))
-        for f in range(4, 14, 2):
+        load_w(4, 2)
+        nc.sync.dma_start(out=b_first[:], in_=b_rows[:, 0:1, :])
+        for f in range(6, 14, 2):
             load_w(f, 2)
+            if f == 6:
+                nc.sync.dma_start(out=b_rest[:], in_=b_rows[:, 1:GROUPS, :])
         load_dec(0)
         load_dec_scales()
         load_w(14, 2)
@@ -256,45 +264,38 @@ def tile_sae_encode_decode_fp8_d4_kernel(tc, x_bytes, x_scale, w_enc, b_enc, dec
         for n in range(4):
             x_widen(n, 0, True)
             x_widen(n, 1, n >= 2)
-        for n in range(4):
-            x_turn(n, "acc")
-            x_out(n, False)
-        w_perm(0)
-        x_quant(0)
-        x_quant(1)
-        w_perm(2)
-        for f in range(4):
+        x_turn(0, "acc")
+        x_turn(1, "acc")
+        w_turn(0)
+        x_turn(2, "acc")
+        x_turn(3, "acc")
+        for f in range(1, 4):
             w_turn(f)
-        x_quant(2)
-        w_out(0)
-        x_quant(3)
-        w_out(1, True)
-        nc.scalar.copy(out=b_f[:], in_=b_bf[:])
+        x_out(0, False)
+        x_out(1, False)
+        x_quant(0)
+        w_out(0, True)
+        x_out(2, False)
+        x_quant(1)
         w_quant(0, 1)
+        x_out(3, False)
+        x_quant(2)
+        w_out(1)
+        x_quant(3)
         w_out(2)
-        w_perm(4)
         w_quant(1, 1)
+        w_perm(4)
         w_out(3)
+        nc.scalar.copy(out=b_f[:, 0:1, :], in_=b_first[:])
         encode(0)
         encode(1)
         w_perm(6)
         w_quant(2, 2)
         relu_out(0)
         relu_out(1)
+        nc.scalar.copy(out=b_f[:, 1:GROUPS, :], in_=b_rest[:])
 
         last = GROUPS - 1
-        late = []
-        for g in range(GROUPS):
-            late.append((z_lace, g))
-            if g >= 1:
-                late.append((z_quant, g - 1))
-        late.append((z_quant, last))
-
-        def late_work(count):
-            for i in range(count):
-                step, g = late.pop(0)
-                step(1, g)
-
         for g in range(1, GROUPS):
             first = 4 * g
             for f in range(first, first + 4):
@@ -304,46 +305,62 @@ def tile_sae_encode_decode_fp8_d4_kernel(tc, x_bytes, x_scale, w_enc, b_enc, dec
                 z_quant(0, g - 2)
             w_quant(first, 2)
             if g >= 3:
-                decode(0, g - 3, 3)
+                for b in range(2, 4):
+                    decode(0, g - 3, b)
             for f in range(first - 2, first + 2):
                 encode(f)
                 relu_out(f)
-            w_perm(first + 4)
             if g >= 2:
-                for b in range(3):
+                for b in range(2):
                     decode(0, g - 2, b)
+            w_perm(first + 4)
+            if g == last:
+                z_lace(1, 1)
             w_quant(first + 2, 2)
             w_perm(first + 6)
             if g == last:
-                late_work(2)
+                z_quant(1, 0)
             z_lace(0, g - 1)
-            late_work(1 if g >= 3 else 0)
-        z_quant(0, last - 1)
+            if g == last - 1:
+                z_lace(1, 0)
 
-        decode(0, last - 2, 3)
+        z_quant(1, 1)
+        z_quant(0, last - 1)
+        for b in range(2, 4):
+            decode(0, last - 2, b)
         for f in range(TILES - 2, TILES):
             encode(f)
             relu_out(f)
-        late_work(3)
+        z_lace(1, 2)
+        z_lace(1, 3)
+        z_quant(1, 2)
         z_lace(0, last)
-        late_work(1)
+        z_quant(1, 3)
         z_quant(0, last)
+        z_lace(1, 4)
+        for g in range(5, GROUPS):
+            z_lace(1, g, False)
+        z_quant(1, 4)
         for b in range(4):
             decode(0, last - 1, b)
-        for g in range(2):
-            for b in range(4):
+        for g in range(3):
+            for b in range(3):
                 decode(1, g, b)
         for b in range(4):
             decode(0, last, b)
-        late_work(4)
-        store(0, 0)
-        late_work(1)
-        for g in range(2, 4):
-            for b in range(4):
+        for g in range(5, GROUPS):
+            z_quant(1, g)
+            store(0, g - 5)
+        store(0, 3)
+        for g in range(3, 5):
+            for b in range(3):
                 decode(1, g, b)
-        for b in range(1, 4):
-            store(0, b)
-        for b in range(4):
-            for g in range(4, GROUPS):
+        for b in range(3):
+            for g in range(5, GROUPS):
                 decode(1, g, b)
-            store(1, b, 2 if b == 3 else 1)
+            store(1, b)
+        for q in range(4):
+            piece = psum.tile([P, 512], F32, name="piece", tag="acc")
+            for g in range(GROUPS):
+                decode_cols(piece, 3, g, 512 + P * q, P)
+            store_cols(piece, 3, 512 + P * q, P)

@@ -48,8 +48,15 @@ def tile_sae_encode_decode_fp8_d4_kernel(tc, x_bytes, x_scale, w_enc, b_enc, dec
 
         ctx.enter_context(tc.manual_schedule())
 
+        warm = keep.tile([P, 512], BF16, name="warm")
+        early = keep.tile([P, 2], BF16, name="early")
         make_identity(nc, ident[:])
+        nc.vector.memset(warm[:], 0.0)
         nc.vector.memset(dsc[:].rearrange("p g n -> p (g n)").bitcast(I32), 0)
+
+        def warm_up(tag):
+            idle = psum.tile([P, 512], F32, name="idle", tag=tag)
+            nc.tensor.matmul(idle[:], lhsT=warm[:, 0:P], rhs=warm[:], start=True, stop=True)
 
         xr = x_bytes.rearrange("(p i n) k -> i p n k", p=P, n=2)
         wr = w_enc.rearrange("(g m t) k -> g m t k", m=P, t=4)
@@ -95,8 +102,7 @@ def tile_sae_encode_decode_fp8_d4_kernel(tc, x_bytes, x_scale, w_enc, b_enc, dec
                     nc.tensor.transpose(bank[:, c, u, :], src, ident[:])
             return bank
 
-        def words_out(dst, bank, on_vector):
-            words = dst.rearrange("p c r t -> p (c r t)").bitcast(F32).rearrange("p (c r u) -> p c r u", c=2, u=2)
+        def words_out(words, bank, on_vector):
             src = bank[:].rearrange("p c u r -> p c r u")
             if on_vector:
                 nc.vector.tensor_copy(out=words, in_=src)
@@ -109,15 +115,18 @@ def tile_sae_encode_decode_fp8_d4_kernel(tc, x_bytes, x_scale, w_enc, b_enc, dec
             xbank[n] = turn(xw[n][:].bitcast(F32), [sorted_words[n, c] for c in range(2)], tag)
 
         def x_out(n, on_vector):
-            xg[n] = work.tile([P, 2, P, 4], BF16, name="xg", bufs=4, align_bytes=64)
-            words_out(xg[n][:], xbank[n], on_vector)
+            if n % 2 == 0:
+                xg[n // 2] = work.tile([P, 2, 2, P, 4], BF16, name="xg", bufs=2, align_bytes=64)
+            words = xg[n // 2][:].rearrange("p c i r t -> p c i (r t)").bitcast(F32)[:, :, n % 2, :]
+            words_out(words.rearrange("p c (r u) -> p c r u", u=2), xbank[n], on_vector)
 
-        def x_quant(n):
+        def x_quant(half):
+            cols = slice(HALF * half, HALF * (half + 1))
             for c in range(2):
                 nc.vector.quantize_mx(
-                    out=xc[:, c, P * n : P * (n + 1)].bitcast(FP8X4),
-                    scales=xs[:, c, P * n : P * (n + 1)],
-                    in_=xg[n][:, c, :, :].rearrange("p r t -> p (r t)"),
+                    out=xc[:, c, cols].bitcast(FP8X4),
+                    scales=xs[:, c, cols],
+                    in_=xg[half][:, c, :, :, :].rearrange("p i r t -> p (i r t)"),
                 )
 
         perm, wbank, wg, wc, ws = {}, {}, {}, {}, {}
@@ -141,7 +150,8 @@ def tile_sae_encode_decode_fp8_d4_kernel(tc, x_bytes, x_scale, w_enc, b_enc, dec
         def w_out(f, on_vector=False):
             if f % 2 == 0:
                 wg[f // 2] = work.tile([P, 2, 2, P, 4], BF16, name="wg", align_bytes=64, bufs=4)
-            words_out(wg[f // 2][:, f % 2, :, :, :], wbank[f], on_vector)
+            words = wg[f // 2][:, f % 2, :, :, :].rearrange("p c r t -> p (c r t)").bitcast(F32)
+            words_out(words.rearrange("p (c r u) -> p c r u", c=2, u=2), wbank[f], on_vector)
 
         def w_quant(f, count):
             j = f // 2
@@ -240,6 +250,7 @@ def tile_sae_encode_decode_fp8_d4_kernel(tc, x_bytes, x_scale, w_enc, b_enc, dec
 
         b_rows = b_enc.rearrange("(g p t) -> p g t", p=P, t=4)
         nc.scalar.dma_start(out=xsc[:], in_=x_scale.rearrange("(p n) b -> p n b", p=P))
+        nc.scalar.activation(out=early[:], in_=warm[:, 0:2], func=ACT.Copy)
         nc.sync.dma_start(out=xin[0][:], in_=xr[0])
         nc.sync.dma_start(out=xin[1][:], in_=xr[1])
         load_w(0, 2)
@@ -261,9 +272,11 @@ def tile_sae_encode_decode_fp8_d4_kernel(tc, x_bytes, x_scale, w_enc, b_enc, dec
             load_dec(g)
         nc.sync.dma_start(out=bd[:], in_=b_dec.partition_broadcast(P))
 
+        for i in range(4):
+            warm_up("step")
         for n in range(4):
             x_widen(n, 0, True)
-            x_widen(n, 1, n >= 2)
+            x_widen(n, 1, n == 3)
         x_turn(0, "acc")
         x_turn(1, "acc")
         w_turn(0)
@@ -271,17 +284,15 @@ def tile_sae_encode_decode_fp8_d4_kernel(tc, x_bytes, x_scale, w_enc, b_enc, dec
         x_turn(3, "acc")
         for f in range(1, 4):
             w_turn(f)
-        x_out(0, False)
+        x_out(0, True)
         x_out(1, False)
-        x_quant(0)
         w_out(0, True)
         x_out(2, False)
-        x_quant(1)
-        w_quant(0, 1)
+        x_quant(0)
         x_out(3, False)
-        x_quant(2)
+        w_quant(0, 1)
         w_out(1)
-        x_quant(3)
+        x_quant(1)
         w_out(2)
         w_quant(1, 1)
         w_perm(4)

@@ -72,11 +72,11 @@ def tile_sae_encode_decode_fp8_d4_kernel(tc, x_bytes, x_scale, w_enc, b_enc, dec
         def load_dec(g):
             nc.sync.dma_start(out=dw[:, g, :].bitcast(I32), in_=dec_words[g].bitcast(I32))
 
-        def load_dec_scales():
-            for q in range(4):
+        def load_dec_scales(lo, hi):
+            for q in (0, 2, 1, 3):
                 nc.sync.dma_start(
-                    out=dsc[32 * q : 32 * q + 4, :, :].bitcast(I32),
-                    in_=dec_scales[:, 4 * q : 4 * q + 4, :].rearrange("g q n -> q g n").bitcast(I32),
+                    out=dsc[32 * q : 32 * q + 4, lo:hi, :].bitcast(I32),
+                    in_=dec_scales[lo:hi, 4 * q : 4 * q + 4, :].rearrange("g q n -> q g n").bitcast(I32),
                 )
 
         xw, xg, sorted_words = {}, {}, {}
@@ -261,13 +261,15 @@ def tile_sae_encode_decode_fp8_d4_kernel(tc, x_bytes, x_scale, w_enc, b_enc, dec
             load_w(f, 2)
             if f == 6:
                 nc.sync.dma_start(out=b_rest[:], in_=b_rows[:, 1:GROUPS, :])
-        load_dec(0)
-        load_dec_scales()
         load_w(14, 2)
+        load_dec(0)
+        load_dec_scales(0, 2)
         for g in range(4, GROUPS):
             load_w(4 * g, 2)
             load_w(4 * g + 2, 2)
             load_dec(g - 3)
+            if g % 2 == 0:
+                load_dec_scales(g - 2, 4 * (g // 2 - 1))
         for g in range(GROUPS - 3, GROUPS):
             load_dec(g)
         nc.sync.dma_start(out=bd[:], in_=b_dec.partition_broadcast(P))

@@ -42,7 +42,6 @@ def tile_sae_encode_decode_fp8_d4_kernel(tc, x_bytes, x_scale, w_enc, b_enc, dec
         xsc = keep.tile([P, 4, 8], F32, name="xsc")
         b_first = keep.tile([P, 1, 4], BF16, name="b_first")
         b_rest = keep.tile([P, GROUPS - 1, 4], BF16, name="b_rest")
-        b_f = keep.tile([P, GROUPS, 4], F32, name="b_f")
         bd = keep.tile([P, K], BF16, name="bd")
         xin = [keep.tile([P, 2, K], U8, name="xin%d" % i) for i in range(2)]
 
@@ -183,7 +182,8 @@ def tile_sae_encode_decode_fp8_d4_kernel(tc, x_bytes, x_scale, w_enc, b_enc, dec
             g, t = f // 4, f % 4
             if g not in zt:
                 zt[g] = work.tile([P, 4, T], BF16, name="zt", bufs=GROUPS)
-            nc.scalar.activation(out=zt[g][:, t, cols], in_=src, func=ACT.Relu, bias=b_f[:, g, t : t + 1], scale=1.0)
+            bias = b_first[:, 0, t : t + 1] if g == 0 else b_rest[:, g - 1, t : t + 1]
+            nc.scalar.activation(out=zt[g][:, t, cols], in_=src, func=ACT.Relu, bias=bias, scale=1.0)
 
         pre = {}
 
@@ -259,7 +259,7 @@ def tile_sae_encode_decode_fp8_d4_kernel(tc, x_bytes, x_scale, w_enc, b_enc, dec
         nc.sync.dma_start(out=b_first[:], in_=b_rows[:, 0:1, :])
         for f in range(6, 14, 2):
             load_w(f, 2)
-            if f == 6:
+            if f == 8:
                 nc.sync.dma_start(out=b_rest[:], in_=b_rows[:, 1:GROUPS, :])
         load_w(14, 2)
         load_dec(0)
@@ -299,14 +299,14 @@ def tile_sae_encode_decode_fp8_d4_kernel(tc, x_bytes, x_scale, w_enc, b_enc, dec
         w_quant(1, 1)
         w_perm(4)
         w_out(3)
-        nc.scalar.copy(out=b_f[:, 0:1, :], in_=b_first[:])
+        for i in range(1):
+            warm_up("acc")
         encode(0)
         encode(1)
         w_perm(6)
         w_quant(2, 2)
         relu_out(0)
         relu_out(1)
-        nc.scalar.copy(out=b_f[:, 1:GROUPS, :], in_=b_rest[:])
 
         last = GROUPS - 1
         for g in range(1, GROUPS):

@@ -201,6 +201,12 @@ def tile_sae_encode_decode_fp8_d4_kernel(tc, x_bytes, x_scale, w_enc, b_enc, dec
             for i in range(2):
                 z_out(f + i, slice(HALF * half, HALF * (half + 1)), pre[f, half][:, i, :])
 
+        def encode_in_halves(f):
+            pre[f] = psum.tile([P, T], F32, name="pre", tag="step")
+            for half in range(2):
+                cols = slice(HALF * half, HALF * (half + 1))
+                passes(pre[f][:, cols], f, cols)
+
         def relu_out(f):
             z_out(f, slice(0, T), pre[f][:])
 
@@ -268,8 +274,9 @@ def tile_sae_encode_decode_fp8_d4_kernel(tc, x_bytes, x_scale, w_enc, b_enc, dec
             load_w(4 * g, 2)
             load_w(4 * g + 2, 2)
             load_dec(g - 3)
-            if g % 2 == 0:
-                load_dec_scales(g - 2, 4 * (g // 2 - 1))
+            if g == 5:
+                load_dec_scales(2, 4)
+        load_dec_scales(4, GROUPS)
         for g in range(GROUPS - 3, GROUPS):
             load_dec(g)
         nc.sync.dma_start(out=bd[:], in_=b_dec.partition_broadcast(P))
@@ -284,9 +291,11 @@ def tile_sae_encode_decode_fp8_d4_kernel(tc, x_bytes, x_scale, w_enc, b_enc, dec
         w_turn(0)
         x_turn(2, "acc")
         x_turn(3, "acc")
-        for f in range(1, 4):
-            w_turn(f)
+        w_turn(1)
         x_out(0, True)
+        warm_up("acc")
+        w_turn(2)
+        w_turn(3)
         x_out(1, False)
         w_out(0, True)
         x_out(2, False)
@@ -299,9 +308,7 @@ def tile_sae_encode_decode_fp8_d4_kernel(tc, x_bytes, x_scale, w_enc, b_enc, dec
         w_quant(1, 1)
         w_perm(4)
         w_out(3)
-        for i in range(1):
-            warm_up("acc")
-        encode(0)
+        encode_in_halves(0)
         encode(1)
         w_perm(6)
         w_quant(2, 2)

@@ -22,7 +22,7 @@ GROUPS = F // 512
 TILES = F // P
 HALF = T // 2
 DIRECT = 4
-WIDEN_V = 5
+VT_FROM = 3
 
 
 def tile_sae_encode_decode_fp8_d4_kernel(tc, x_bytes, x_scale, w_enc, b_enc, dec_words, dec_scales, b_dec, out):
@@ -62,11 +62,23 @@ def tile_sae_encode_decode_fp8_d4_kernel(tc, x_bytes, x_scale, w_enc, b_enc, dec
         raw, pair_raw = {}, {}
 
         def load_w(f, count):
-            tile = work.tile([P, count, K], BF16, name="raw%d" % count, bufs=16)
+            tile = work.tile([P, count, K], BF16, name="raw%d" % count, bufs=11 if count == 2 else 5)
             nc.sync.dma_start(out=tile[:], in_=wr[f // 4][:, f % 4 : f % 4 + count, :])
             for i in range(count):
                 raw[f + i] = tile[:, i, :].bitcast(F32)
             pair_raw[f] = tile[:].bitcast(F32)
+
+        vraw = {}
+        wq = w_enc.rearrange("(a r t) k -> t r a k", r=32, t=4)[3]
+
+        def load_v(lo, hi):
+            tile = keep.tile([P, 4 * (hi - lo), 2, B], BF16, name="vraw%d" % lo)
+            for c in range(2):
+                for q in (0, 2, 1, 3):
+                    k0 = 512 * c + B * q
+                    nc.sync.dma_start(out=tile[32 * q : 32 * (q + 1), :, c, :], in_=wq[:, 4 * lo : 4 * hi, k0 : k0 + B])
+            for g in range(lo, hi):
+                vraw[g] = tile[:, 4 * (g - lo) : 4 * (g - lo + 1), :, :]
 
         def load_dec(g):
             nc.sync.dma_start(out=dw[:, g, :].bitcast(I32), in_=dec_words[g].bitcast(I32))
@@ -130,15 +142,36 @@ def tile_sae_encode_decode_fp8_d4_kernel(tc, x_bytes, x_scale, w_enc, b_enc, dec
 
         perm, wbank, wg, wc, ws = {}, {}, {}, {}, {}
 
-        def w_perm(f):
+        def w_perm(f, count=2):
             if DIRECT <= f < TILES:
                 both = work.tile([P, 2, 2, 2, P], F32, name="perm", bufs=3)
                 nc.vector.tensor_copy(
-                    out=both[:].rearrange("p i c u m -> p (i c) u m"),
+                    out=both[:, 0:count, :, :, :].rearrange("p i c u m -> p (i c) u m"),
                     in_=pair_raw[f].rearrange("p i (c m u) -> p (i c) u m", m=P, u=2),
                 )
-                for i in range(2):
+                for i in range(count):
                     perm[f + i] = both[:, i, :, :, :]
+
+        vsort, vturn = {}, {}
+
+        def v_perm(g):
+            vsort[g] = work.tile([P, 8, 2, 32], F32, name="vsort", bufs=2, align_bytes=64)
+            words = vraw[g].rearrange("p a c k -> p (a c) k").bitcast(F32)
+            nc.vector.tensor_copy(out=vsort[g][:], in_=words.rearrange("p b (j u) -> p b u j", u=2))
+
+        def v_turn(g):
+            vturn[g] = work.tile([P, 4, 2, 2, 32], F32, name="vturn", bufs=2, align_bytes=64)
+            nc.vector.transpose(
+                out=vturn[g][:].rearrange("p a c u r -> p (a c u r)"),
+                in_=vsort[g][:].rearrange("p b u j -> p (b u j)"),
+            )
+
+        def v_out(g):
+            words = wg[2 * g + 1][:, 1, :, :, :].rearrange("p c r t -> p (c r t)").bitcast(F32)
+            nc.vector.tensor_copy(
+                out=words.rearrange("p (c a r u) -> p c a r u", c=2, a=4, u=2),
+                in_=vturn[g][:].rearrange("p a c u r -> p c a r u"),
+            )
 
         def w_turn(f, tag="step"):
             if f in perm:
@@ -241,10 +274,10 @@ def tile_sae_encode_decode_fp8_d4_kernel(tc, x_bytes, x_scale, w_enc, b_enc, dec
             )
 
         def store_cols(bank, n, lo, width):
-            o = work.tile([P, 512], F32, name="o", bufs=5)
+            o = work.tile([P, width], F32, name="o%d" % width, bufs=5 if width == 512 else 4)
             cols = slice(lo, lo + width)
-            nc.vector.tensor_tensor(out=o[:, 0:width], in0=bank[:, 0:width], in1=bd[:, cols], op=ALU.add)
-            nc.sync.dma_start(out=orows[n][:, cols], in_=o[:, 0:width])
+            nc.vector.tensor_tensor(out=o[:], in0=bank[:, 0:width], in1=bd[:, cols], op=ALU.add)
+            nc.sync.dma_start(out=orows[n][:, cols], in_=o[:])
 
         def decode(half, g, b):
             if g == 0:
@@ -267,16 +300,19 @@ def tile_sae_encode_decode_fp8_d4_kernel(tc, x_bytes, x_scale, w_enc, b_enc, dec
             load_w(f, 2)
             if f == 8:
                 nc.sync.dma_start(out=b_rest[:], in_=b_rows[:, 1:GROUPS, :])
-        load_w(14, 2)
+        load_w(14, 1)
         load_dec(0)
         load_dec_scales(0, 2)
+        load_v(3, 4)
         for g in range(4, GROUPS):
             load_w(4 * g, 2)
-            load_w(4 * g + 2, 2)
+            load_w(4 * g + 2, 1)
+            if g % 2 == 1:
+                load_dec_scales(g - 3, g - 1)
             load_dec(g - 3)
-            if g == 5:
-                load_dec_scales(2, 4)
-        load_dec_scales(4, GROUPS)
+            if g % 2 == 0:
+                load_v(g, g + 2)
+        load_dec_scales(6, GROUPS)
         for g in range(GROUPS - 3, GROUPS):
             load_dec(g)
         nc.sync.dma_start(out=bd[:], in_=b_dec.partition_broadcast(P))
@@ -316,17 +352,14 @@ def tile_sae_encode_decode_fp8_d4_kernel(tc, x_bytes, x_scale, w_enc, b_enc, dec
         relu_out(1)
 
         last = GROUPS - 1
-        for g in range(1, GROUPS):
+        for g in range(1, VT_FROM):
             first = 4 * g
             for f in range(first, first + 4):
-                w_turn(f, "acc" if g <= 2 else "step")
+                w_turn(f, "acc")
                 w_out(f, f == first + 1)
             if g >= 2:
                 z_quant(0, g - 2)
             w_quant(first, 2)
-            if g >= 3:
-                for b in range(2, 4):
-                    decode(0, g - 3, b)
             for f in range(first - 2, first + 2):
                 encode(f)
                 relu_out(f)
@@ -334,19 +367,38 @@ def tile_sae_encode_decode_fp8_d4_kernel(tc, x_bytes, x_scale, w_enc, b_enc, dec
                 for b in range(2):
                     decode(0, g - 2, b)
             w_perm(first + 4)
+            w_quant(first + 2, 2)
+            w_perm(first + 6, 1 if g + 1 == VT_FROM else 2)
+            z_lace(0, g - 1)
+        for g in range(VT_FROM, GROUPS):
+            first = 4 * g
+            for f in range(first, first + 3):
+                w_turn(f)
+                w_out(f)
+            v_perm(g)
+            z_quant(0, g - 2)
+            v_turn(g)
+            w_quant(first, 2)
+            v_out(g)
+            for b in range(2 if g == VT_FROM else 1, 4):
+                decode(0, g - 3, b)
+            for f in range(first - 2, first + 2):
+                encode(f)
+                relu_out(f)
+            decode(0, g - 2, 0)
+            w_perm(first + 4)
+            if g == last:
+                z_lace(1, 0)
+            w_quant(first + 2, 2)
+            w_perm(first + 6, 1)
             if g == last:
                 z_lace(1, 1)
-            w_quant(first + 2, 2)
-            w_perm(first + 6)
-            if g == last:
                 z_quant(1, 0)
             z_lace(0, g - 1)
-            if g == last - 1:
-                z_lace(1, 0)
 
         z_quant(1, 1)
         z_quant(0, last - 1)
-        for b in range(2, 4):
+        for b in range(1, 4):
             decode(0, last - 2, b)
         for f in range(TILES - 2, TILES):
             encode(f)

@@ -33,15 +33,15 @@ def tile_sae_encode_decode_fp8_d4_kernel(tc, x_bytes, x_scale, w_enc, b_enc, dec
         psum = ctx.enter_context(tc.psum_pool(name="psum", bufs=4))
 
         ident = keep.tile([P, P], F32, name="ident")
-        dsc = keep.tile([P, GROUPS, K], U8, name="dsc", align_bytes=64)
+        dsc = [keep.tile([P, 2 * K], U8, name="dsc%d" % i, align_bytes=64) for i in range(GROUPS // 2)]
         dw = keep.tile([P, GROUPS, 2 * K], U8, name="dw", align_bytes=64)
         zc = keep.tile([P, GROUPS, T], U32, name="zc", align_bytes=64)
         zs = keep.tile([P, GROUPS, T], U8, name="zs", align_bytes=64)
         xc = keep.tile([P, 2, T], U32, name="xc", align_bytes=64)
         xs = keep.tile([P, 2, T], U8, name="xs", align_bytes=64)
         xsc = keep.tile([P, 4, 8], F32, name="xsc")
-        b_first = keep.tile([P, 1, 4], BF16, name="b_first")
-        b_rest = keep.tile([P, GROUPS - 1, 4], BF16, name="b_rest")
+        b_rows = keep.tile([P, 512], BF16, name="b_rows")
+        b_cols = keep.tile([P, GROUPS, 4], BF16, name="b_cols")
         bd = keep.tile([P, K], BF16, name="bd")
         xin = [keep.tile([P, 2, K], U8, name="xin%d" % i) for i in range(2)]
 
@@ -50,8 +50,10 @@ def tile_sae_encode_decode_fp8_d4_kernel(tc, x_bytes, x_scale, w_enc, b_enc, dec
         warm = keep.tile([P, 512], BF16, name="warm")
         early = keep.tile([P, 2], BF16, name="early")
         make_identity(nc, ident[:])
+        nc.vector.memset(b_rows[:], 0.0)
         nc.vector.memset(warm[:], 0.0)
-        nc.vector.memset(dsc[:].rearrange("p g n -> p (g n)").bitcast(I32), 0)
+        for plane in dsc:
+            nc.vector.memset(plane[:].bitcast(I32), 0)
 
         def warm_up(tag):
             idle = psum.tile([P, 512], F32, name="idle", tag=tag)
@@ -62,7 +64,7 @@ def tile_sae_encode_decode_fp8_d4_kernel(tc, x_bytes, x_scale, w_enc, b_enc, dec
         raw, pair_raw = {}, {}
 
         def load_w(f, count):
-            tile = work.tile([P, count, K], BF16, name="raw%d" % count, bufs=11 if count == 2 else 5)
+            tile = work.tile([P, count, K], BF16, name="raw%d" % count, bufs=6 if count == 2 else 5)
             nc.sync.dma_start(out=tile[:], in_=wr[f // 4][:, f % 4 : f % 4 + count, :])
             for i in range(count):
                 raw[f + i] = tile[:, i, :].bitcast(F32)
@@ -84,10 +86,10 @@ def tile_sae_encode_decode_fp8_d4_kernel(tc, x_bytes, x_scale, w_enc, b_enc, dec
             nc.sync.dma_start(out=dw[:, g, :].bitcast(I32), in_=dec_words[g].bitcast(I32))
 
         def load_dec_scales(lo, hi):
-            for q in (0, 2, 1, 3):
+            for r in range(4):
                 nc.sync.dma_start(
-                    out=dsc[32 * q : 32 * q + 4, lo:hi, :].bitcast(I32),
-                    in_=dec_scales[lo:hi, 4 * q : 4 * q + 4, :].rearrange("g q n -> q g n").bitcast(I32),
+                    out=dsc[lo // 2][r:P:32, :].bitcast(I32),
+                    in_=dec_scales[lo:hi, r:16:4, :].rearrange("g q n -> q g n").bitcast(I32),
                 )
 
         xw, xg, sorted_words = {}, {}, {}
@@ -144,9 +146,9 @@ def tile_sae_encode_decode_fp8_d4_kernel(tc, x_bytes, x_scale, w_enc, b_enc, dec
 
         def w_perm(f, count=2):
             if DIRECT <= f < TILES:
-                both = work.tile([P, 2, 2, 2, P], F32, name="perm", bufs=3)
+                both = work.tile([P, count, 2, 2, P], F32, name="perm", bufs=2)
                 nc.vector.tensor_copy(
-                    out=both[:, 0:count, :, :, :].rearrange("p i c u m -> p (i c) u m"),
+                    out=both[:].rearrange("p i c u m -> p (i c) u m"),
                     in_=pair_raw[f].rearrange("p i (c m u) -> p (i c) u m", m=P, u=2),
                 )
                 for i in range(count):
@@ -215,7 +217,7 @@ def tile_sae_encode_decode_fp8_d4_kernel(tc, x_bytes, x_scale, w_enc, b_enc, dec
             g, t = f // 4, f % 4
             if g not in zt:
                 zt[g] = work.tile([P, 4, T], BF16, name="zt", bufs=GROUPS)
-            bias = b_first[:, 0, t : t + 1] if g == 0 else b_rest[:, g - 1, t : t + 1]
+            bias = b_cols[:, g, t : t + 1]
             nc.scalar.activation(out=zt[g][:, t, cols], in_=src, func=ACT.Relu, bias=bias, scale=1.0)
 
         pre = {}
@@ -268,7 +270,7 @@ def tile_sae_encode_decode_fp8_d4_kernel(tc, x_bytes, x_scale, w_enc, b_enc, dec
                 lhsT=zc[:, g, P * n : P * (n + 1)].bitcast(FP8X4),
                 lhsT_scale=zs[:, g, P * n : P * (n + 1)],
                 rhs=dw[:, g, 2 * lo : 2 * (lo + width)].bitcast(FP4X4),
-                rhs_scale=dsc[:, g, lo : lo + width],
+                rhs_scale=dsc[g // 2][:, K * (g % 2) + lo : K * (g % 2) + lo + width],
                 start=(g == 0),
                 stop=(g == GROUPS - 1),
             )
@@ -287,26 +289,19 @@ def tile_sae_encode_decode_fp8_d4_kernel(tc, x_bytes, x_scale, w_enc, b_enc, dec
         def store(half, b):
             store_cols(acc[half, b], 2 * half + b // 2, 512 * (b % 2), 512)
 
-        b_rows = b_enc.rearrange("(g p t) -> p g t", p=P, t=4)
         nc.scalar.dma_start(out=xsc[:], in_=x_scale.rearrange("(p n) b -> p n b", p=P))
-        nc.scalar.activation(out=early[:], in_=warm[:, 0:2], func=ACT.Copy)
         nc.sync.dma_start(out=xin[0][:], in_=xr[0])
         nc.sync.dma_start(out=xin[1][:], in_=xr[1])
-        load_w(0, 2)
-        load_w(2, 2)
-        load_w(4, 2)
-        nc.sync.dma_start(out=b_first[:], in_=b_rows[:, 0:1, :])
-        for f in range(6, 14, 2):
+        nc.scalar.dma_start(out=b_rows[0:GROUPS, :], in_=b_enc.rearrange("(g k) -> g k", g=GROUPS))
+        nc.scalar.activation(out=early[:], in_=warm[:, 0:2], func=ACT.Copy)
+        for f in range(0, 4 * VT_FROM, 2):
             load_w(f, 2)
-            if f == 8:
-                nc.sync.dma_start(out=b_rest[:], in_=b_rows[:, 1:GROUPS, :])
-        load_w(14, 1)
+        load_w(12, 3)
         load_dec(0)
         load_dec_scales(0, 2)
         load_v(3, 4)
         for g in range(4, GROUPS):
-            load_w(4 * g, 2)
-            load_w(4 * g + 2, 1)
+            load_w(4 * g, 3)
             if g % 2 == 1:
                 load_dec_scales(g - 3, g - 1)
             load_dec(g - 3)
@@ -319,9 +314,13 @@ def tile_sae_encode_decode_fp8_d4_kernel(tc, x_bytes, x_scale, w_enc, b_enc, dec
 
         for i in range(4):
             warm_up("step")
+        b_bank = psum.tile([P, 2, P], F32, name="b_bank", tag="step")
+        for u in range(2):
+            nc.tensor.transpose(b_bank[:, u, :], b_rows[:].bitcast(F32)[:, u : 2 * P : 2], ident[:])
         for n in range(4):
             x_widen(n, 0, True)
             x_widen(n, 1, n == 3)
+        nc.scalar.copy(out=b_cols[:].bitcast(F32), in_=b_bank[:, :, 0:GROUPS].rearrange("p u g -> p g u"))
         x_turn(0, "acc")
         x_turn(1, "acc")
         w_turn(0)
@@ -366,9 +365,10 @@ def tile_sae_encode_decode_fp8_d4_kernel(tc, x_bytes, x_scale, w_enc, b_enc, dec
             if g >= 2:
                 for b in range(2):
                     decode(0, g - 2, b)
-            w_perm(first + 4)
+            w_perm(first + 4, 3 if g + 1 == VT_FROM else 2)
             w_quant(first + 2, 2)
-            w_perm(first + 6, 1 if g + 1 == VT_FROM else 2)
+            if g + 1 < VT_FROM:
+                w_perm(first + 6)
             z_lace(0, g - 1)
         for g in range(VT_FROM, GROUPS):
             first = 4 * g
@@ -386,11 +386,10 @@ def tile_sae_encode_decode_fp8_d4_kernel(tc, x_bytes, x_scale, w_enc, b_enc, dec
                 encode(f)
                 relu_out(f)
             decode(0, g - 2, 0)
-            w_perm(first + 4)
+            w_perm(first + 4, 3)
             if g == last:
                 z_lace(1, 0)
             w_quant(first + 2, 2)
-            w_perm(first + 6, 1)
             if g == last:
                 z_lace(1, 1)
                 z_quant(1, 0)

@@ -50,8 +50,8 @@ def tile_sae_encode_decode_fp8_d4_kernel(tc, x_bytes, x_scale, w_enc, b_enc, dec
         warm = keep.tile([P, 512], BF16, name="warm")
         early = keep.tile([P, 2], BF16, name="early")
         make_identity(nc, ident[:])
-        nc.vector.memset(b_rows[:], 0.0)
         nc.vector.memset(warm[:], 0.0)
+        nc.vector.memset(b_rows[:].bitcast(I32), 0)
         for plane in dsc:
             nc.vector.memset(plane[:].bitcast(I32), 0)
 
@@ -290,10 +290,10 @@ def tile_sae_encode_decode_fp8_d4_kernel(tc, x_bytes, x_scale, w_enc, b_enc, dec
             store_cols(acc[half, b], 2 * half + b // 2, 512 * (b % 2), 512)
 
         nc.scalar.dma_start(out=xsc[:], in_=x_scale.rearrange("(p n) b -> p n b", p=P))
+        nc.scalar.activation(out=early[:], in_=warm[:, 0:2], func=ACT.Copy)
         nc.sync.dma_start(out=xin[0][:], in_=xr[0])
         nc.sync.dma_start(out=xin[1][:], in_=xr[1])
-        nc.scalar.dma_start(out=b_rows[0:GROUPS, :], in_=b_enc.rearrange("(g k) -> g k", g=GROUPS))
-        nc.scalar.activation(out=early[:], in_=warm[:, 0:2], func=ACT.Copy)
+        nc.sync.dma_start(out=b_rows[0:GROUPS, :], in_=b_enc.rearrange("(g k) -> g k", g=GROUPS))
         for f in range(0, 4 * VT_FROM, 2):
             load_w(f, 2)
         load_w(12, 3)
@@ -314,15 +314,15 @@ def tile_sae_encode_decode_fp8_d4_kernel(tc, x_bytes, x_scale, w_enc, b_enc, dec
 
         for i in range(4):
             warm_up("step")
-        b_bank = psum.tile([P, 2, P], F32, name="b_bank", tag="step")
-        for u in range(2):
-            nc.tensor.transpose(b_bank[:, u, :], b_rows[:].bitcast(F32)[:, u : 2 * P : 2], ident[:])
         for n in range(4):
             x_widen(n, 0, True)
             x_widen(n, 1, n == 3)
-        nc.scalar.copy(out=b_cols[:].bitcast(F32), in_=b_bank[:, :, 0:GROUPS].rearrange("p u g -> p g u"))
+        b_bank = psum.tile([P, 2, P], F32, name="b_bank", tag="step")
+        for u in range(2):
+            nc.tensor.transpose(b_bank[:, u, :], b_rows[:].bitcast(F32)[:, u : 2 * P : 2], ident[:])
         x_turn(0, "acc")
         x_turn(1, "acc")
+        nc.scalar.copy(out=b_cols[:].bitcast(F32), in_=b_bank[:, :, 0:GROUPS].rearrange("p u g -> p g u"))
         w_turn(0)
         x_turn(2, "acc")
         x_turn(3, "acc")

@@ -148,8 +148,8 @@ def tile_sae_encode_decode_fp8_d4_kernel(tc, x_bytes, x_scale, w_enc, b_enc, dec
             if DIRECT <= f < TILES:
                 both = work.tile([P, count, 2, 2, P], F32, name="perm", bufs=2)
                 nc.vector.tensor_copy(
-                    out=both[:].rearrange("p i c u m -> p (i c) u m"),
-                    in_=pair_raw[f].rearrange("p i (c m u) -> p (i c) u m", m=P, u=2),
+                    out=both[:].rearrange("p i c u (m j) -> p (i c) m u j", j=4),
+                    in_=pair_raw[f].rearrange("p i (c m j u) -> p (i c) m u j", m=32, j=4, u=2),
                 )
                 for i in range(count):
                     perm[f + i] = both[:, i, :, :, :]
@@ -159,7 +159,10 @@ def tile_sae_encode_decode_fp8_d4_kernel(tc, x_bytes, x_scale, w_enc, b_enc, dec
         def v_perm(g):
             vsort[g] = work.tile([P, 8, 2, 32], F32, name="vsort", bufs=2, align_bytes=64)
             words = vraw[g].rearrange("p a c k -> p (a c) k").bitcast(F32)
-            nc.vector.tensor_copy(out=vsort[g][:], in_=words.rearrange("p b (j u) -> p b u j", u=2))
+            nc.vector.tensor_copy(
+                out=vsort[g][:].rearrange("p b u (m j) -> p b m u j", j=4),
+                in_=words.rearrange("p b (m j u) -> p b m u j", j=4, u=2),
+            )
 
         def v_turn(g):
             vturn[g] = work.tile([P, 4, 2, 2, 32], F32, name="vturn", bufs=2, align_bytes=64)
@@ -276,7 +279,7 @@ def tile_sae_encode_decode_fp8_d4_kernel(tc, x_bytes, x_scale, w_enc, b_enc, dec
             )
 
         def store_cols(bank, n, lo, width):
-            o = work.tile([P, width], F32, name="o%d" % width, bufs=5 if width == 512 else 4)
+            o = work.tile([P, width], F32, name="o%d" % width, bufs=5 if width == 512 else 2)
             cols = slice(lo, lo + width)
             nc.vector.tensor_tensor(out=o[:], in0=bank[:, 0:width], in1=bd[:, cols], op=ALU.add)
             nc.sync.dma_start(out=orows[n][:, cols], in_=o[:])
@@ -430,8 +433,8 @@ def tile_sae_encode_decode_fp8_d4_kernel(tc, x_bytes, x_scale, w_enc, b_enc, dec
             for g in range(5, GROUPS):
                 decode(1, g, b)
             store(1, b)
-        for q in range(4):
+        for lo, width in ((512, 256), (768, P), (896, P)):
             piece = psum.tile([P, 512], F32, name="piece", tag="acc")
             for g in range(GROUPS):
-                decode_cols(piece, 3, g, 512 + P * q, P)
-            store_cols(piece, 3, 512 + P * q, P)
+                decode_cols(piece, 3, g, lo, width)
+            store_cols(piece, 3, lo, width)

@@ -33,7 +33,7 @@ def tile_sae_encode_decode_fp8_d4_kernel(tc, x_bytes, x_scale, w_enc, b_enc, dec
         psum = ctx.enter_context(tc.psum_pool(name="psum", bufs=4))
 
         ident = keep.tile([P, P], F32, name="ident")
-        dsc = [keep.tile([P, 2 * K], U8, name="dsc%d" % i, align_bytes=64) for i in range(GROUPS // 2)]
+        dsc = [keep.tile([P, n * K], U8, name="dsc%d" % i, align_bytes=64) for i, n in enumerate((2, 2, 4))]
         dw = keep.tile([P, GROUPS, 2 * K], U8, name="dw", align_bytes=64)
         zc = keep.tile([P, GROUPS, T], U32, name="zc", align_bytes=64)
         zs = keep.tile([P, GROUPS, T], U8, name="zs", align_bytes=64)
@@ -96,7 +96,7 @@ def tile_sae_encode_decode_fp8_d4_kernel(tc, x_bytes, x_scale, w_enc, b_enc, dec
 
         def x_widen(n, c, on_vector):
             if n not in xw:
-                xw[n] = work.tile([P, 2, 512], BF16, name="xw", bufs=4)
+                xw[n] = work.tile([P, 2, 512], BF16, name="xw", tag="laced", align_bytes=64, bufs=6)
             sorted_words[n, c] = on_vector
             for q in range(4):
                 src = xin[n // 2][:, n % 2, 512 * c + B * q : 512 * c + B * (q + 1)].bitcast(FP8)
@@ -249,7 +249,7 @@ def tile_sae_encode_decode_fp8_d4_kernel(tc, x_bytes, x_scale, w_enc, b_enc, dec
             z_out(f, slice(0, T), pre[f][:])
 
         def z_lace(half, g, on_vector=True):
-            zi[half, g] = work.tile([P, HALF, 4], BF16, name="zi", align_bytes=64, bufs=5)
+            zi[half, g] = work.tile([P, HALF, 4], BF16, name="zi", tag="laced", align_bytes=64, bufs=6)
             copy = nc.vector.tensor_copy if on_vector else nc.scalar.copy
             copy(
                 out=zi[half, g][:].rearrange("p (c i) t -> p c t i", i=4),
@@ -268,18 +268,19 @@ def tile_sae_encode_decode_fp8_d4_kernel(tc, x_bytes, x_scale, w_enc, b_enc, dec
         orows = out.rearrange("(p n) k -> n p k", p=P)
 
         def decode_cols(bank, n, g, lo, width):
+            part = min(g // 2, 2)
             nc.tensor.matmul_mx(
                 out=bank[:, 0:width],
                 lhsT=zc[:, g, P * n : P * (n + 1)].bitcast(FP8X4),
                 lhsT_scale=zs[:, g, P * n : P * (n + 1)],
                 rhs=dw[:, g, 2 * lo : 2 * (lo + width)].bitcast(FP4X4),
-                rhs_scale=dsc[g // 2][:, K * (g % 2) + lo : K * (g % 2) + lo + width],
+                rhs_scale=dsc[part][:, K * (g - 2 * part) + lo : K * (g - 2 * part) + lo + width],
                 start=(g == 0),
                 stop=(g == GROUPS - 1),
             )
 
         def store_cols(bank, n, lo, width):
-            o = work.tile([P, width], F32, name="o%d" % width, bufs=5 if width == 512 else 2)
+            o = work.tile([P, width], F32, name="o%d" % width, bufs=7 if width == 512 else 2)
             cols = slice(lo, lo + width)
             nc.vector.tensor_tensor(out=o[:], in0=bank[:, 0:width], in1=bd[:, cols], op=ALU.add)
             nc.sync.dma_start(out=orows[n][:, cols], in_=o[:])
@@ -306,11 +307,10 @@ def tile_sae_encode_decode_fp8_d4_kernel(tc, x_bytes, x_scale, w_enc, b_enc, dec
         for g in range(4, GROUPS):
             load_w(4 * g, 3)
             if g % 2 == 1:
-                load_dec_scales(g - 3, g - 1)
+                load_dec_scales(g - 3, g - 1 if g < 7 else GROUPS)
             load_dec(g - 3)
             if g % 2 == 0:
                 load_v(g, g + 2)
-        load_dec_scales(6, GROUPS)
         for g in range(GROUPS - 3, GROUPS):
             load_dec(g)
         nc.sync.dma_start(out=bd[:], in_=b_dec.partition_broadcast(P))
@@ -358,17 +358,20 @@ def tile_sae_encode_decode_fp8_d4_kernel(tc, x_bytes, x_scale, w_enc, b_enc, dec
             first = 4 * g
             for f in range(first, first + 4):
                 w_turn(f, "acc")
-                w_out(f, f == first + 1)
+                w_out(f, f == first)
             if g >= 2:
                 z_quant(0, g - 2)
-            w_quant(first, 2)
+            else:
+                w_perm(first + 4)
+            w_quant(first, 1)
+            w_quant(first + 1, 1)
             for f in range(first - 2, first + 2):
                 encode(f)
                 relu_out(f)
             if g >= 2:
                 for b in range(2):
                     decode(0, g - 2, b)
-            w_perm(first + 4, 3 if g + 1 == VT_FROM else 2)
+                w_perm(first + 4, 3)
             w_quant(first + 2, 2)
             if g + 1 < VT_FROM:
                 w_perm(first + 6)
@@ -394,11 +397,10 @@ def tile_sae_encode_decode_fp8_d4_kernel(tc, x_bytes, x_scale, w_enc, b_enc, dec
                 z_lace(1, 0)
             w_quant(first + 2, 2)
             if g == last:
-                z_lace(1, 1)
                 z_quant(1, 0)
             z_lace(0, g - 1)
 
-        z_quant(1, 1)
+        z_lace(1, 1)
         z_quant(0, last - 1)
         for b in range(1, 4):
             decode(0, last - 2, b)
@@ -406,13 +408,13 @@ def tile_sae_encode_decode_fp8_d4_kernel(tc, x_bytes, x_scale, w_enc, b_enc, dec
             encode(f)
             relu_out(f)
         z_lace(1, 2)
+        z_quant(1, 1)
         z_lace(1, 3)
         z_quant(1, 2)
         z_lace(0, last)
         z_quant(1, 3)
         z_quant(0, last)
-        z_lace(1, 4)
-        for g in range(5, GROUPS):
+        for g in range(4, GROUPS):
             z_lace(1, g, False)
         z_quant(1, 4)
         for b in range(4):

@@ -21,19 +21,21 @@ P = 128
 GROUPS = F // 512
 TILES = F // P
 HALF = T // 2
-DIRECT = 4
-VT_FROM = 3
+RUN = 16
+BY_VECTOR = 3
+SCALE_PARTS = ((0, 2), (2, 4), (4, 8))
 
 
 def tile_sae_encode_decode_fp8_d4_kernel(tc, x_bytes, x_scale, w_enc, b_enc, dec_words, dec_scales, b_dec, out):
     nc = tc.nc
+    last = GROUPS - 1
     with ExitStack() as ctx:
         keep = ctx.enter_context(tc.tile_pool(name="keep", bufs=1))
-        work = ctx.enter_context(tc.tile_pool(name="work", bufs=3))
+        work = ctx.enter_context(tc.tile_pool(name="work", bufs=2))
         psum = ctx.enter_context(tc.psum_pool(name="psum", bufs=4))
 
         ident = keep.tile([P, P], F32, name="ident")
-        dsc = [keep.tile([P, n * K], U8, name="dsc%d" % i, align_bytes=64) for i, n in enumerate((2, 2, 4))]
+        dsc = [keep.tile([P, (hi - lo) * K], U8, name="dsc%d" % lo, align_bytes=64) for lo, hi in SCALE_PARTS]
         dw = keep.tile([P, GROUPS, 2 * K], U8, name="dw", align_bytes=64)
         zc = keep.tile([P, GROUPS, T], U32, name="zc", align_bytes=64)
         zs = keep.tile([P, GROUPS, T], U8, name="zs", align_bytes=64)
@@ -44,11 +46,11 @@ def tile_sae_encode_decode_fp8_d4_kernel(tc, x_bytes, x_scale, w_enc, b_enc, dec
         b_cols = keep.tile([P, GROUPS, 4], BF16, name="b_cols")
         bd = keep.tile([P, K], BF16, name="bd")
         xin = [keep.tile([P, 2, K], U8, name="xin%d" % i) for i in range(2)]
+        warm = keep.tile([P, 512], BF16, name="warm")
+        early = keep.tile([P, 2], BF16, name="early")
 
         ctx.enter_context(tc.manual_schedule())
 
-        warm = keep.tile([P, 512], BF16, name="warm")
-        early = keep.tile([P, 2], BF16, name="early")
         make_identity(nc, ident[:])
         nc.vector.memset(warm[:], 0.0)
         nc.vector.memset(b_rows[:].bitcast(I32), 0)
@@ -61,75 +63,66 @@ def tile_sae_encode_decode_fp8_d4_kernel(tc, x_bytes, x_scale, w_enc, b_enc, dec
 
         xr = x_bytes.rearrange("(p i n) k -> i p n k", p=P, n=2)
         wr = w_enc.rearrange("(g m t) k -> g m t k", m=P, t=4)
-        raw, pair_raw = {}, {}
+        wq = w_enc.rearrange("(a r t) k -> t r a k", r=32, t=4)[3]
+        raw, vraw = {}, {}
 
         def load_w(f, count):
-            tile = work.tile([P, count, K], BF16, name="raw%d" % count, bufs=6 if count == 2 else 5)
-            nc.sync.dma_start(out=tile[:], in_=wr[f // 4][:, f % 4 : f % 4 + count, :])
-            for i in range(count):
-                raw[f + i] = tile[:, i, :].bitcast(F32)
-            pair_raw[f] = tile[:].bitcast(F32)
-
-        vraw = {}
-        wq = w_enc.rearrange("(a r t) k -> t r a k", r=32, t=4)[3]
+            raw[f] = work.tile([P, count, K], BF16, name="raw%d" % count, bufs=6 if count == 2 else 5)
+            nc.sync.dma_start(out=raw[f][:], in_=wr[f // 4][:, f % 4 : f % 4 + count, :])
 
         def load_v(lo, hi):
-            tile = keep.tile([P, 4 * (hi - lo), 2, B], BF16, name="vraw%d" % lo)
-            for c in range(2):
-                for q in (0, 2, 1, 3):
-                    k0 = 512 * c + B * q
-                    nc.sync.dma_start(out=tile[32 * q : 32 * (q + 1), :, c, :], in_=wq[:, 4 * lo : 4 * hi, k0 : k0 + B])
+            tile = keep.tile([P, 4 * (hi - lo), 256], BF16, name="vraw%d" % lo)
+            for q in (0, 2, 1, 3):
+                nc.sync.dma_start(out=tile[32 * q : 32 * (q + 1), :, :], in_=wq[:, 4 * lo : 4 * hi, 256 * q : 256 * (q + 1)])
             for g in range(lo, hi):
-                vraw[g] = tile[:, 4 * (g - lo) : 4 * (g - lo + 1), :, :]
+                vraw[g] = tile[:, 4 * (g - lo) : 4 * (g - lo + 1), :]
 
         def load_dec(g):
             nc.sync.dma_start(out=dw[:, g, :].bitcast(I32), in_=dec_words[g].bitcast(I32))
 
-        def load_dec_scales(lo, hi):
+        def load_dec_scales(part):
+            lo, hi = SCALE_PARTS[part]
             for r in range(4):
                 nc.sync.dma_start(
-                    out=dsc[lo // 2][r:P:32, :].bitcast(I32),
+                    out=dsc[part][r:P:32, :].bitcast(I32),
                     in_=dec_scales[lo:hi, r:16:4, :].rearrange("g q n -> q g n").bitcast(I32),
                 )
 
-        xw, xg, sorted_words = {}, {}, {}
+        def deal(dst, src, on_vector=True):
+            copy = nc.vector.tensor_copy if on_vector else nc.scalar.copy
+            copy(out=dst.rearrange("p s (m j) -> p m s j", j=RUN), in_=src.rearrange("p (m s j) -> p m s j", s=4, j=RUN))
 
-        def x_widen(n, c, on_vector):
-            if n not in xw:
-                xw[n] = work.tile([P, 2, 512], BF16, name="xw", tag="laced", align_bytes=64, bufs=6)
-            sorted_words[n, c] = on_vector
-            for q in range(4):
-                src = xin[n // 2][:, n % 2, 512 * c + B * q : 512 * c + B * (q + 1)].bitcast(FP8)
-                s = xsc[:, n, 4 * c + q : 4 * c + q + 1]
-                if on_vector:
-                    dst = xw[n][:, c, :].rearrange("p (u m e) -> p m u e", u=2, e=2)[:, 32 * q : 32 * (q + 1), :, :]
-                    nc.vector.tensor_scalar(out=dst, in0=src, scalar1=s, scalar2=None, op0=ALU.mult)
-                else:
-                    nc.scalar.activation(out=xw[n][:, c, B * q : B * (q + 1)], in_=src, func=ACT.Copy, scale=s)
-
-        def turn(words, in_order, tag):
-            bank = psum.tile([P, 2, 2, P], F32, name="turned", tag=tag)
-            for c in range(2):
-                for u in range(2):
-                    src = words[:, c, P * u : P * (u + 1)] if in_order[c] else words[:, c, u : 2 * P : 2]
-                    nc.tensor.transpose(bank[:, c, u, :], src, ident[:])
+        def turn(rows, tag):
+            bank = psum.tile([P, 4, P], F32, name="turned", tag=tag)
+            for s in range(4):
+                nc.tensor.transpose(bank[:, s, :], rows[:, s, :].bitcast(F32), ident[:])
             return bank
 
         def words_out(words, bank, on_vector):
-            src = bank[:].rearrange("p c u r -> p c r u")
-            if on_vector:
-                nc.vector.tensor_copy(out=words, in_=src)
-            else:
-                nc.scalar.copy(out=words, in_=src)
+            copy = nc.vector.tensor_copy if on_vector else nc.scalar.copy
+            copy(out=words, in_=bank[:].rearrange("p (c u) r -> p c r u", u=2))
 
-        xbank = {}
+        xw, flat, xg, xbank = {}, {}, {}, {}
 
-        def x_turn(n, tag):
-            xbank[n] = turn(xw[n][:].bitcast(F32), [sorted_words[n, c] for c in range(2)], tag)
+        def x_widen(n, on_vector):
+            xw[n] = work.tile([P, 4, 256], BF16, name="xw", tag="laced", align_bytes=64, bufs=6)
+            if not on_vector:
+                flat[n] = work.tile([P, K], BF16, name="flat", tag="laced", align_bytes=64, bufs=6)
+            for block in range(8):
+                src = xin[n // 2][:, n % 2, B * block : B * (block + 1)].bitcast(FP8)
+                s = xsc[:, n, block : block + 1]
+                if on_vector:
+                    dst = xw[n][:, :, 32 * block : 32 * (block + 1)].rearrange("p s (m j) -> p m s j", j=RUN)
+                    nc.vector.tensor_scalar(out=dst, in0=src, scalar1=s, scalar2=None, op0=ALU.mult)
+                else:
+                    nc.scalar.activation(out=flat[n][:, B * block : B * (block + 1)], in_=src, func=ACT.Copy, scale=s)
 
-        def x_out(n, on_vector):
-            if n % 2 == 0:
-                xg[n // 2] = work.tile([P, 2, 2, P, 4], BF16, name="xg", bufs=2, align_bytes=64)
+        def x_turn(n):
+            xbank[n] = turn(xw[n][:], "acc")
+
+        def x_out(n, on_vector=False):
+            if n // 2 not in xg:
+                xg[n // 2] = work.tile([P, 2, 2, P, 4], BF16, name="xg", align_bytes=64)
             words = xg[n // 2][:].rearrange("p c i r t -> p c i (r t)").bitcast(F32)[:, :, n % 2, :]
             words_out(words.rearrange("p c (r u) -> p c r u", u=2), xbank[n], on_vector)
 
@@ -142,53 +135,38 @@ def tile_sae_encode_decode_fp8_d4_kernel(tc, x_bytes, x_scale, w_enc, b_enc, dec
                     in_=xg[half][:, c, :, :, :].rearrange("p i r t -> p (i r t)"),
                 )
 
-        perm, wbank, wg, wc, ws = {}, {}, {}, {}, {}
+        dealt, wbank, wg, wc, ws, vsort, vturn = {}, {}, {}, {}, {}, {}, {}
 
-        def w_perm(f, count=2):
-            if DIRECT <= f < TILES:
-                both = work.tile([P, count, 2, 2, P], F32, name="perm", bufs=2)
-                nc.vector.tensor_copy(
-                    out=both[:].rearrange("p i c u (m j) -> p (i c) m u j", j=4),
-                    in_=pair_raw[f].rearrange("p i (c m j u) -> p (i c) m u j", m=32, j=4, u=2),
-                )
-                for i in range(count):
-                    perm[f + i] = both[:, i, :, :, :]
-
-        vsort, vturn = {}, {}
-
-        def v_perm(g):
-            vsort[g] = work.tile([P, 8, 2, 32], F32, name="vsort", bufs=2, align_bytes=64)
-            words = vraw[g].rearrange("p a c k -> p (a c) k").bitcast(F32)
-            nc.vector.tensor_copy(
-                out=vsort[g][:].rearrange("p b u (m j) -> p b m u j", j=4),
-                in_=words.rearrange("p b (m j u) -> p b m u j", j=4, u=2),
-            )
-
-        def v_turn(g):
-            vturn[g] = work.tile([P, 4, 2, 2, 32], F32, name="vturn", bufs=2, align_bytes=64)
-            nc.vector.transpose(
-                out=vturn[g][:].rearrange("p a c u r -> p (a c u r)"),
-                in_=vsort[g][:].rearrange("p b u j -> p (b u j)"),
-            )
-
-        def v_out(g):
-            words = wg[2 * g + 1][:, 1, :, :, :].rearrange("p c r t -> p (c r t)").bitcast(F32)
-            nc.vector.tensor_copy(
-                out=words.rearrange("p (c a r u) -> p c a r u", c=2, a=4, u=2),
-                in_=vturn[g][:].rearrange("p a c u r -> p c a r u"),
-            )
+        def w_deal(f, count=2, on_vector=True):
+            rows = work.tile([P, 4, count * 256], BF16, name="dealt")
+            deal(rows[:], raw[f][:].rearrange("p i k -> p (i k)"), on_vector)
+            for i in range(count):
+                dealt[f + i] = rows[:, :, 256 * i : 256 * (i + 1)]
 
         def w_turn(f, tag="step"):
-            if f in perm:
-                wbank[f] = turn(perm[f].rearrange("p c u m -> p c (u m)"), [True, True], tag)
-            else:
-                wbank[f] = turn(raw[f].rearrange("p (c w) -> p c w", c=2), [False, False], tag)
+            wbank[f] = turn(dealt[f], tag)
+
+        def laid(f):
+            if f // 2 not in wg:
+                wg[f // 2] = work.tile([P, 2, 2, P, 4], BF16, name="wg", align_bytes=64, bufs=4)
+            return wg[f // 2][:, f % 2, :, :, :].rearrange("p c r t -> p (c r t)").bitcast(F32)
 
         def w_out(f, on_vector=False):
-            if f % 2 == 0:
-                wg[f // 2] = work.tile([P, 2, 2, P, 4], BF16, name="wg", align_bytes=64, bufs=4)
-            words = wg[f // 2][:, f % 2, :, :, :].rearrange("p c r t -> p (c r t)").bitcast(F32)
-            words_out(words.rearrange("p (c r u) -> p c r u", c=2, u=2), wbank[f], on_vector)
+            words_out(laid(f).rearrange("p (c r u) -> p c r u", c=2, u=2), wbank[f], on_vector)
+
+        def v_deal(g):
+            vsort[g] = work.tile([P, 4, 256], BF16, name="vsort", align_bytes=64)
+            deal(vsort[g][:], vraw[g].rearrange("p a k -> p (a k)"))
+
+        def v_turn(g):
+            vturn[g] = work.tile([P, 512], F32, name="vturn", align_bytes=64)
+            nc.vector.transpose(out=vturn[g][:], in_=vsort[g][:].rearrange("p s k -> p (s k)").bitcast(F32))
+
+        def v_out(g):
+            nc.vector.tensor_copy(
+                out=laid(4 * g + 3).rearrange("p (c m u) -> p c m u", c=2, u=2),
+                in_=vturn[g][:].rearrange("p (c u m) -> p c m u", c=2, u=2),
+            )
 
         def w_quant(f, count):
             j = f // 2
@@ -202,51 +180,28 @@ def tile_sae_encode_decode_fp8_d4_kernel(tc, x_bytes, x_scale, w_enc, b_enc, dec
                 in_=wg[j][:, part, :, :, :].rearrange("p i c r t -> p (i c r t)"),
             )
 
-        zt, zi = {}, {}
+        pre, zt, zi, acc = {}, {}, {}, {}
 
-        def passes(dst, f, cols):
-            for c in range(2):
-                nc.tensor.matmul_mx(
-                    out=dst,
-                    lhsT=wc[f // 2][:, f % 2, c, :].bitcast(FP8X4),
-                    lhsT_scale=ws[f // 2][:, f % 2, c, :],
-                    rhs=xc[:, c, cols].bitcast(FP8X4),
-                    rhs_scale=xs[:, c, cols],
-                    start=(c == 0),
-                    stop=(c == 1),
-                )
-
-        def z_out(f, cols, src):
-            g, t = f // 4, f % 4
-            if g not in zt:
-                zt[g] = work.tile([P, 4, T], BF16, name="zt", bufs=GROUPS)
-            bias = b_cols[:, g, t : t + 1]
-            nc.scalar.activation(out=zt[g][:, t, cols], in_=src, func=ACT.Relu, bias=bias, scale=1.0)
-
-        pre = {}
-
-        def encode(f, tag="step"):
-            pre[f] = psum.tile([P, T], F32, name="pre", tag=tag)
-            passes(pre[f][:], f, slice(0, T))
-
-        def encode_pair(f, half, tag="step"):
-            cols = slice(HALF * half, HALF * (half + 1))
-            pre[f, half] = psum.tile([P, 2, HALF], F32, name="pre2", tag=tag)
-            for i in range(2):
-                passes(pre[f, half][:, i, :], f + i, cols)
-
-        def relu_pair(f, half):
-            for i in range(2):
-                z_out(f + i, slice(HALF * half, HALF * (half + 1)), pre[f, half][:, i, :])
-
-        def encode_in_halves(f):
+        def encode(f, parts=1):
             pre[f] = psum.tile([P, T], F32, name="pre", tag="step")
-            for half in range(2):
-                cols = slice(HALF * half, HALF * (half + 1))
-                passes(pre[f][:, cols], f, cols)
+            for part in range(parts):
+                cols = slice(T // parts * part, T // parts * (part + 1))
+                for c in range(2):
+                    nc.tensor.matmul_mx(
+                        out=pre[f][:, cols],
+                        lhsT=wc[f // 2][:, f % 2, c, :].bitcast(FP8X4),
+                        lhsT_scale=ws[f // 2][:, f % 2, c, :],
+                        rhs=xc[:, c, cols].bitcast(FP8X4),
+                        rhs_scale=xs[:, c, cols],
+                        start=(c == 0),
+                        stop=(c == 1),
+                    )
 
         def relu_out(f):
-            z_out(f, slice(0, T), pre[f][:])
+            g, t = divmod(f, 4)
+            if t == 0:
+                zt[g] = work.tile([P, 4, T], BF16, name="zt", bufs=GROUPS)
+            nc.scalar.activation(out=zt[g][:, t, :], in_=pre[f][:], func=ACT.Relu, bias=b_cols[:, g, t : t + 1], scale=1.0)
 
         def z_lace(half, g, on_vector=True):
             zi[half, g] = work.tile([P, HALF, 4], BF16, name="zi", tag="laced", align_bytes=64, bufs=6)
@@ -264,19 +219,19 @@ def tile_sae_encode_decode_fp8_d4_kernel(tc, x_bytes, x_scale, w_enc, b_enc, dec
                 in_=zi[half, g][:].rearrange("p n t -> p (n t)"),
             )
 
-        acc = {}
         orows = out.rearrange("(p n) k -> n p k", p=P)
 
         def decode_cols(bank, n, g, lo, width):
             part = min(g // 2, 2)
+            at = K * (g - SCALE_PARTS[part][0]) + lo
             nc.tensor.matmul_mx(
                 out=bank[:, 0:width],
                 lhsT=zc[:, g, P * n : P * (n + 1)].bitcast(FP8X4),
                 lhsT_scale=zs[:, g, P * n : P * (n + 1)],
                 rhs=dw[:, g, 2 * lo : 2 * (lo + width)].bitcast(FP4X4),
-                rhs_scale=dsc[part][:, K * (g - 2 * part) + lo : K * (g - 2 * part) + lo + width],
+                rhs_scale=dsc[part][:, at : at + width],
                 start=(g == 0),
-                stop=(g == GROUPS - 1),
+                stop=(g == last),
             )
 
         def store_cols(bank, n, lo, width):
@@ -295,21 +250,20 @@ def tile_sae_encode_decode_fp8_d4_kernel(tc, x_bytes, x_scale, w_enc, b_enc, dec
 
         nc.scalar.dma_start(out=xsc[:], in_=x_scale.rearrange("(p n) b -> p n b", p=P))
         nc.scalar.activation(out=early[:], in_=warm[:, 0:2], func=ACT.Copy)
-        nc.sync.dma_start(out=xin[0][:], in_=xr[0])
-        nc.sync.dma_start(out=xin[1][:], in_=xr[1])
+        for i in range(2):
+            nc.sync.dma_start(out=xin[i][:], in_=xr[i])
         nc.sync.dma_start(out=b_rows[0:GROUPS, :], in_=b_enc.rearrange("(g k) -> g k", g=GROUPS))
-        for f in range(0, 4 * VT_FROM, 2):
+        for f in range(0, 4 * BY_VECTOR, 2):
             load_w(f, 2)
-        load_w(12, 3)
-        load_dec(0)
-        load_dec_scales(0, 2)
-        load_v(3, 4)
-        for g in range(4, GROUPS):
+        for g in range(BY_VECTOR, GROUPS):
             load_w(4 * g, 3)
-            if g % 2 == 1:
-                load_dec_scales(g - 3, g - 1 if g < 7 else GROUPS)
+            if g in (5, 7):
+                load_dec_scales((g - 3) // 2)
             load_dec(g - 3)
-            if g % 2 == 0:
+            if g == 3:
+                load_dec_scales(0)
+                load_v(g, g + 1)
+            elif g % 2 == 0:
                 load_v(g, g + 2)
         for g in range(GROUPS - 3, GROUPS):
             load_dec(g)
@@ -317,86 +271,94 @@ def tile_sae_encode_decode_fp8_d4_kernel(tc, x_bytes, x_scale, w_enc, b_enc, dec
 
         for i in range(4):
             warm_up("step")
-        for n in range(4):
-            x_widen(n, 0, True)
-            x_widen(n, 1, n == 3)
         b_bank = psum.tile([P, 2, P], F32, name="b_bank", tag="step")
         for u in range(2):
             nc.tensor.transpose(b_bank[:, u, :], b_rows[:].bitcast(F32)[:, u : 2 * P : 2], ident[:])
-        x_turn(0, "acc")
-        x_turn(1, "acc")
+        x_widen(0, True)
+        x_widen(1, False)
+        x_widen(2, True)
+        deal(xw[1][:], flat[1][:])
+        x_widen(3, True)
         nc.scalar.copy(out=b_cols[:].bitcast(F32), in_=b_bank[:, :, 0:GROUPS].rearrange("p u g -> p g u"))
+        x_turn(0)
+        x_out(0)
+        x_turn(2)
+        x_out(2)
+        warm_up("step")
+        x_turn(1)
+        x_out(1)
+        x_turn(3)
+        x_out(3)
+        w_deal(0)
         w_turn(0)
-        x_turn(2, "acc")
-        x_turn(3, "acc")
         w_turn(1)
-        x_out(0, True)
-        warm_up("acc")
+        w_deal(2)
+        x_quant(0)
         w_turn(2)
         w_turn(3)
-        x_out(1, False)
-        w_out(0, True)
-        x_out(2, False)
-        x_quant(0)
-        x_out(3, False)
-        w_quant(0, 1)
-        w_out(1)
+        w_out(0)
         x_quant(1)
-        w_out(2)
+        w_out(1)
+        w_quant(0, 1)
         w_quant(1, 1)
-        w_perm(4)
+        w_deal(4)
+        w_out(2)
         w_out(3)
-        encode_in_halves(0)
-        encode(1)
-        w_perm(6)
+        w_deal(6)
         w_quant(2, 2)
+        encode(0)
+        encode(1)
         relu_out(0)
         relu_out(1)
 
-        last = GROUPS - 1
-        for g in range(1, VT_FROM):
+        for g in range(1, BY_VECTOR):
             first = 4 * g
             for f in range(first, first + 4):
                 w_turn(f, "acc")
-                w_out(f, f == first)
-            if g >= 2:
-                z_quant(0, g - 2)
+                if f < first + 3 or g == 1:
+                    w_out(f, f == first)
+            if g == 1:
+                w_deal(first + 4)
             else:
-                w_perm(first + 4)
+                z_quant(0, 0)
             w_quant(first, 1)
             w_quant(first + 1, 1)
+            if g == 2:
+                w_out(first + 3, True)
             for f in range(first - 2, first + 2):
                 encode(f)
                 relu_out(f)
-            if g >= 2:
+            if g == 2:
                 for b in range(2):
-                    decode(0, g - 2, b)
-                w_perm(first + 4, 3)
+                    decode(0, 0, b)
+                w_deal(first + 4, 3)
             w_quant(first + 2, 2)
-            if g + 1 < VT_FROM:
-                w_perm(first + 6)
+            if g == 1:
+                w_deal(first + 6)
             z_lace(0, g - 1)
-        for g in range(VT_FROM, GROUPS):
+
+        for g in range(BY_VECTOR, GROUPS):
             first = 4 * g
             for f in range(first, first + 3):
                 w_turn(f)
                 w_out(f)
-            v_perm(g)
+            v_deal(g)
             z_quant(0, g - 2)
             v_turn(g)
             w_quant(first, 2)
             v_out(g)
-            for b in range(2 if g == VT_FROM else 1, 4):
+            for b in range(2 if g == BY_VECTOR else 1, 4):
                 decode(0, g - 3, b)
             for f in range(first - 2, first + 2):
                 encode(f)
                 relu_out(f)
             decode(0, g - 2, 0)
-            w_perm(first + 4, 3)
-            if g == last:
+            if g < last:
+                w_deal(first + 4, 3)
+                w_quant(first + 2, 2)
+            else:
                 z_lace(1, 0)
-            w_quant(first + 2, 2)
-            if g == last:
+                w_quant(first + 2, 2)
                 z_quant(1, 0)
             z_lace(0, g - 1)
 

@@ -182,20 +182,19 @@ def tile_sae_encode_decode_fp8_d4_kernel(tc, x_bytes, x_scale, w_enc, b_enc, dec
 
         pre, zt, zi, acc = {}, {}, {}, {}
 
-        def encode(f, parts=1):
-            pre[f] = psum.tile([P, T], F32, name="pre", tag="step")
-            for part in range(parts):
-                cols = slice(T // parts * part, T // parts * (part + 1))
-                for c in range(2):
-                    nc.tensor.matmul_mx(
-                        out=pre[f][:, cols],
-                        lhsT=wc[f // 2][:, f % 2, c, :].bitcast(FP8X4),
-                        lhsT_scale=ws[f // 2][:, f % 2, c, :],
-                        rhs=xc[:, c, cols].bitcast(FP8X4),
-                        rhs_scale=xs[:, c, cols],
-                        start=(c == 0),
-                        stop=(c == 1),
-                    )
+        def encode(f, cols=slice(0, T)):
+            if f not in pre:
+                pre[f] = psum.tile([P, T], F32, name="pre", tag="step")
+            for c in range(2):
+                nc.tensor.matmul_mx(
+                    out=pre[f][:, cols],
+                    lhsT=wc[f // 2][:, f % 2, c, :].bitcast(FP8X4),
+                    lhsT_scale=ws[f // 2][:, f % 2, c, :],
+                    rhs=xc[:, c, cols].bitcast(FP8X4),
+                    rhs_scale=xs[:, c, cols],
+                    start=(c == 0),
+                    stop=(c == 1),
+                )
 
         def relu_out(f):
             g, t = divmod(f, 4)
@@ -278,6 +277,7 @@ def tile_sae_encode_decode_fp8_d4_kernel(tc, x_bytes, x_scale, w_enc, b_enc, dec
         x_widen(1, False)
         x_widen(2, True)
         deal(xw[1][:], flat[1][:])
+        w_deal(0)
         x_widen(3, True)
         nc.scalar.copy(out=b_cols[:].bitcast(F32), in_=b_bank[:, :, 0:GROUPS].rearrange("p u g -> p g u"))
         x_turn(0)
@@ -287,55 +287,64 @@ def tile_sae_encode_decode_fp8_d4_kernel(tc, x_bytes, x_scale, w_enc, b_enc, dec
         warm_up("step")
         x_turn(1)
         x_out(1)
-        x_turn(3)
-        x_out(3)
-        w_deal(0)
         w_turn(0)
         w_turn(1)
+        x_turn(3)
         w_deal(2)
-        x_quant(0)
         w_turn(2)
         w_turn(3)
+        x_quant(0)
         w_out(0)
-        x_quant(1)
         w_out(1)
+        x_out(3)
         w_quant(0, 1)
         w_quant(1, 1)
-        w_deal(4)
         w_out(2)
         w_out(3)
+        encode(0, slice(0, HALF))
+        encode(1, slice(0, HALF))
+        w_deal(4)
+        w_turn(4, "acc")
+        w_turn(5, "acc")
+        x_quant(1)
+        encode(0, slice(HALF, T))
+        encode(1, slice(HALF, T))
         w_deal(6)
         w_quant(2, 2)
-        encode(0)
-        encode(1)
+        w_out(4)
+        w_out(5)
         relu_out(0)
         relu_out(1)
 
-        for g in range(1, BY_VECTOR):
-            first = 4 * g
-            for f in range(first, first + 4):
-                w_turn(f, "acc")
-                if f < first + 3 or g == 1:
-                    w_out(f, f == first)
-            if g == 1:
-                w_deal(first + 4)
-            else:
-                z_quant(0, 0)
-            w_quant(first, 1)
-            w_quant(first + 1, 1)
-            if g == 2:
-                w_out(first + 3, True)
-            for f in range(first - 2, first + 2):
-                encode(f)
-                relu_out(f)
-            if g == 2:
-                for b in range(2):
-                    decode(0, 0, b)
-                w_deal(first + 4, 3)
-            w_quant(first + 2, 2)
-            if g == 1:
-                w_deal(first + 6)
-            z_lace(0, g - 1)
+        w_turn(6, "acc")
+        w_turn(7, "acc")
+        w_deal(8)
+        w_quant(4, 2)
+        w_out(6, True)
+        w_out(7)
+        w_deal(10)
+        for f in range(2, 6):
+            encode(f)
+            relu_out(f)
+        w_quant(6, 2)
+        z_lace(0, 0)
+        for f in range(8, 12):
+            w_turn(f, "acc")
+        w_out(8, True)
+        w_out(9)
+        w_out(10)
+        z_quant(0, 0)
+        w_quant(8, 1)
+        w_quant(9, 1)
+        w_out(11, True)
+        for f in range(6, 10):
+            encode(f)
+            relu_out(f)
+        for b in range(2):
+            decode(0, 0, b)
+        w_deal(12, 3)
+        w_quant(10, 2)
+        z_lace(0, 1)
 
         for g in range(BY_VECTOR, GROUPS):
             first = 4 * g

@@ -22,7 +22,7 @@ GROUPS = F // 512
 TILES = F // P
 HALF = T // 2
 RUN = 16
-BY_VECTOR = 3
+BY_TENSOR = 26
 SCALE_PARTS = ((0, 2), (2, 4), (4, 8))
 
 
@@ -32,7 +32,7 @@ def tile_sae_encode_decode_fp8_d4_kernel(tc, x_bytes, x_scale, w_enc, b_enc, dec
     with ExitStack() as ctx:
         keep = ctx.enter_context(tc.tile_pool(name="keep", bufs=1))
         work = ctx.enter_context(tc.tile_pool(name="work", bufs=2))
-        psum = ctx.enter_context(tc.psum_pool(name="psum", bufs=4))
+        psum = ctx.enter_context(tc.psum_pool(name="psum", bufs=1))
 
         ident = keep.tile([P, P], F32, name="ident")
         dsc = [keep.tile([P, (hi - lo) * K], U8, name="dsc%d" % lo, align_bytes=64) for lo, hi in SCALE_PARTS]
@@ -45,7 +45,7 @@ def tile_sae_encode_decode_fp8_d4_kernel(tc, x_bytes, x_scale, w_enc, b_enc, dec
         b_rows = keep.tile([P, 512], BF16, name="b_rows")
         b_cols = keep.tile([P, GROUPS, 4], BF16, name="b_cols")
         bd = keep.tile([P, K], BF16, name="bd")
-        xin = [keep.tile([P, 2, K], U8, name="xin%d" % i) for i in range(2)]
+        xin = [keep.tile([P, K], U8, name="xin%d" % i) for i in range(4)]
         warm = keep.tile([P, 512], BF16, name="warm")
         early = keep.tile([P, 2], BF16, name="early")
 
@@ -57,25 +57,24 @@ def tile_sae_encode_decode_fp8_d4_kernel(tc, x_bytes, x_scale, w_enc, b_enc, dec
         for plane in dsc:
             nc.vector.memset(plane[:].bitcast(I32), 0)
 
-        def warm_up(tag):
-            idle = psum.tile([P, 512], F32, name="idle", tag=tag)
+        def warm_up(bank):
+            idle = psum.tile([P, 512], F32, name="idle", tag="bank%d" % bank)
             nc.tensor.matmul(idle[:], lhsT=warm[:, 0:P], rhs=warm[:], start=True, stop=True)
 
-        xr = x_bytes.rearrange("(p i n) k -> i p n k", p=P, n=2)
+        xr = x_bytes.rearrange("(p n) k -> n p k", p=P)
         wr = w_enc.rearrange("(g m t) k -> g m t k", m=P, t=4)
-        wq = w_enc.rearrange("(a r t) k -> t r a k", r=32, t=4)[3]
+        wq = w_enc.rearrange("(a r t) k -> t r a k", r=32, t=4)
         raw, vraw = {}, {}
 
         def load_w(f, count):
-            raw[f] = work.tile([P, count, K], BF16, name="raw%d" % count, bufs=6 if count == 2 else 5)
+            raw[f] = work.tile([P, count, K], BF16, name="raw%d" % count, tag="raw%d" % count, bufs=12 if count == 2 else 2)
             nc.sync.dma_start(out=raw[f][:], in_=wr[f // 4][:, f % 4 : f % 4 + count, :])
 
-        def load_v(lo, hi):
-            tile = keep.tile([P, 4 * (hi - lo), 256], BF16, name="vraw%d" % lo)
+        def load_v(f):
+            g, t = divmod(f, 4)
+            vraw[f] = keep.tile([P, 4, 256], BF16, name="vraw%d" % f)
             for q in (0, 2, 1, 3):
-                nc.sync.dma_start(out=tile[32 * q : 32 * (q + 1), :, :], in_=wq[:, 4 * lo : 4 * hi, 256 * q : 256 * (q + 1)])
-            for g in range(lo, hi):
-                vraw[g] = tile[:, 4 * (g - lo) : 4 * (g - lo + 1), :]
+                nc.sync.dma_start(out=vraw[f][32 * q : 32 * (q + 1), :, :], in_=wq[t][:, 4 * g : 4 * g + 4, 256 * q : 256 * (q + 1)])
 
         def load_dec(g):
             nc.sync.dma_start(out=dw[:, g, :].bitcast(I32), in_=dec_words[g].bitcast(I32))
@@ -92,8 +91,8 @@ def tile_sae_encode_decode_fp8_d4_kernel(tc, x_bytes, x_scale, w_enc, b_enc, dec
             copy = nc.vector.tensor_copy if on_vector else nc.scalar.copy
             copy(out=dst.rearrange("p s (m j) -> p m s j", j=RUN), in_=src.rearrange("p (m s j) -> p m s j", s=4, j=RUN))
 
-        def turn(rows, tag):
-            bank = psum.tile([P, 4, P], F32, name="turned", tag=tag)
+        def turn(rows, at):
+            bank = psum.tile([P, 4, P], F32, name="turned", tag="bank%d" % at)
             for s in range(4):
                 nc.tensor.transpose(bank[:, s, :], rows[:, s, :].bitcast(F32), ident[:])
             return bank
@@ -109,7 +108,7 @@ def tile_sae_encode_decode_fp8_d4_kernel(tc, x_bytes, x_scale, w_enc, b_enc, dec
             if not on_vector:
                 flat[n] = work.tile([P, K], BF16, name="flat", tag="laced", align_bytes=64, bufs=6)
             for block in range(8):
-                src = xin[n // 2][:, n % 2, B * block : B * (block + 1)].bitcast(FP8)
+                src = xin[n][:, B * block : B * (block + 1)].bitcast(FP8)
                 s = xsc[:, n, block : block + 1]
                 if on_vector:
                     dst = xw[n][:, :, 32 * block : 32 * (block + 1)].rearrange("p s (m j) -> p m s j", j=RUN)
@@ -117,8 +116,8 @@ def tile_sae_encode_decode_fp8_d4_kernel(tc, x_bytes, x_scale, w_enc, b_enc, dec
                 else:
                     nc.scalar.activation(out=flat[n][:, B * block : B * (block + 1)], in_=src, func=ACT.Copy, scale=s)
 
-        def x_turn(n):
-            xbank[n] = turn(xw[n][:], "acc")
+        def x_turn(n, at):
+            xbank[n] = turn(xw[n][:], at)
 
         def x_out(n, on_vector=False):
             if n // 2 not in xg:
@@ -138,13 +137,13 @@ def tile_sae_encode_decode_fp8_d4_kernel(tc, x_bytes, x_scale, w_enc, b_enc, dec
         dealt, wbank, wg, wc, ws, vsort, vturn = {}, {}, {}, {}, {}, {}, {}
 
         def w_deal(f, count=2, on_vector=True):
-            rows = work.tile([P, 4, count * 256], BF16, name="dealt")
+            rows = work.tile([P, 4, count * 256], BF16, name="dealt%d" % count, bufs=4 if count == 2 else 2)
             deal(rows[:], raw[f][:].rearrange("p i k -> p (i k)"), on_vector)
             for i in range(count):
                 dealt[f + i] = rows[:, :, 256 * i : 256 * (i + 1)]
 
-        def w_turn(f, tag="step"):
-            wbank[f] = turn(dealt[f], tag)
+        def w_turn(f, at):
+            wbank[f] = turn(dealt[f], at)
 
         def laid(f):
             if f // 2 not in wg:
@@ -156,23 +155,24 @@ def tile_sae_encode_decode_fp8_d4_kernel(tc, x_bytes, x_scale, w_enc, b_enc, dec
 
         def v_deal(g):
             vsort[g] = work.tile([P, 4, 256], BF16, name="vsort", align_bytes=64)
-            deal(vsort[g][:], vraw[g].rearrange("p a k -> p (a k)"))
+            deal(vsort[g][:], vraw[g][:].rearrange("p a k -> p (a k)"))
 
         def v_turn(g):
             vturn[g] = work.tile([P, 512], F32, name="vturn", align_bytes=64)
             nc.vector.transpose(out=vturn[g][:], in_=vsort[g][:].rearrange("p s k -> p (s k)").bitcast(F32))
 
-        def v_out(g):
-            nc.vector.tensor_copy(
-                out=laid(4 * g + 3).rearrange("p (c m u) -> p c m u", c=2, u=2),
+        def v_out(g, on_vector=True):
+            copy = nc.vector.tensor_copy if on_vector else nc.scalar.copy
+            copy(
+                out=laid(g).rearrange("p (c m u) -> p c m u", c=2, u=2),
                 in_=vturn[g][:].rearrange("p (c u m) -> p c m u", c=2, u=2),
             )
 
         def w_quant(f, count):
             j = f // 2
             if f % 2 == 0:
-                wc[j] = work.tile([P, 2, 2, P], U32, name="wc", align_bytes=64, bufs=4)
-                ws[j] = work.tile([P, 2, 2, P], U8, name="ws", align_bytes=64, bufs=4)
+                wc[j] = work.tile([P, 2, 2, P], U32, name="wc", align_bytes=64, bufs=6)
+                ws[j] = work.tile([P, 2, 2, P], U8, name="ws", align_bytes=64, bufs=6)
             part = slice(f % 2, f % 2 + count)
             nc.vector.quantize_mx(
                 out=wc[j][:, part, :, :].rearrange("p i c r -> p (i c r)").bitcast(FP8X4),
@@ -182,9 +182,9 @@ def tile_sae_encode_decode_fp8_d4_kernel(tc, x_bytes, x_scale, w_enc, b_enc, dec
 
         pre, zt, zi, acc = {}, {}, {}, {}
 
-        def encode(f, cols=slice(0, T)):
+        def encode(f, at, cols=slice(0, T)):
             if f not in pre:
-                pre[f] = psum.tile([P, T], F32, name="pre", tag="step")
+                pre[f] = psum.tile([P, T], F32, name="pre", tag="bank%d" % at)
             for c in range(2):
                 nc.tensor.matmul_mx(
                     out=pre[f][:, cols],
@@ -202,20 +202,20 @@ def tile_sae_encode_decode_fp8_d4_kernel(tc, x_bytes, x_scale, w_enc, b_enc, dec
                 zt[g] = work.tile([P, 4, T], BF16, name="zt", bufs=GROUPS)
             nc.scalar.activation(out=zt[g][:, t, :], in_=pre[f][:], func=ACT.Relu, bias=b_cols[:, g, t : t + 1], scale=1.0)
 
-        def z_lace(half, g, on_vector=True):
-            zi[half, g] = work.tile([P, HALF, 4], BF16, name="zi", tag="laced", align_bytes=64, bufs=6)
+        def z_lace(g, n, count=1, on_vector=True):
+            zi[g, n] = work.tile([P, count * P, 4], BF16, name="zi", tag="laced", align_bytes=64, bufs=6)
             copy = nc.vector.tensor_copy if on_vector else nc.scalar.copy
             copy(
-                out=zi[half, g][:].rearrange("p (c i) t -> p c t i", i=4),
-                in_=zt[g][:, :, HALF * half : HALF * (half + 1)].rearrange("p t (c i) -> p c t i", i=4),
+                out=zi[g, n][:].rearrange("p (c i) t -> p c t i", i=4),
+                in_=zt[g][:, :, P * n : P * (n + count)].rearrange("p t (c i) -> p c t i", i=4),
             )
 
-        def z_quant(half, g):
-            cols = slice(HALF * half, HALF * (half + 1))
+        def z_quant(g, n, count=1):
+            cols = slice(P * n, P * (n + count))
             nc.vector.quantize_mx(
                 out=zc[:, g, cols].bitcast(FP8X4),
                 scales=zs[:, g, cols],
-                in_=zi[half, g][:].rearrange("p n t -> p (n t)"),
+                in_=zi[g, n][:].rearrange("p n t -> p (n t)"),
             )
 
         orows = out.rearrange("(p n) k -> n p k", p=P)
@@ -234,180 +234,273 @@ def tile_sae_encode_decode_fp8_d4_kernel(tc, x_bytes, x_scale, w_enc, b_enc, dec
             )
 
         def store_cols(bank, n, lo, width):
-            o = work.tile([P, width], F32, name="o%d" % width, bufs=7 if width == 512 else 2)
+            o = work.tile([P, width], F32, name="o", tag="raw2", bufs=12)
             cols = slice(lo, lo + width)
             nc.vector.tensor_tensor(out=o[:], in0=bank[:, 0:width], in1=bd[:, cols], op=ALU.add)
             nc.sync.dma_start(out=orows[n][:, cols], in_=o[:])
 
-        def decode(half, g, b):
+        def decode(n, g, h, at=None):
             if g == 0:
-                acc[half, b] = psum.tile([P, 512], F32, name="acc", tag="step" if half else "acc")
-            decode_cols(acc[half, b], 2 * half + b // 2, g, 512 * (b % 2), 512)
+                acc[n, h] = psum.tile([P, 512], F32, name="acc", tag="bank%d" % at)
+            decode_cols(acc[n, h], n, g, 512 * h, 512)
 
-        def store(half, b):
-            store_cols(acc[half, b], 2 * half + b // 2, 512 * (b % 2), 512)
+        def store(n, h):
+            store_cols(acc[n, h], n, 512 * h, 512)
 
         nc.scalar.dma_start(out=xsc[:], in_=x_scale.rearrange("(p n) b -> p n b", p=P))
         nc.scalar.activation(out=early[:], in_=warm[:, 0:2], func=ACT.Copy)
-        for i in range(2):
-            nc.sync.dma_start(out=xin[i][:], in_=xr[i])
+        for n in (0, 2, 1):
+            nc.sync.dma_start(out=xin[n][:], in_=xr[n])
+        load_w(0, 1)
+        nc.sync.dma_start(out=xin[3][:], in_=xr[3])
+        load_w(1, 1)
+        load_w(2, 2)
         nc.sync.dma_start(out=b_rows[0:GROUPS, :], in_=b_enc.rearrange("(g k) -> g k", g=GROUPS))
-        for f in range(0, 4 * BY_VECTOR, 2):
+        for f in range(4, 14, 2):
             load_w(f, 2)
-        for g in range(BY_VECTOR, GROUPS):
-            load_w(4 * g, 3)
-            if g in (5, 7):
-                load_dec_scales((g - 3) // 2)
-            load_dec(g - 3)
-            if g == 3:
-                load_dec_scales(0)
-                load_v(g, g + 1)
-            elif g % 2 == 0:
-                load_v(g, g + 2)
-        for g in range(GROUPS - 3, GROUPS):
+        load_dec(0)
+        load_dec_scales(0)
+        for f in range(14, 20, 2):
+            load_w(f, 2)
+        load_dec(1)
+        for f in range(20, BY_TENSOR, 2):
+            load_w(f, 2)
+        load_v(26)
+        load_dec(2)
+        load_dec_scales(1)
+        load_v(27)
+        load_dec(3)
+        load_v(28)
+        load_v(29)
+        load_dec(4)
+        load_dec_scales(2)
+        load_v(30)
+        load_v(31)
+        for g in range(5, GROUPS):
             load_dec(g)
         nc.sync.dma_start(out=bd[:], in_=b_dec.partition_broadcast(P))
 
         for i in range(4):
-            warm_up("step")
-        b_bank = psum.tile([P, 2, P], F32, name="b_bank", tag="step")
+            warm_up(4 + i)
+        x_widen(0, True)
+        x_widen(2, False)
+        x_widen(1, True)
+        w_deal(0, 1)
+        x_turn(0, 0)
+        warm_up(7)
+        x_turn(1, 1)
+        w_turn(0, 2)
+        deal(xw[2][:], flat[2][:])
+        w_deal(1, 1)
+        x_out(0)
+        x_out(1)
+        w_out(0)
+        x_turn(2, 3)
+        w_turn(1, 4)
+        x_widen(3, True)
+        w_deal(2)
+        x_quant(0)
+        w_quant(0, 1)
+        x_turn(3, 5)
+        b_bank = psum.tile([P, 2, P], F32, name="b_bank", tag="bank6")
         for u in range(2):
             nc.tensor.transpose(b_bank[:, u, :], b_rows[:].bitcast(F32)[:, u : 2 * P : 2], ident[:])
-        x_widen(0, True)
-        x_widen(1, False)
-        x_widen(2, True)
-        deal(xw[1][:], flat[1][:])
-        w_deal(0)
-        x_widen(3, True)
-        nc.scalar.copy(out=b_cols[:].bitcast(F32), in_=b_bank[:, :, 0:GROUPS].rearrange("p u g -> p g u"))
-        x_turn(0)
-        x_out(0)
-        x_turn(2)
-        x_out(2)
-        warm_up("step")
-        x_turn(1)
-        x_out(1)
-        w_turn(0)
-        w_turn(1)
-        x_turn(3)
-        w_deal(2)
-        w_turn(2)
-        w_turn(3)
-        x_quant(0)
-        w_out(0)
+        w_turn(2, 7)
+        w_turn(3, 0)
         w_out(1)
+        x_out(2)
         x_out(3)
-        w_quant(0, 1)
+        encode(0, 1, slice(0, HALF))
+        w_deal(4)
         w_quant(1, 1)
+        x_quant(1)
+        encode(1, 2, slice(0, HALF))
+        nc.scalar.copy(out=b_cols[:].bitcast(F32), in_=b_bank[:, :, 0:GROUPS].rearrange("p u g -> p g u"))
         w_out(2)
         w_out(3)
-        encode(0, slice(0, HALF))
-        encode(1, slice(0, HALF))
-        w_deal(4)
-        w_turn(4, "acc")
-        w_turn(5, "acc")
-        x_quant(1)
-        encode(0, slice(HALF, T))
-        encode(1, slice(HALF, T))
+        w_turn(4, 3)
+        w_turn(5, 4)
+        encode(0, 1, slice(HALF, T))
+        encode(1, 2, slice(HALF, T))
         w_deal(6)
         w_quant(2, 2)
         w_out(4)
         w_out(5)
         relu_out(0)
         relu_out(1)
-
-        w_turn(6, "acc")
-        w_turn(7, "acc")
+        encode(2, 5)
+        encode(3, 6)
         w_deal(8)
         w_quant(4, 2)
-        w_out(6, True)
-        w_out(7)
         w_deal(10)
-        for f in range(2, 6):
-            encode(f)
-            relu_out(f)
-        w_quant(6, 2)
-        z_lace(0, 0)
-        for f in range(8, 12):
-            w_turn(f, "acc")
-        w_out(8, True)
-        w_out(9)
-        w_out(10)
-        z_quant(0, 0)
-        w_quant(8, 1)
-        w_quant(9, 1)
-        w_out(11, True)
-        for f in range(6, 10):
-            encode(f)
-            relu_out(f)
-        for b in range(2):
-            decode(0, 0, b)
-        w_deal(12, 3)
+        relu_out(2)
+        relu_out(3)
+
+        for i, f in enumerate(range(6, 14)):
+            if f == 12:
+                w_deal(12)
+            w_turn(f, (7 + i) % 8)
+        for f in range(6, 14):
+            w_out(f, f in (6, 8, 10))
+            if f in (9, 11):
+                w_quant(f - 3, 2)
         w_quant(10, 2)
-        z_lace(0, 1)
-
-        for g in range(BY_VECTOR, GROUPS):
-            first = 4 * g
-            for f in range(first, first + 3):
-                w_turn(f)
-                w_out(f)
-            v_deal(g)
-            z_quant(0, g - 2)
-            v_turn(g)
-            w_quant(first, 2)
-            v_out(g)
-            for b in range(2 if g == BY_VECTOR else 1, 4):
-                decode(0, g - 3, b)
-            for f in range(first - 2, first + 2):
-                encode(f)
-                relu_out(f)
-            decode(0, g - 2, 0)
-            if g < last:
-                w_deal(first + 4, 3)
-                w_quant(first + 2, 2)
-            else:
-                z_lace(1, 0)
-                w_quant(first + 2, 2)
-                z_quant(1, 0)
-            z_lace(0, g - 1)
-
-        z_lace(1, 1)
-        z_quant(0, last - 1)
-        for b in range(1, 4):
-            decode(0, last - 2, b)
-        for f in range(TILES - 2, TILES):
-            encode(f)
+        z_lace(0, 0)
+        w_deal(14)
+        w_quant(12, 2)
+        z_quant(0, 0)
+        w_deal(16)
+        w_deal(18)
+        for i, f in enumerate(range(4, 11)):
+            encode(f, (7, 0, 1, 2, 3, 4, 5)[i])
             relu_out(f)
-        z_lace(1, 2)
-        z_quant(1, 1)
+        decode(0, 0, 0, 6)
+        for i, f in enumerate(range(14, 20)):
+            w_turn(f, i)
+        z_lace(1, 0)
+        for f in range(14, 20):
+            w_out(f, f in (14, 16))
+        z_quant(1, 0)
+        w_quant(14, 2)
+        w_deal(20)
+        w_quant(16, 2)
+        w_deal(22)
+        w_quant(18, 2)
+        w_deal(24)
+        decode(0, 0, 1, 7)
+        for i, f in enumerate(range(11, 17)):
+            encode(f, i)
+            relu_out(f)
+        z_lace(2, 0)
+        v_deal(26)
+        z_quant(2, 0)
+        v_turn(26)
+        decode(0, 1, 0)
+        decode(0, 1, 1)
+        for i, f in enumerate(range(20, 26)):
+            w_turn(f, i)
+        for f in range(20, 26):
+            w_out(f, f in (20, 22))
+        w_quant(20, 2)
+        v_out(26)
+        z_lace(3, 0)
+        w_quant(22, 2)
+        z_quant(3, 0)
+        v_deal(27)
+        w_quant(24, 2)
+        v_turn(27)
+        z_lace(0, 1, 2)
+        v_out(27)
+        z_quant(0, 1, 2)
+        decode(0, 2, 0)
+        decode(0, 2, 1)
+        for i, f in enumerate(range(17, 23)):
+            encode(f, i)
+            relu_out(f)
+        decode(0, 3, 0)
+        decode(0, 3, 1)
+
+        def both(n, g, at=None):
+            for h in range(2):
+                decode(n, g, h, None if at is None else at + h)
+
+        def feature(f):
+            encode(f, 4 + (f + 1) % 2)
+            relu_out(f)
+
+        v_deal(28)
+        w_quant(26, 2)
+        z_lace(1, 1, 2)
+        v_turn(28)
+        z_quant(1, 1, 2)
+        feature(23)
+        z_lace(2, 1, 1, False)
+        both(1, 0, 0)
+        feature(24)
+        z_lace(2, 2, 1, False)
+        both(2, 0, 2)
+        z_lace(4, 0)
+        v_deal(29)
+        z_quant(4, 0)
+        v_turn(29)
+        v_out(28)
+        z_quant(2, 1)
+        v_out(29)
+        z_quant(2, 2)
+        w_quant(28, 2)
+        feature(25)
+        z_lace(3, 1, 1, False)
+        both(1, 1)
+        feature(26)
+        z_lace(3, 2, 1, False)
+        both(2, 1)
+        feature(27)
+        z_lace(4, 1, 2, False)
+        both(0, 4)
+        both(1, 2)
+        v_deal(30)
+        z_quant(3, 1)
+        v_turn(30)
+        z_quant(3, 2)
+        v_deal(31)
+        v_out(30)
+        v_turn(31)
+        w_quant(30, 1)
+        v_out(31)
+        z_quant(4, 1, 2)
+        w_quant(31, 1)
+        feature(28)
+        z_lace(5, 0, 1, False)
+        both(2, 2)
+        feature(29)
+        z_lace(5, 1, 2, False)
+        both(1, 3)
+        both(2, 3)
+        feature(30)
+        both(1, 4)
+        feature(31)
+        both(2, 4)
+        z_lace(6, 0, 2)
+        z_quant(5, 0)
+        z_lace(0, 3)
+        z_quant(6, 0, 2)
         z_lace(1, 3)
-        z_quant(1, 2)
-        z_lace(0, last)
+        z_quant(5, 1, 2)
+        z_quant(0, 3)
         z_quant(1, 3)
-        z_quant(0, last)
-        for g in range(4, GROUPS):
-            z_lace(1, g, False)
-        z_quant(1, 4)
-        for b in range(4):
-            decode(0, last - 1, b)
-        for g in range(3):
-            for b in range(3):
-                decode(1, g, b)
-        for b in range(4):
-            decode(0, last, b)
-        for g in range(5, GROUPS):
-            z_quant(1, g)
-            store(0, g - 5)
-        store(0, 3)
-        for g in range(3, 5):
-            for b in range(3):
-                decode(1, g, b)
-        for b in range(3):
-            for g in range(5, GROUPS):
-                decode(1, g, b)
-            store(1, b)
-        for lo, width in ((512, 256), (768, P), (896, P)):
-            piece = psum.tile([P, 512], F32, name="piece", tag="acc")
+        z_lace(7, 0, 2)
+        z_lace(6, 2, 2, False)
+        z_lace(7, 2, 2, False)
+        z_lace(2, 3)
+        z_quant(7, 0, 2)
+        z_lace(3, 3)
+        z_quant(6, 2, 2)
+        z_quant(2, 3)
+        z_quant(3, 3)
+        for n in range(3):
+            both(n, 5)
+        both(0, 6)
+        both(1, 6)
+        both(0, 7)
+        both(2, 6)
+        both(1, 7)
+        store(0, 0)
+        z_quant(7, 2, 2)
+        both(2, 7)
+        for g in range(4, 6):
+            z_lace(g, 3, 1, False)
+        store(0, 1)
+        z_quant(4, 3)
+        store(1, 0)
+        z_quant(5, 3)
+        store(1, 1)
+        store(2, 0)
+        store(2, 1)
+        for g in range(GROUPS):
+            decode(3, g, 0, 4)
+        store(3, 0)
+        for lo, width, at in ((512, 256, 5), (768, P, 6), (896, P, 7)):
+            piece = psum.tile([P, 512], F32, name="piece", tag="bank%d" % at)
             for g in range(GROUPS):
                 decode_cols(piece, 3, g, lo, width)
             store_cols(piece, 3, lo, width)

@@ -22,7 +22,7 @@ GROUPS = F // 512
 TILES = F // P
 HALF = T // 2
 RUN = 16
-BY_TENSOR = 26
+BY_TENSOR = 28
 SCALE_PARTS = ((0, 2), (2, 4), (4, 8))
 
 
@@ -67,7 +67,7 @@ def tile_sae_encode_decode_fp8_d4_kernel(tc, x_bytes, x_scale, w_enc, b_enc, dec
         raw, vraw = {}, {}
 
         def load_w(f, count):
-            raw[f] = work.tile([P, count, K], BF16, name="raw%d" % count, tag="raw%d" % count, bufs=12 if count == 2 else 2)
+            raw[f] = work.tile([P, count, K], BF16, name="raw%d" % count, tag="raw%d" % count, bufs=13 if count == 2 else 2)
             nc.sync.dma_start(out=raw[f][:], in_=wr[f // 4][:, f % 4 : f % 4 + count, :])
 
         def load_v(f):
@@ -234,7 +234,7 @@ def tile_sae_encode_decode_fp8_d4_kernel(tc, x_bytes, x_scale, w_enc, b_enc, dec
             )
 
         def store_cols(bank, n, lo, width):
-            o = work.tile([P, width], F32, name="o", tag="raw2", bufs=12)
+            o = work.tile([P, width], F32, name="o", tag="raw2", bufs=13)
             cols = slice(lo, lo + width)
             nc.vector.tensor_tensor(out=o[:], in0=bank[:, 0:width], in1=bd[:, cols], op=ALU.add)
             nc.sync.dma_start(out=orows[n][:, cols], in_=o[:])
@@ -256,21 +256,19 @@ def tile_sae_encode_decode_fp8_d4_kernel(tc, x_bytes, x_scale, w_enc, b_enc, dec
         load_w(1, 1)
         load_w(2, 2)
         nc.sync.dma_start(out=b_rows[0:GROUPS, :], in_=b_enc.rearrange("(g k) -> g k", g=GROUPS))
-        for f in range(4, 14, 2):
+        for f in range(4, 16, 2):
             load_w(f, 2)
         load_dec(0)
         load_dec_scales(0)
-        for f in range(14, 20, 2):
+        for f in range(16, 22, 2):
             load_w(f, 2)
         load_dec(1)
-        for f in range(20, BY_TENSOR, 2):
+        for f in range(22, BY_TENSOR, 2):
             load_w(f, 2)
-        load_v(26)
         load_dec(2)
         load_dec_scales(1)
-        load_v(27)
-        load_dec(3)
         load_v(28)
+        load_dec(3)
         load_v(29)
         load_dec(4)
         load_dec_scales(2)
@@ -313,183 +311,182 @@ def tile_sae_encode_decode_fp8_d4_kernel(tc, x_bytes, x_scale, w_enc, b_enc, dec
         encode(0, 1, slice(0, HALF))
         w_deal(4)
         w_quant(1, 1)
+        w_deal(6)
         x_quant(1)
         encode(1, 2, slice(0, HALF))
         nc.scalar.copy(out=b_cols[:].bitcast(F32), in_=b_bank[:, :, 0:GROUPS].rearrange("p u g -> p g u"))
         w_out(2)
         w_out(3)
-        w_turn(4, 3)
-        w_turn(5, 4)
+        for f in range(4, 8):
+            w_turn(f, f - 1)
         encode(0, 1, slice(HALF, T))
         encode(1, 2, slice(HALF, T))
-        w_deal(6)
         w_quant(2, 2)
+        w_out(5, True)
         w_out(4)
-        w_out(5)
+        w_deal(8)
+        w_out(6)
+        w_out(7)
+        w_quant(4, 2)
         relu_out(0)
         relu_out(1)
-        encode(2, 5)
-        encode(3, 6)
-        w_deal(8)
-        w_quant(4, 2)
+        encode(2, 7)
+        encode(3, 0)
+        encode(4, 3)
         w_deal(10)
+        w_quant(6, 2)
+        w_deal(12)
         relu_out(2)
         relu_out(3)
+        relu_out(4)
 
-        for i, f in enumerate(range(6, 14)):
-            if f == 12:
-                w_deal(12)
-            w_turn(f, (7 + i) % 8)
-        for f in range(6, 14):
-            w_out(f, f in (6, 8, 10))
-            if f in (9, 11):
-                w_quant(f - 3, 2)
-        w_quant(10, 2)
+        for f, at in zip(range(8, 16), (4, 5, 6, 1, 2, 7, 0, 3)):
+            if f == 14:
+                w_out(8, True)
+                w_deal(14)
+            w_turn(f, at)
+        for f in range(9, 16):
+            w_out(f, f in (10, 12))
+            if f in (10, 12):
+                w_quant(f - 2, 2)
         z_lace(0, 0)
-        w_deal(14)
+        w_deal(16)
         w_quant(12, 2)
         z_quant(0, 0)
-        w_deal(16)
         w_deal(18)
-        for i, f in enumerate(range(4, 11)):
-            encode(f, (7, 0, 1, 2, 3, 4, 5)[i])
-            relu_out(f)
-        decode(0, 0, 0, 6)
-        for i, f in enumerate(range(14, 20)):
-            w_turn(f, i)
-        z_lace(1, 0)
-        for f in range(14, 20):
-            w_out(f, f in (14, 16))
-        z_quant(1, 0)
         w_quant(14, 2)
         w_deal(20)
+        for f, at in zip(range(5, 12), (4, 5, 6, 1, 2, 7, 0)):
+            encode(f, at)
+            relu_out(f)
+        decode(0, 0, 0, 3)
+        for f, at in zip(range(16, 22), (4, 5, 6, 1, 2, 0)):
+            w_turn(f, at)
+        z_lace(1, 0)
+        for f in range(16, 22):
+            w_out(f, f in (16, 18))
+        z_quant(1, 0)
         w_quant(16, 2)
         w_deal(22)
         w_quant(18, 2)
         w_deal(24)
+        w_quant(20, 2)
+        w_deal(26)
         decode(0, 0, 1, 7)
-        for i, f in enumerate(range(11, 17)):
-            encode(f, i)
+        for f, at in zip(range(12, 18), (4, 5, 6, 1, 2, 0)):
+            encode(f, at)
             relu_out(f)
         z_lace(2, 0)
-        v_deal(26)
+        z_lace(3, 0)
         z_quant(2, 0)
-        v_turn(26)
         decode(0, 1, 0)
         decode(0, 1, 1)
-        for i, f in enumerate(range(20, 26)):
-            w_turn(f, i)
-        for f in range(20, 26):
-            w_out(f, f in (20, 22))
-        w_quant(20, 2)
-        v_out(26)
-        z_lace(3, 0)
+        for f, at in zip(range(22, 28), (4, 5, 6, 1, 2, 0)):
+            w_turn(f, at)
+        for f in range(22, 28):
+            w_out(f, f == 22)
+            if f == 22:
+                z_quant(3, 0)
+                z_lace(0, 1, 2)
         w_quant(22, 2)
-        z_quant(3, 0)
-        v_deal(27)
-        w_quant(24, 2)
-        v_turn(27)
-        z_lace(0, 1, 2)
-        v_out(27)
+        v_deal(28)
         z_quant(0, 1, 2)
+        w_quant(24, 2)
+        v_turn(28)
+        z_lace(1, 1, 2)
+        w_quant(26, 2)
+        z_quant(1, 1, 2)
         decode(0, 2, 0)
         decode(0, 2, 1)
-        for i, f in enumerate(range(17, 23)):
-            encode(f, i)
+        for f, at in zip(range(18, 24), (4, 5, 6, 1, 2, 0)):
+            encode(f, at)
             relu_out(f)
         decode(0, 3, 0)
         decode(0, 3, 1)
 
         def both(n, g, at=None):
             for h in range(2):
-                decode(n, g, h, None if at is None else at + h)
+                decode(n, g, h, None if at is None else at[h])
 
         def feature(f):
-            encode(f, 4 + (f + 1) % 2)
+            encode(f, 2 * (f % 2 == 0))
             relu_out(f)
 
-        v_deal(28)
-        w_quant(26, 2)
-        z_lace(1, 1, 2)
-        v_turn(28)
-        z_quant(1, 1, 2)
-        feature(23)
-        z_lace(2, 1, 1, False)
-        both(1, 0, 0)
-        feature(24)
-        z_lace(2, 2, 1, False)
-        both(2, 0, 2)
-        z_lace(4, 0)
         v_deal(29)
-        z_quant(4, 0)
-        v_turn(29)
         v_out(28)
-        z_quant(2, 1)
-        v_out(29)
-        z_quant(2, 2)
-        w_quant(28, 2)
+        v_turn(29)
+        z_lace(4, 0)
+        both(1, 0, (4, 5))
+        feature(24)
+        z_lace(2, 1, 1, False)
+        both(2, 0, (6, 1))
         feature(25)
-        z_lace(3, 1, 1, False)
+        z_lace(2, 2, 1, False)
+        v_deal(30)
+        v_out(29)
+        z_quant(4, 0)
+        v_turn(30)
+        z_quant(2, 1)
+        w_quant(28, 2)
+        z_quant(2, 2)
         both(1, 1)
         feature(26)
-        z_lace(3, 2, 1, False)
+        z_lace(3, 1, 1, False)
         both(2, 1)
         feature(27)
-        z_lace(4, 1, 2, False)
-        both(0, 4)
-        both(1, 2)
-        v_deal(30)
-        z_quant(3, 1)
-        v_turn(30)
-        z_quant(3, 2)
+        z_lace(3, 2, 1, False)
         v_deal(31)
         v_out(30)
         v_turn(31)
-        w_quant(30, 1)
+        z_quant(3, 1)
+        z_lace(5, 0)
         v_out(31)
-        z_quant(4, 1, 2)
-        w_quant(31, 1)
+        z_quant(3, 2)
+        z_quant(5, 0)
+        w_quant(30, 2)
+        both(0, 4)
+        both(1, 2)
         feature(28)
-        z_lace(5, 0, 1, False)
+        z_lace(4, 1, 1, False)
         both(2, 2)
         feature(29)
-        z_lace(5, 1, 2, False)
+        z_lace(4, 2, 1, False)
         both(1, 3)
         both(2, 3)
         feature(30)
-        both(1, 4)
+        both(0, 5)
         feature(31)
-        both(2, 4)
-        z_lace(6, 0, 2)
-        z_quant(5, 0)
-        z_lace(0, 3)
-        z_quant(6, 0, 2)
-        z_lace(1, 3)
+        z_lace(5, 1, 2)
+        z_quant(4, 1)
+        z_quant(4, 2)
         z_quant(5, 1, 2)
-        z_quant(0, 3)
-        z_quant(1, 3)
-        z_lace(7, 0, 2)
+        z_lace(6, 0, 2)
         z_lace(6, 2, 2, False)
         z_lace(7, 2, 2, False)
-        z_lace(2, 3)
-        z_quant(7, 0, 2)
-        z_lace(3, 3)
+        z_lace(0, 3)
+        z_quant(6, 0, 2)
+        z_lace(7, 0, 2)
+        z_quant(0, 3)
         z_quant(6, 2, 2)
-        z_quant(2, 3)
-        z_quant(3, 3)
-        for n in range(3):
-            both(n, 5)
+        z_quant(7, 0, 2)
+        z_lace(1, 3)
+        for g in (4, 5):
+            both(1, g)
+            both(2, g)
         both(0, 6)
         both(1, 6)
         both(0, 7)
         both(2, 6)
         both(1, 7)
-        store(0, 0)
         z_quant(7, 2, 2)
+        z_quant(1, 3)
         both(2, 7)
-        for g in range(4, 6):
+        for g in range(2, 6):
             z_lace(g, 3, 1, False)
+        store(0, 0)
+        z_quant(2, 3)
         store(0, 1)
+        z_quant(3, 3)
         z_quant(4, 3)
         store(1, 0)
         z_quant(5, 3)
@@ -497,9 +494,9 @@ def tile_sae_encode_decode_fp8_d4_kernel(tc, x_bytes, x_scale, w_enc, b_enc, dec
         store(2, 0)
         store(2, 1)
         for g in range(GROUPS):
-            decode(3, g, 0, 4)
+            decode(3, g, 0, 2)
         store(3, 0)
-        for lo, width, at in ((512, 256, 5), (768, P, 6), (896, P, 7)):
+        for lo, width, at in ((512, 256, 0), (768, P, 3), (896, P, 7)):
             piece = psum.tile([P, 512], F32, name="piece", tag="bank%d" % at)
             for g in range(GROUPS):
                 decode_cols(piece, 3, g, lo, width)

@@ -45,7 +45,7 @@ def tile_sae_encode_decode_fp8_d4_kernel(tc, x_bytes, x_scale, w_enc, b_enc, dec
         b_rows = keep.tile([P, 512], BF16, name="b_rows")
         b_cols = keep.tile([P, GROUPS, 4], BF16, name="b_cols")
         bd = keep.tile([P, K], BF16, name="bd")
-        xin = [keep.tile([P, K], U8, name="xin%d" % i) for i in range(4)]
+        xin = [keep.tile([P, 2, K], U8, name="xin%d" % i) for i in range(2)]
         warm = keep.tile([P, 512], BF16, name="warm")
         early = keep.tile([P, 2], BF16, name="early")
 
@@ -61,20 +61,21 @@ def tile_sae_encode_decode_fp8_d4_kernel(tc, x_bytes, x_scale, w_enc, b_enc, dec
             idle = psum.tile([P, 512], F32, name="idle", tag="bank%d" % bank)
             nc.tensor.matmul(idle[:], lhsT=warm[:, 0:P], rhs=warm[:], start=True, stop=True)
 
-        xr = x_bytes.rearrange("(p n) k -> n p k", p=P)
+        xr = x_bytes.rearrange("(p i n) k -> i p n k", p=P, n=2)
         wr = w_enc.rearrange("(g m t) k -> g m t k", m=P, t=4)
         wq = w_enc.rearrange("(a r t) k -> t r a k", r=32, t=4)
         raw, vraw = {}, {}
 
         def load_w(f, count):
-            raw[f] = work.tile([P, count, K], BF16, name="raw%d" % count, tag="raw%d" % count, bufs=13 if count == 2 else 2)
+            raw[f] = work.tile([P, count, K], BF16, name="raw%d" % count, bufs=14)
             nc.sync.dma_start(out=raw[f][:], in_=wr[f // 4][:, f % 4 : f % 4 + count, :])
 
-        def load_v(f):
-            g, t = divmod(f, 4)
-            vraw[f] = keep.tile([P, 4, 256], BF16, name="vraw%d" % f)
+        def load_v(t, lo, hi):
+            tile = keep.tile([P, 4 * (hi - lo), 256], BF16, name="vraw%d" % (4 * lo + t))
             for q in (0, 2, 1, 3):
-                nc.sync.dma_start(out=vraw[f][32 * q : 32 * (q + 1), :, :], in_=wq[t][:, 4 * g : 4 * g + 4, 256 * q : 256 * (q + 1)])
+                nc.sync.dma_start(out=tile[32 * q : 32 * (q + 1), :, :], in_=wq[t][:, 4 * lo : 4 * hi, 256 * q : 256 * (q + 1)])
+            for g in range(lo, hi):
+                vraw[4 * g + t] = tile[:, 4 * (g - lo) : 4 * (g - lo + 1), :]
 
         def load_dec(g):
             nc.sync.dma_start(out=dw[:, g, :].bitcast(I32), in_=dec_words[g].bitcast(I32))
@@ -104,11 +105,11 @@ def tile_sae_encode_decode_fp8_d4_kernel(tc, x_bytes, x_scale, w_enc, b_enc, dec
         xw, flat, xg, xbank = {}, {}, {}, {}
 
         def x_widen(n, on_vector):
-            xw[n] = work.tile([P, 4, 256], BF16, name="xw", tag="laced", align_bytes=64, bufs=6)
+            xw[n] = work.tile([P, 4, 256], BF16, name="xw", tag="laced", align_bytes=64, bufs=7)
             if not on_vector:
-                flat[n] = work.tile([P, K], BF16, name="flat", tag="laced", align_bytes=64, bufs=6)
+                flat[n] = work.tile([P, K], BF16, name="flat", tag="laced", align_bytes=64, bufs=7)
             for block in range(8):
-                src = xin[n][:, B * block : B * (block + 1)].bitcast(FP8)
+                src = xin[n // 2][:, n % 2, B * block : B * (block + 1)].bitcast(FP8)
                 s = xsc[:, n, block : block + 1]
                 if on_vector:
                     dst = xw[n][:, :, 32 * block : 32 * (block + 1)].rearrange("p s (m j) -> p m s j", j=RUN)
@@ -137,7 +138,7 @@ def tile_sae_encode_decode_fp8_d4_kernel(tc, x_bytes, x_scale, w_enc, b_enc, dec
         dealt, wbank, wg, wc, ws, vsort, vturn = {}, {}, {}, {}, {}, {}, {}
 
         def w_deal(f, count=2, on_vector=True):
-            rows = work.tile([P, 4, count * 256], BF16, name="dealt%d" % count, bufs=4 if count == 2 else 2)
+            rows = work.tile([P, 4, count * 256], BF16, name="dealt", bufs=4)
             deal(rows[:], raw[f][:].rearrange("p i k -> p (i k)"), on_vector)
             for i in range(count):
                 dealt[f + i] = rows[:, :, 256 * i : 256 * (i + 1)]
@@ -145,35 +146,39 @@ def tile_sae_encode_decode_fp8_d4_kernel(tc, x_bytes, x_scale, w_enc, b_enc, dec
         def w_turn(f, at):
             wbank[f] = turn(dealt[f], at)
 
+        def pair_of(f):
+            return {26: (13, 0), 30: (13, 1), 27: (15, 0), 31: (15, 1)}.get(f, divmod(f, 2))
+
         def laid(f):
-            if f // 2 not in wg:
-                wg[f // 2] = work.tile([P, 2, 2, P, 4], BF16, name="wg", align_bytes=64, bufs=4)
-            return wg[f // 2][:, f % 2, :, :, :].rearrange("p c r t -> p (c r t)").bitcast(F32)
+            j, i = pair_of(f)
+            if j not in wg:
+                wg[j] = work.tile([P, 2, 2, P, 4], BF16, name="wg", align_bytes=64, bufs=4)
+            return wg[j][:, i, :, :, :].rearrange("p c r t -> p (c r t)").bitcast(F32)
 
         def w_out(f, on_vector=False):
             words_out(laid(f).rearrange("p (c r u) -> p c r u", c=2, u=2), wbank[f], on_vector)
 
-        def v_deal(g):
-            vsort[g] = work.tile([P, 4, 256], BF16, name="vsort", align_bytes=64)
-            deal(vsort[g][:], vraw[g][:].rearrange("p a k -> p (a k)"))
+        def v_deal(f):
+            vsort[f] = work.tile([P, 4, 256], BF16, name="vsort", align_bytes=64)
+            deal(vsort[f][:], vraw[f].rearrange("p a k -> p (a k)"))
 
-        def v_turn(g):
-            vturn[g] = work.tile([P, 512], F32, name="vturn", align_bytes=64)
-            nc.vector.transpose(out=vturn[g][:], in_=vsort[g][:].rearrange("p s k -> p (s k)").bitcast(F32))
+        def v_turn(f):
+            vturn[f] = work.tile([P, 512], F32, name="vturn", align_bytes=64)
+            nc.vector.transpose(out=vturn[f][:], in_=vsort[f][:].rearrange("p s k -> p (s k)").bitcast(F32))
 
-        def v_out(g, on_vector=True):
+        def v_out(f, on_vector=True):
             copy = nc.vector.tensor_copy if on_vector else nc.scalar.copy
             copy(
-                out=laid(g).rearrange("p (c m u) -> p c m u", c=2, u=2),
-                in_=vturn[g][:].rearrange("p (c u m) -> p c m u", c=2, u=2),
+                out=laid(f).rearrange("p (c m u) -> p c m u", c=2, u=2),
+                in_=vturn[f][:].rearrange("p (c u m) -> p c m u", c=2, u=2),
             )
 
         def w_quant(f, count):
-            j = f // 2
-            if f % 2 == 0:
+            j, i = pair_of(f)
+            if i == 0:
                 wc[j] = work.tile([P, 2, 2, P], U32, name="wc", align_bytes=64, bufs=6)
                 ws[j] = work.tile([P, 2, 2, P], U8, name="ws", align_bytes=64, bufs=6)
-            part = slice(f % 2, f % 2 + count)
+            part = slice(i, i + count)
             nc.vector.quantize_mx(
                 out=wc[j][:, part, :, :].rearrange("p i c r -> p (i c r)").bitcast(FP8X4),
                 scales=ws[j][:, part, :, :].rearrange("p i c r -> p (i c r)"),
@@ -185,11 +190,12 @@ def tile_sae_encode_decode_fp8_d4_kernel(tc, x_bytes, x_scale, w_enc, b_enc, dec
         def encode(f, at, cols=slice(0, T)):
             if f not in pre:
                 pre[f] = psum.tile([P, T], F32, name="pre", tag="bank%d" % at)
+            j, i = pair_of(f)
             for c in range(2):
                 nc.tensor.matmul_mx(
                     out=pre[f][:, cols],
-                    lhsT=wc[f // 2][:, f % 2, c, :].bitcast(FP8X4),
-                    lhsT_scale=ws[f // 2][:, f % 2, c, :],
+                    lhsT=wc[j][:, i, c, :].bitcast(FP8X4),
+                    lhsT_scale=ws[j][:, i, c, :],
                     rhs=xc[:, c, cols].bitcast(FP8X4),
                     rhs_scale=xs[:, c, cols],
                     start=(c == 0),
@@ -198,12 +204,12 @@ def tile_sae_encode_decode_fp8_d4_kernel(tc, x_bytes, x_scale, w_enc, b_enc, dec
 
         def relu_out(f):
             g, t = divmod(f, 4)
-            if t == 0:
-                zt[g] = work.tile([P, 4, T], BF16, name="zt", bufs=GROUPS)
+            if g not in zt:
+                zt[g] = work.tile([P, 4, T], BF16, name="zt", tag="zt", bufs=GROUPS)
             nc.scalar.activation(out=zt[g][:, t, :], in_=pre[f][:], func=ACT.Relu, bias=b_cols[:, g, t : t + 1], scale=1.0)
 
         def z_lace(g, n, count=1, on_vector=True):
-            zi[g, n] = work.tile([P, count * P, 4], BF16, name="zi", tag="laced", align_bytes=64, bufs=6)
+            zi[g, n] = work.tile([P, count * P, 4], BF16, name="zi", tag="laced", align_bytes=64, bufs=7)
             copy = nc.vector.tensor_copy if on_vector else nc.scalar.copy
             copy(
                 out=zi[g, n][:].rearrange("p (c i) t -> p c t i", i=4),
@@ -234,7 +240,7 @@ def tile_sae_encode_decode_fp8_d4_kernel(tc, x_bytes, x_scale, w_enc, b_enc, dec
             )
 
         def store_cols(bank, n, lo, width):
-            o = work.tile([P, width], F32, name="o", tag="raw2", bufs=13)
+            o = work.tile([P, width], F32, name="o", tag="zt", bufs=GROUPS)
             cols = slice(lo, lo + width)
             nc.vector.tensor_tensor(out=o[:], in0=bank[:, 0:width], in1=bd[:, cols], op=ALU.add)
             nc.sync.dma_start(out=orows[n][:, cols], in_=o[:])
@@ -249,254 +255,235 @@ def tile_sae_encode_decode_fp8_d4_kernel(tc, x_bytes, x_scale, w_enc, b_enc, dec
 
         nc.scalar.dma_start(out=xsc[:], in_=x_scale.rearrange("(p n) b -> p n b", p=P))
         nc.scalar.activation(out=early[:], in_=warm[:, 0:2], func=ACT.Copy)
-        for n in (0, 2, 1):
-            nc.sync.dma_start(out=xin[n][:], in_=xr[n])
-        load_w(0, 1)
-        nc.sync.dma_start(out=xin[3][:], in_=xr[3])
-        load_w(1, 1)
-        load_w(2, 2)
+        for i in range(2):
+            nc.sync.dma_start(out=xin[i][:], in_=xr[i])
         nc.sync.dma_start(out=b_rows[0:GROUPS, :], in_=b_enc.rearrange("(g k) -> g k", g=GROUPS))
-        for f in range(4, 16, 2):
+        for f in range(0, 22, 2):
             load_w(f, 2)
         load_dec(0)
         load_dec_scales(0)
-        for f in range(16, 22, 2):
-            load_w(f, 2)
+        load_w(22, 2)
+        load_w(24, 2)
+        load_w(28, 2)
         load_dec(1)
-        for f in range(22, BY_TENSOR, 2):
-            load_w(f, 2)
         load_dec(2)
         load_dec_scales(1)
-        load_v(28)
+        load_v(3, 6, 8)
         load_dec(3)
-        load_v(29)
+        load_v(2, 6, 8)
         load_dec(4)
         load_dec_scales(2)
-        load_v(30)
-        load_v(31)
         for g in range(5, GROUPS):
             load_dec(g)
         nc.sync.dma_start(out=bd[:], in_=b_dec.partition_broadcast(P))
 
         for i in range(4):
             warm_up(4 + i)
-        x_widen(0, True)
-        x_widen(2, False)
-        x_widen(1, True)
-        w_deal(0, 1)
-        x_turn(0, 0)
-        warm_up(7)
-        x_turn(1, 1)
-        w_turn(0, 2)
-        deal(xw[2][:], flat[2][:])
-        w_deal(1, 1)
-        x_out(0)
-        x_out(1)
-        w_out(0)
-        x_turn(2, 3)
-        w_turn(1, 4)
-        x_widen(3, True)
-        w_deal(2)
-        x_quant(0)
-        w_quant(0, 1)
-        x_turn(3, 5)
-        b_bank = psum.tile([P, 2, P], F32, name="b_bank", tag="bank6")
+        b_bank = psum.tile([P, 2, P], F32, name="b_bank", tag="bank4")
         for u in range(2):
             nc.tensor.transpose(b_bank[:, u, :], b_rows[:].bitcast(F32)[:, u : 2 * P : 2], ident[:])
-        w_turn(2, 7)
-        w_turn(3, 0)
-        w_out(1)
-        x_out(2)
-        x_out(3)
-        encode(0, 1, slice(0, HALF))
-        w_deal(4)
-        w_quant(1, 1)
-        w_deal(6)
-        x_quant(1)
-        encode(1, 2, slice(0, HALF))
+        x_widen(0, True)
+        x_widen(1, False)
+        x_widen(2, True)
+        deal(xw[1][:], flat[1][:])
+        w_deal(0)
+        x_widen(3, True)
         nc.scalar.copy(out=b_cols[:].bitcast(F32), in_=b_bank[:, :, 0:GROUPS].rearrange("p u g -> p g u"))
+        x_turn(0, 0)
+        x_out(0)
+        x_turn(2, 1)
+        x_out(2)
+        warm_up(5)
+        x_turn(1, 2)
+        x_out(1)
+        w_turn(0, 6)
+        w_turn(1, 7)
+        x_turn(3, 3)
+        w_deal(2)
+        w_turn(2, 4)
+        w_turn(3, 5)
+        x_quant(0)
+        w_out(0)
+        w_out(1)
+        x_out(3)
+        w_quant(0, 1)
+        w_quant(1, 1)
         w_out(2)
         w_out(3)
-        for f in range(4, 8):
-            w_turn(f, f - 1)
-        encode(0, 1, slice(HALF, T))
-        encode(1, 2, slice(HALF, T))
+        encode(0, 6, slice(0, HALF))
+        encode(1, 7, slice(0, HALF))
+        w_deal(4)
+        w_turn(4, 0)
+        w_turn(5, 1)
+        x_quant(1)
+        encode(0, 6, slice(HALF, T))
+        encode(1, 7, slice(HALF, T))
+        w_deal(6)
         w_quant(2, 2)
-        w_out(5, True)
         w_out(4)
-        w_deal(8)
-        w_out(6)
-        w_out(7)
-        w_quant(4, 2)
+        w_out(5)
         relu_out(0)
         relu_out(1)
-        encode(2, 7)
-        encode(3, 0)
-        encode(4, 3)
-        w_deal(10)
-        w_quant(6, 2)
-        w_deal(12)
-        relu_out(2)
-        relu_out(3)
-        relu_out(4)
 
-        for f, at in zip(range(8, 16), (4, 5, 6, 1, 2, 7, 0, 3)):
-            if f == 14:
-                w_out(8, True)
-                w_deal(14)
-            w_turn(f, at)
-        for f in range(9, 16):
-            w_out(f, f in (10, 12))
-            if f in (10, 12):
-                w_quant(f - 2, 2)
-        z_lace(0, 0)
-        w_deal(16)
-        w_quant(12, 2)
-        z_quant(0, 0)
-        w_deal(18)
-        w_quant(14, 2)
-        w_deal(20)
-        for f, at in zip(range(5, 12), (4, 5, 6, 1, 2, 7, 0)):
-            encode(f, at)
-            relu_out(f)
-        decode(0, 0, 0, 3)
-        for f, at in zip(range(16, 22), (4, 5, 6, 1, 2, 0)):
-            w_turn(f, at)
-        z_lace(1, 0)
-        for f in range(16, 22):
-            w_out(f, f in (16, 18))
-        z_quant(1, 0)
-        w_quant(16, 2)
-        w_deal(22)
-        w_quant(18, 2)
-        w_deal(24)
-        w_quant(20, 2)
-        w_deal(26)
-        decode(0, 0, 1, 7)
-        for f, at in zip(range(12, 18), (4, 5, 6, 1, 2, 0)):
-            encode(f, at)
-            relu_out(f)
-        z_lace(2, 0)
-        z_lace(3, 0)
-        z_quant(2, 0)
-        decode(0, 1, 0)
-        decode(0, 1, 1)
-        for f, at in zip(range(22, 28), (4, 5, 6, 1, 2, 0)):
-            w_turn(f, at)
-        for f in range(22, 28):
-            w_out(f, f == 22)
-            if f == 22:
-                z_quant(3, 0)
-                z_lace(0, 1, 2)
-        w_quant(22, 2)
-        v_deal(28)
-        z_quant(0, 1, 2)
-        w_quant(24, 2)
-        v_turn(28)
-        z_lace(1, 1, 2)
-        w_quant(26, 2)
-        z_quant(1, 1, 2)
-        decode(0, 2, 0)
-        decode(0, 2, 1)
-        for f, at in zip(range(18, 24), (4, 5, 6, 1, 2, 0)):
-            encode(f, at)
-            relu_out(f)
-        decode(0, 3, 0)
-        decode(0, 3, 1)
+        def turns(tiles, banks):
+            for f, at in zip(tiles, banks):
+                w_turn(f, at)
+
+        def encodes(tiles, banks):
+            for f, at in zip(tiles, banks):
+                encode(f, at)
+                relu_out(f)
 
         def both(n, g, at=None):
             for h in range(2):
                 decode(n, g, h, None if at is None else at[h])
 
-        def feature(f):
-            encode(f, 2 * (f % 2 == 0))
+        turns((6, 7), (2, 3))
+        w_deal(8)
+        w_quant(4, 2)
+        w_out(6, True)
+        w_out(7)
+        w_deal(10)
+        w_deal(12)
+        encodes(range(2, 6), (4, 5, 0, 1))
+        turns(range(8, 12), (6, 7, 2, 4))
+        w_deal(14)
+        w_quant(6, 2)
+        turns(range(12, 16), (3, 0, 5, 1))
+        for f in (8, 9, 12):
+            w_out(f, True)
+        for f in (10, 11, 13, 14, 15):
+            w_out(f)
+        w_quant(8, 2)
+        w_deal(16)
+        w_quant(10, 2)
+        w_deal(18)
+        w_quant(12, 2)
+        w_deal(20)
+        w_quant(14, 2)
+        z_lace(0, 0)
+        encodes(range(6, 14), (6, 7, 3, 4, 2, 5, 0, 1))
+        turns(range(16, 22), (6, 7, 3, 4, 2, 5))
+        z_lace(1, 0)
+        z_quant(0, 0)
+        for f in range(16, 22):
+            w_out(f, f < 18)
+        z_quant(1, 0)
+        w_quant(16, 2)
+        w_deal(22)
+        w_deal(24)
+        w_quant(18, 2)
+        z_lace(2, 0)
+        w_deal(28)
+        z_quant(2, 0)
+        w_quant(20, 2)
+        encodes((14, 15), (6, 7))
+        both(0, 0, (0, 3))
+        encodes(range(16, 20), (1, 2, 4, 5))
+        both(0, 1)
+        z_lace(0, 1, 2)
+        z_lace(3, 0)
+        z_quant(0, 1, 2)
+        turns((22, 23, 24, 25, 28, 29), (6, 7, 1, 2, 4, 5))
+        for f in (22, 23, 24, 25, 28, 29):
+            w_out(f, f == 22)
+        z_quant(3, 0)
+        z_lace(1, 1, 2)
+        w_quant(22, 2)
+        v_deal(27)
+        z_quant(1, 1, 2)
+        w_quant(24, 2)
+        v_turn(27)
+        v_deal(31)
+        v_out(27)
+        v_turn(31)
+        both(0, 2)
+        encodes((20, 21, 22, 23, 24, 25), (6, 1, 7, 4, 2, 5))
+        both(0, 3)
+
+        def feature(f, at):
+            encode(f, at)
             relu_out(f)
 
-        v_deal(29)
-        v_out(28)
-        v_turn(29)
-        z_lace(4, 0)
-        both(1, 0, (4, 5))
-        feature(24)
-        z_lace(2, 1, 1, False)
-        both(2, 0, (6, 1))
-        feature(25)
-        z_lace(2, 2, 1, False)
-        v_deal(30)
-        v_out(29)
-        z_quant(4, 0)
-        v_turn(30)
-        z_quant(2, 1)
         w_quant(28, 2)
-        z_quant(2, 2)
-        both(1, 1)
-        feature(26)
-        z_lace(3, 1, 1, False)
-        both(2, 1)
-        feature(27)
-        z_lace(3, 2, 1, False)
-        v_deal(31)
-        v_out(30)
-        v_turn(31)
-        z_quant(3, 1)
-        z_lace(5, 0)
         v_out(31)
-        z_quant(3, 2)
+        z_lace(4, 0)
+        v_deal(26)
+        w_quant(27, 2)
+        v_turn(26)
+        z_quant(4, 0)
+        z_lace(2, 1, 2, False)
+        both(1, 0, (6, 1))
+        both(2, 0, (7, 4))
+        feature(28, 2)
+        z_lace(3, 1, 1, False)
+        both(1, 1)
+        feature(29, 5)
+        z_lace(3, 2, 1, False)
+        v_deal(30)
+        z_quant(2, 1, 2)
+        v_out(26)
+        v_turn(30)
+        z_lace(5, 0)
+        z_quant(3, 1)
+        v_out(30)
         z_quant(5, 0)
-        w_quant(30, 2)
+        z_quant(3, 2)
+        w_quant(26, 2)
+        z_lace(4, 1, 2)
+        both(2, 1)
+        feature(27, 2)
         both(0, 4)
+        feature(31, 5)
+        z_lace(1, 3, 1, False)
         both(1, 2)
-        feature(28)
-        z_lace(4, 1, 1, False)
         both(2, 2)
-        feature(29)
-        z_lace(4, 2, 1, False)
         both(1, 3)
+        feature(26, 2)
+        z_lace(0, 3, 1, False)
         both(2, 3)
-        feature(30)
-        both(0, 5)
-        feature(31)
+        feature(30, 5)
         z_lace(5, 1, 2)
-        z_quant(4, 1)
-        z_quant(4, 2)
+        z_quant(4, 1, 2)
+        z_lace(2, 3)
         z_quant(5, 1, 2)
         z_lace(6, 0, 2)
+        z_quant(1, 3)
+        z_quant(2, 3)
+        z_quant(0, 3)
+        z_lace(7, 0, 2)
+        z_quant(6, 0, 2)
         z_lace(6, 2, 2, False)
         z_lace(7, 2, 2, False)
-        z_lace(0, 3)
-        z_quant(6, 0, 2)
-        z_lace(7, 0, 2)
-        z_quant(0, 3)
-        z_quant(6, 2, 2)
+        z_lace(3, 3)
         z_quant(7, 0, 2)
-        z_lace(1, 3)
+        z_quant(6, 2, 2)
+        both(0, 5)
         for g in (4, 5):
             both(1, g)
             both(2, g)
         both(0, 6)
-        both(1, 6)
         both(0, 7)
-        both(2, 6)
+        both(1, 6)
         both(1, 7)
+        both(2, 6)
+        z_quant(3, 3)
         z_quant(7, 2, 2)
-        z_quant(1, 3)
         both(2, 7)
-        for g in range(2, 6):
+        for g in range(4, 6):
             z_lace(g, 3, 1, False)
         store(0, 0)
-        z_quant(2, 3)
-        store(0, 1)
-        z_quant(3, 3)
         z_quant(4, 3)
-        store(1, 0)
+        store(0, 1)
         z_quant(5, 3)
+        store(1, 0)
         store(1, 1)
         store(2, 0)
         store(2, 1)
         for g in range(GROUPS):
             decode(3, g, 0, 2)
         store(3, 0)
-        for lo, width, at in ((512, 256, 0), (768, P, 3), (896, P, 7)):
+        for lo, width, at in ((512, 256, 5), (768, P, 0), (896, P, 3)):
             piece = psum.tile([P, 512], F32, name="piece", tag="bank%d" % at)
             for g in range(GROUPS):
                 decode_cols(piece, 3, g, lo, width)

@@ -23,7 +23,7 @@ TILES = F // P
 HALF = T // 2
 RUN = 16
 BY_TENSOR = 28
-SCALE_PARTS = ((0, 2), (2, 4), (4, 8))
+SCALE_PARTS = ((0, 4), (4, 8))
 
 
 def tile_sae_encode_decode_fp8_d4_kernel(tc, x_bytes, x_scale, w_enc, b_enc, dec_words, dec_scales, b_dec, out):
@@ -70,15 +70,13 @@ def tile_sae_encode_decode_fp8_d4_kernel(tc, x_bytes, x_scale, w_enc, b_enc, dec
             raw[f] = work.tile([P, count, K], BF16, name="raw%d" % count, bufs=14)
             nc.sync.dma_start(out=raw[f][:], in_=wr[f // 4][:, f % 4 : f % 4 + count, :])
 
-        def load_v(t, lo, hi):
-            tile = keep.tile([P, 4 * (hi - lo), 256], BF16, name="vraw%d" % (4 * lo + t))
+        def load_v(t):
+            vraw[t] = keep.tile([P, 8, 256], BF16, name="vraw%d" % t)
             for q in (0, 2, 1, 3):
-                nc.sync.dma_start(out=tile[32 * q : 32 * (q + 1), :, :], in_=wq[t][:, 4 * lo : 4 * hi, 256 * q : 256 * (q + 1)])
-            for g in range(lo, hi):
-                vraw[4 * g + t] = tile[:, 4 * (g - lo) : 4 * (g - lo + 1), :]
+                nc.sync.dma_start(out=vraw[t][32 * q : 32 * (q + 1), :, :], in_=wq[t][:, 24:32, 256 * q : 256 * (q + 1)])
 
-        def load_dec(g):
-            nc.sync.dma_start(out=dw[:, g, :].bitcast(I32), in_=dec_words[g].bitcast(I32))
+        def load_dec(g, count=1):
+            nc.sync.dma_start(out=dw[:, g : g + count, :].bitcast(I32), in_=dec_words[g : g + count].rearrange("g p n -> p g n").bitcast(I32))
 
         def load_dec_scales(part):
             lo, hi = SCALE_PARTS[part]
@@ -105,9 +103,9 @@ def tile_sae_encode_decode_fp8_d4_kernel(tc, x_bytes, x_scale, w_enc, b_enc, dec
         xw, flat, xg, xbank = {}, {}, {}, {}
 
         def x_widen(n, on_vector):
-            xw[n] = work.tile([P, 4, 256], BF16, name="xw", tag="laced", align_bytes=64, bufs=7)
+            xw[n] = work.tile([P, 4, 256], BF16, name="xw", tag="laced", align_bytes=64, bufs=8)
             if not on_vector:
-                flat[n] = work.tile([P, K], BF16, name="flat", tag="laced", align_bytes=64, bufs=7)
+                flat[n] = work.tile([P, K], BF16, name="flat", tag="laced", align_bytes=64, bufs=8)
             for block in range(8):
                 src = xin[n // 2][:, n % 2, B * block : B * (block + 1)].bitcast(FP8)
                 s = xsc[:, n, block : block + 1]
@@ -158,19 +156,20 @@ def tile_sae_encode_decode_fp8_d4_kernel(tc, x_bytes, x_scale, w_enc, b_enc, dec
         def w_out(f, on_vector=False):
             words_out(laid(f).rearrange("p (c r u) -> p c r u", c=2, u=2), wbank[f], on_vector)
 
-        def v_deal(f):
-            vsort[f] = work.tile([P, 4, 256], BF16, name="vsort", align_bytes=64)
-            deal(vsort[f][:], vraw[f].rearrange("p a k -> p (a k)"))
+        def v_deal(t):
+            vsort[t] = work.tile([P, 4, 512], BF16, name="vsort", align_bytes=64, bufs=1)
+            deal(vsort[t][:], vraw[t][:].rearrange("p a k -> p (a k)"))
 
-        def v_turn(f):
-            vturn[f] = work.tile([P, 512], F32, name="vturn", align_bytes=64)
-            nc.vector.transpose(out=vturn[f][:], in_=vsort[f][:].rearrange("p s k -> p (s k)").bitcast(F32))
+        def v_turn(t):
+            vturn[t] = work.tile([P, 1024], F32, name="vturn", align_bytes=64, bufs=1)
+            nc.vector.transpose(out=vturn[t][:], in_=vsort[t][:].rearrange("p s k -> p (s k)").bitcast(F32))
 
-        def v_out(f, on_vector=True):
-            copy = nc.vector.tensor_copy if on_vector else nc.scalar.copy
-            copy(
-                out=laid(f).rearrange("p (c m u) -> p c m u", c=2, u=2),
-                in_=vturn[f][:].rearrange("p (c u m) -> p c m u", c=2, u=2),
+        def v_out(t):
+            laid(24 + t)
+            words = wg[pair_of(24 + t)[0]][:].rearrange("p i c r t -> p (i c r t)").bitcast(F32)
+            nc.vector.tensor_copy(
+                out=words.rearrange("p (i c m u) -> p i c m u", i=2, c=2, u=2),
+                in_=vturn[t][:].rearrange("p (c u i m) -> p i c m u", c=2, u=2, i=2),
             )
 
         def w_quant(f, count):
@@ -208,11 +207,13 @@ def tile_sae_encode_decode_fp8_d4_kernel(tc, x_bytes, x_scale, w_enc, b_enc, dec
                 zt[g] = work.tile([P, 4, T], BF16, name="zt", tag="zt", bufs=GROUPS)
             nc.scalar.activation(out=zt[g][:, t, :], in_=pre[f][:], func=ACT.Relu, bias=b_cols[:, g, t : t + 1], scale=1.0)
 
-        def z_lace(g, n, count=1, on_vector=True):
-            zi[g, n] = work.tile([P, count * P, 4], BF16, name="zi", tag="laced", align_bytes=64, bufs=7)
+        def z_lace(g, n, count=1, on_vector=True, into=None):
+            first = n if into is None else into
+            if (g, first) not in zi:
+                zi[g, first] = work.tile([P, (count if into is None else 2) * P, 4], BF16, name="zi", tag="laced", align_bytes=64, bufs=8)
             copy = nc.vector.tensor_copy if on_vector else nc.scalar.copy
             copy(
-                out=zi[g, n][:].rearrange("p (c i) t -> p c t i", i=4),
+                out=zi[g, first][:, P * (n - first) : P * (n - first + count), :].rearrange("p (c i) t -> p c t i", i=4),
                 in_=zt[g][:, :, P * n : P * (n + count)].rearrange("p t (c i) -> p c t i", i=4),
             )
 
@@ -227,7 +228,7 @@ def tile_sae_encode_decode_fp8_d4_kernel(tc, x_bytes, x_scale, w_enc, b_enc, dec
         orows = out.rearrange("(p n) k -> n p k", p=P)
 
         def decode_cols(bank, n, g, lo, width):
-            part = min(g // 2, 2)
+            part = g // 4
             at = K * (g - SCALE_PARTS[part][0]) + lo
             nc.tensor.matmul_mx(
                 out=bank[:, 0:width],
@@ -265,16 +266,13 @@ def tile_sae_encode_decode_fp8_d4_kernel(tc, x_bytes, x_scale, w_enc, b_enc, dec
         load_w(22, 2)
         load_w(24, 2)
         load_w(28, 2)
-        load_dec(1)
-        load_dec(2)
+        load_dec(1, 2)
+        load_v(3)
+        load_dec(3, 2)
+        load_v(2)
         load_dec_scales(1)
-        load_v(3, 6, 8)
-        load_dec(3)
-        load_v(2, 6, 8)
-        load_dec(4)
-        load_dec_scales(2)
-        for g in range(5, GROUPS):
-            load_dec(g)
+        load_dec(5)
+        load_dec(6, 2)
         nc.sync.dma_start(out=bd[:], in_=b_dec.partition_broadcast(P))
 
         for i in range(4):
@@ -386,17 +384,16 @@ def tile_sae_encode_decode_fp8_d4_kernel(tc, x_bytes, x_scale, w_enc, b_enc, dec
         z_quant(0, 1, 2)
         turns((22, 23, 24, 25, 28, 29), (6, 7, 1, 2, 4, 5))
         for f in (22, 23, 24, 25, 28, 29):
-            w_out(f, f == 22)
+            w_out(f, f < 24)
         z_quant(3, 0)
         z_lace(1, 1, 2)
         w_quant(22, 2)
-        v_deal(27)
         z_quant(1, 1, 2)
         w_quant(24, 2)
-        v_turn(27)
-        v_deal(31)
-        v_out(27)
-        v_turn(31)
+        v_deal(3)
+        z_lace(4, 0)
+        v_turn(3)
+        w_quant(28, 2)
         both(0, 2)
         encodes((20, 21, 22, 23, 24, 25), (6, 1, 7, 4, 2, 5))
         both(0, 3)
@@ -405,38 +402,32 @@ def tile_sae_encode_decode_fp8_d4_kernel(tc, x_bytes, x_scale, w_enc, b_enc, dec
             encode(f, at)
             relu_out(f)
 
-        w_quant(28, 2)
-        v_out(31)
-        z_lace(4, 0)
-        v_deal(26)
-        w_quant(27, 2)
-        v_turn(26)
+        v_out(3)
         z_quant(4, 0)
+        v_deal(2)
         z_lace(2, 1, 2, False)
+        w_quant(27, 2)
+        z_quant(2, 1, 2)
+        v_turn(2)
         both(1, 0, (6, 1))
         both(2, 0, (7, 4))
         feature(28, 2)
-        z_lace(3, 1, 1, False)
+        z_lace(3, 1, 1, False, 1)
         both(1, 1)
         feature(29, 5)
-        z_lace(3, 2, 1, False)
-        v_deal(30)
-        z_quant(2, 1, 2)
-        v_out(26)
-        v_turn(30)
+        z_lace(3, 2, 1, False, 1)
+        z_lace(4, 1, 1, False, 1)
         z_lace(5, 0)
-        z_quant(3, 1)
-        v_out(30)
+        v_out(2)
+        z_quant(3, 1, 2)
         z_quant(5, 0)
-        z_quant(3, 2)
         w_quant(26, 2)
-        z_lace(4, 1, 2)
         both(2, 1)
+        both(1, 2)
         feature(27, 2)
+        z_lace(4, 2, 1, False, 1)
         both(0, 4)
         feature(31, 5)
-        z_lace(1, 3, 1, False)
-        both(1, 2)
         both(2, 2)
         both(1, 3)
         feature(26, 2)
@@ -447,17 +438,19 @@ def tile_sae_encode_decode_fp8_d4_kernel(tc, x_bytes, x_scale, w_enc, b_enc, dec
         z_quant(4, 1, 2)
         z_lace(2, 3)
         z_quant(5, 1, 2)
-        z_lace(6, 0, 2)
-        z_quant(1, 3)
         z_quant(2, 3)
+        z_lace(6, 0, 2)
         z_quant(0, 3)
         z_lace(7, 0, 2)
         z_quant(6, 0, 2)
         z_lace(6, 2, 2, False)
         z_lace(7, 2, 2, False)
-        z_lace(3, 3)
+        z_lace(1, 3)
         z_quant(7, 0, 2)
+        z_lace(3, 3)
         z_quant(6, 2, 2)
+        z_quant(1, 3)
+        z_quant(3, 3)
         both(0, 5)
         for g in (4, 5):
             both(1, g)
@@ -467,7 +460,6 @@ def tile_sae_encode_decode_fp8_d4_kernel(tc, x_bytes, x_scale, w_enc, b_enc, dec
         both(1, 6)
         both(1, 7)
         both(2, 6)
-        z_quant(3, 3)
         z_quant(7, 2, 2)
         both(2, 7)
         for g in range(4, 6):

@@ -353,10 +353,10 @@ def tile_sae_encode_decode_fp8_d4_kernel(tc, x_bytes, x_scale, w_enc, b_enc, dec
         for f in (10, 11, 13, 14, 15):
             w_out(f)
         w_quant(8, 2)
-        w_deal(16)
         w_quant(10, 2)
-        w_deal(18)
+        w_deal(16)
         w_quant(12, 2)
+        w_deal(18)
         w_deal(20)
         w_quant(14, 2)
         z_lace(0, 0)
@@ -381,19 +381,19 @@ def tile_sae_encode_decode_fp8_d4_kernel(tc, x_bytes, x_scale, w_enc, b_enc, dec
         both(0, 1)
         z_lace(0, 1, 2)
         z_lace(3, 0)
-        z_quant(0, 1, 2)
         turns((22, 23, 24, 25, 28, 29), (6, 7, 1, 2, 4, 5))
         for f in (22, 23, 24, 25, 28, 29):
             w_out(f, f < 24)
+        z_quant(0, 1, 2)
         z_quant(3, 0)
-        z_lace(1, 1, 2)
         w_quant(22, 2)
-        z_quant(1, 1, 2)
+        z_lace(1, 1, 2)
         w_quant(24, 2)
+        z_quant(1, 1, 2)
+        w_quant(28, 2)
         v_deal(3)
         z_lace(4, 0)
         v_turn(3)
-        w_quant(28, 2)
         both(0, 2)
         encodes((20, 21, 22, 23, 24, 25), (6, 1, 7, 4, 2, 5))
         both(0, 3)
@@ -402,12 +402,14 @@ def tile_sae_encode_decode_fp8_d4_kernel(tc, x_bytes, x_scale, w_enc, b_enc, dec
             encode(f, at)
             relu_out(f)
 
-        v_out(3)
         z_quant(4, 0)
+        z_lace(5, 0)
+        v_out(3)
+        z_quant(5, 0)
         v_deal(2)
         z_lace(2, 1, 2, False)
-        w_quant(27, 2)
         z_quant(2, 1, 2)
+        w_quant(27, 2)
         v_turn(2)
         both(1, 0, (6, 1))
         both(2, 0, (7, 4))
@@ -416,64 +418,64 @@ def tile_sae_encode_decode_fp8_d4_kernel(tc, x_bytes, x_scale, w_enc, b_enc, dec
         both(1, 1)
         feature(29, 5)
         z_lace(3, 2, 1, False, 1)
-        z_lace(4, 1, 1, False, 1)
-        z_lace(5, 0)
-        v_out(2)
+        z_lace(4, 1, 2, False)
         z_quant(3, 1, 2)
-        z_quant(5, 0)
+        v_out(2)
+        z_quant(4, 1, 2)
         w_quant(26, 2)
         both(2, 1)
+        both(0, 4)
         both(1, 2)
         feature(27, 2)
-        z_lace(4, 2, 1, False, 1)
-        both(0, 4)
-        feature(31, 5)
         both(2, 2)
-        both(1, 3)
-        feature(26, 2)
+        feature(31, 5)
         z_lace(0, 3, 1, False)
+        z_lace(1, 3, 1, False)
+        both(0, 5)
+        both(1, 3)
         both(2, 3)
+        feature(26, 2)
+        both(1, 4)
         feature(30, 5)
         z_lace(5, 1, 2)
-        z_quant(4, 1, 2)
         z_lace(2, 3)
         z_quant(5, 1, 2)
-        z_quant(2, 3)
-        z_lace(6, 0, 2)
+        z_lace(3, 3)
         z_quant(0, 3)
-        z_lace(7, 0, 2)
+        z_quant(1, 3)
+        z_lace(6, 0, 2)
+        z_quant(2, 3)
         z_quant(6, 0, 2)
+        z_lace(7, 0, 2)
         z_lace(6, 2, 2, False)
         z_lace(7, 2, 2, False)
-        z_lace(1, 3)
-        z_quant(7, 0, 2)
-        z_lace(3, 3)
-        z_quant(6, 2, 2)
-        z_quant(1, 3)
         z_quant(3, 3)
-        both(0, 5)
-        for g in (4, 5):
-            both(1, g)
-            both(2, g)
+        z_quant(7, 0, 2)
+        z_lace(4, 3)
+        z_quant(6, 2, 2)
+        z_quant(4, 3)
+        both(2, 4)
+        both(1, 5)
+        both(2, 5)
+        for g in range(2):
+            decode(3, g, 0, 2)
         both(0, 6)
-        both(0, 7)
         both(1, 6)
+        both(0, 7)
         both(1, 7)
         both(2, 6)
         z_quant(7, 2, 2)
         both(2, 7)
-        for g in range(4, 6):
-            z_lace(g, 3, 1, False)
+        z_lace(5, 3, 1, False)
         store(0, 0)
-        z_quant(4, 3)
         store(0, 1)
         z_quant(5, 3)
         store(1, 0)
         store(1, 1)
         store(2, 0)
         store(2, 1)
-        for g in range(GROUPS):
-            decode(3, g, 0, 2)
+        for g in range(2, GROUPS):
+            decode(3, g, 0)
         store(3, 0)
         for lo, width, at in ((512, 256, 5), (768, P, 0), (896, P, 3)):
             piece = psum.tile([P, 512], F32, name="piece", tag="bank%d" % at)

@@ -403,13 +403,11 @@ def tile_sae_encode_decode_fp8_d4_kernel(tc, x_bytes, x_scale, w_enc, b_enc, dec
             relu_out(f)
 
         z_quant(4, 0)
-        z_lace(5, 0)
         v_out(3)
-        z_quant(5, 0)
         v_deal(2)
         z_lace(2, 1, 2, False)
-        z_quant(2, 1, 2)
         w_quant(27, 2)
+        z_quant(2, 1, 2)
         v_turn(2)
         both(1, 0, (6, 1))
         both(2, 0, (7, 4))
@@ -418,64 +416,63 @@ def tile_sae_encode_decode_fp8_d4_kernel(tc, x_bytes, x_scale, w_enc, b_enc, dec
         both(1, 1)
         feature(29, 5)
         z_lace(3, 2, 1, False, 1)
-        z_lace(4, 1, 2, False)
+        z_lace(5, 0, 1, False)
         z_quant(3, 1, 2)
         v_out(2)
-        z_quant(4, 1, 2)
+        z_quant(5, 0)
         w_quant(26, 2)
+        z_lace(4, 1, 2)
         both(2, 1)
         both(0, 4)
-        both(1, 2)
         feature(27, 2)
-        both(2, 2)
+        both(1, 2)
         feature(31, 5)
-        z_lace(0, 3, 1, False)
-        z_lace(1, 3, 1, False)
-        both(0, 5)
+        z_lace(5, 1, 2, False)
+        both(2, 2)
         both(1, 3)
-        both(2, 3)
+        both(0, 5)
         feature(26, 2)
-        both(1, 4)
         feature(30, 5)
-        z_lace(5, 1, 2)
-        z_lace(2, 3)
+        both(2, 3)
+        z_lace(0, 3)
+        z_quant(4, 1, 2)
+        z_lace(1, 3)
         z_quant(5, 1, 2)
-        z_lace(3, 3)
-        z_quant(0, 3)
-        z_quant(1, 3)
         z_lace(6, 0, 2)
-        z_quant(2, 3)
-        z_quant(6, 0, 2)
         z_lace(7, 0, 2)
+        z_quant(6, 0, 2)
         z_lace(6, 2, 2, False)
         z_lace(7, 2, 2, False)
-        z_quant(3, 3)
         z_quant(7, 0, 2)
-        z_lace(4, 3)
+        z_quant(0, 3)
+        z_quant(1, 3)
+        z_lace(2, 3)
         z_quant(6, 2, 2)
-        z_quant(4, 3)
+        z_quant(2, 3)
+        both(1, 4)
         both(2, 4)
         both(1, 5)
         both(2, 5)
-        for g in range(2):
-            decode(3, g, 0, 2)
         both(0, 6)
-        both(1, 6)
         both(0, 7)
+        both(1, 6)
         both(1, 7)
-        both(2, 6)
-        z_quant(7, 2, 2)
-        both(2, 7)
-        z_lace(5, 3, 1, False)
+        for g in range(3, 6):
+            z_lace(g, 3, 1, False)
         store(0, 0)
+        z_quant(7, 2, 2)
         store(0, 1)
-        z_quant(5, 3)
+        z_quant(3, 3)
         store(1, 0)
+        z_quant(4, 3)
+        z_quant(5, 3)
         store(1, 1)
+        both(2, 6)
+        both(2, 7)
         store(2, 0)
         store(2, 1)
-        for g in range(2, GROUPS):
-            decode(3, g, 0)
+        for g in range(GROUPS):
+            decode(3, g, 0, 2)
         store(3, 0)
         for lo, width, at in ((512, 256, 5), (768, P, 0), (896, P, 3)):
             piece = psum.tile([P, 512], F32, name="piece", tag="bank%d" % at)

@@ -275,8 +275,8 @@ def tile_sae_encode_decode_fp8_d4_kernel(tc, x_bytes, x_scale, w_enc, b_enc, dec
         load_dec(6, 2)
         nc.sync.dma_start(out=bd[:], in_=b_dec.partition_broadcast(P))
 
-        for i in range(4):
-            warm_up(4 + i)
+        for i in range(5):
+            warm_up(3 + i)
         b_bank = psum.tile([P, 2, P], F32, name="b_bank", tag="bank4")
         for u in range(2):
             nc.tensor.transpose(b_bank[:, u, :], b_rows[:].bitcast(F32)[:, u : 2 * P : 2], ident[:])
@@ -291,9 +291,9 @@ def tile_sae_encode_decode_fp8_d4_kernel(tc, x_bytes, x_scale, w_enc, b_enc, dec
         x_out(0)
         x_turn(2, 1)
         x_out(2)
-        warm_up(5)
         x_turn(1, 2)
         x_out(1)
+        warm_up(5)
         w_turn(0, 6)
         w_turn(1, 7)
         x_turn(3, 3)

from contextlib import ExitStack

import concourse.mybir as mybir
from concourse.masks import make_identity

T, K, F, B = 512, 1024, 4096, 128
FLOPS = 2 * 2 * T * K * F

F32 = mybir.dt.float32
BF16 = mybir.dt.bfloat16
I32 = mybir.dt.int32
U32 = mybir.dt.uint32
U8 = mybir.dt.uint8
FP8 = mybir.dt.float8_e4m3fn
FP8X4 = mybir.dt.float8_e4m3fn_x4
FP4X4 = mybir.dt.float4_e2m1fn_x4
ALU = mybir.AluOpType
ACT = mybir.ActivationFunctionType

P = 128
GROUPS = F // 512
TILES = F // P
HALF = T // 2
RUN = 16
BY_TENSOR = 28
SCALE_PARTS = ((0, 4), (4, 8))


def tile_sae_encode_decode_fp8_d4_kernel(tc, x_bytes, x_scale, w_enc, b_enc, dec_words, dec_scales, b_dec, out):
    nc = tc.nc
    last = GROUPS - 1
    with ExitStack() as ctx:
        keep = ctx.enter_context(tc.tile_pool(name="keep", bufs=1))
        work = ctx.enter_context(tc.tile_pool(name="work", bufs=2))
        psum = ctx.enter_context(tc.psum_pool(name="psum", bufs=1))

        ident = keep.tile([P, P], F32, name="ident")
        dsc = [keep.tile([P, (hi - lo) * K], U8, name="dsc%d" % lo, align_bytes=64) for lo, hi in SCALE_PARTS]
        dw = keep.tile([P, GROUPS, 2 * K], U8, name="dw", align_bytes=64)
        zc = keep.tile([P, GROUPS, T], U32, name="zc", align_bytes=64)
        zs = keep.tile([P, GROUPS, T], U8, name="zs", align_bytes=64)
        xc = keep.tile([P, 2, T], U32, name="xc", align_bytes=64)
        xs = keep.tile([P, 2, T], U8, name="xs", align_bytes=64)
        xsc = keep.tile([P, 4, 8], F32, name="xsc")
        b_rows = keep.tile([P, 512], BF16, name="b_rows")
        b_cols = keep.tile([P, GROUPS, 4], BF16, name="b_cols")
        bd = keep.tile([P, K], BF16, name="bd")
        xin = [keep.tile([P, 2, K], U8, name="xin%d" % i) for i in range(2)]
        warm = keep.tile([P, 512], BF16, name="warm")
        early = keep.tile([P, 2], BF16, name="early")

        ctx.enter_context(tc.manual_schedule())

        make_identity(nc, ident[:])
        nc.vector.memset(warm[:], 0.0)
        nc.vector.memset(b_rows[:].bitcast(I32), 0)
        for plane in dsc:
            nc.vector.memset(plane[:].bitcast(I32), 0)

        def warm_up(bank):
            idle = psum.tile([P, 512], F32, name="idle", tag="bank%d" % bank)
            nc.tensor.matmul(idle[:], lhsT=warm[:, 0:P], rhs=warm[:], start=True, stop=True)

        xr = x_bytes.rearrange("(p i n) k -> i p n k", p=P, n=2)
        wr = w_enc.rearrange("(g m t) k -> g m t k", m=P, t=4)
        wq = w_enc.rearrange("(a r t) k -> t r a k", r=32, t=4)
        raw, vraw = {}, {}

        def load_w(f, count):
            raw[f] = work.tile([P, count, K], BF16, name="raw%d" % count, bufs=14)
            nc.sync.dma_start(out=raw[f][:], in_=wr[f // 4][:, f % 4 : f % 4 + count, :])

        def load_v(t):
            vraw[t] = keep.tile([P, 8, 256], BF16, name="vraw%d" % t)
            for q in (0, 2, 1, 3):
                nc.sync.dma_start(out=vraw[t][32 * q : 32 * (q + 1), :, :], in_=wq[t][:, 24:32, 256 * q : 256 * (q + 1)])

        def load_dec(g, count=1):
            nc.sync.dma_start(out=dw[:, g : g + count, :].bitcast(I32), in_=dec_words[g : g + count].rearrange("g p n -> p g n").bitcast(I32))

        def load_dec_scales(part):
            lo, hi = SCALE_PARTS[part]
            for r in range(4):
                nc.sync.dma_start(
                    out=dsc[part][r:P:32, :].bitcast(I32),
                    in_=dec_scales[lo:hi, r:16:4, :].rearrange("g q n -> q g n").bitcast(I32),
                )

        def deal(dst, src, on_vector=True):
            copy = nc.vector.tensor_copy if on_vector else nc.scalar.copy
            copy(out=dst.rearrange("p s (m j) -> p m s j", j=RUN), in_=src.rearrange("p (m s j) -> p m s j", s=4, j=RUN))

        def turn(rows, at):
            bank = psum.tile([P, 4, P], F32, name="turned", tag="bank%d" % at)
            for s in range(4):
                nc.tensor.transpose(bank[:, s, :], rows[:, s, :].bitcast(F32), ident[:])
            return bank

        def words_out(words, bank, on_vector):
            copy = nc.vector.tensor_copy if on_vector else nc.scalar.copy
            copy(out=words, in_=bank[:].rearrange("p (c u) r -> p c r u", u=2))

        xw, flat, xg, xbank = {}, {}, {}, {}

        def x_widen(n, on_vector):
            xw[n] = work.tile([P, 4, 256], BF16, name="xw", tag="laced", align_bytes=64, bufs=8)
            if not on_vector:
                flat[n] = work.tile([P, K], BF16, name="flat", tag="laced", align_bytes=64, bufs=8)
            for block in range(8):
                src = xin[n // 2][:, n % 2, B * block : B * (block + 1)].bitcast(FP8)
                s = xsc[:, n, block : block + 1]
                if on_vector:
                    dst = xw[n][:, :, 32 * block : 32 * (block + 1)].rearrange("p s (m j) -> p m s j", j=RUN)
                    nc.vector.tensor_scalar(out=dst, in0=src, scalar1=s, scalar2=None, op0=ALU.mult)
                else:
                    nc.scalar.activation(out=flat[n][:, B * block : B * (block + 1)], in_=src, func=ACT.Copy, scale=s)

        def x_turn(n, at):
            xbank[n] = turn(xw[n][:], at)

        def x_out(n, on_vector=False):
            if n // 2 not in xg:
                xg[n // 2] = work.tile([P, 2, 2, P, 4], BF16, name="xg", align_bytes=64)
            words = xg[n // 2][:].rearrange("p c i r t -> p c i (r t)").bitcast(F32)[:, :, n % 2, :]
            words_out(words.rearrange("p c (r u) -> p c r u", u=2), xbank[n], on_vector)

        def x_quant(half):
            cols = slice(HALF * half, HALF * (half + 1))
            for c in range(2):
                nc.vector.quantize_mx(
                    out=xc[:, c, cols].bitcast(FP8X4),
                    scales=xs[:, c, cols],
                    in_=xg[half][:, c, :, :, :].rearrange("p i r t -> p (i r t)"),
                )

        dealt, wbank, wg, wc, ws, vsort, vturn = {}, {}, {}, {}, {}, {}, {}

        def w_deal(f, count=2, on_vector=True):
            rows = work.tile([P, 4, count * 256], BF16, name="dealt", bufs=4)
            deal(rows[:], raw[f][:].rearrange("p i k -> p (i k)"), on_vector)
            for i in range(count):
                dealt[f + i] = rows[:, :, 256 * i : 256 * (i + 1)]

        def w_turn(f, at):
            wbank[f] = turn(dealt[f], at)

        def pair_of(f):
            return {26: (13, 0), 30: (13, 1), 27: (15, 0), 31: (15, 1)}.get(f, divmod(f, 2))

        def laid(f):
            j, i = pair_of(f)
            if j not in wg:
                wg[j] = work.tile([P, 2, 2, P, 4], BF16, name="wg", align_bytes=64, bufs=4)
            return wg[j][:, i, :, :, :].rearrange("p c r t -> p (c r t)").bitcast(F32)

        def w_out(f, on_vector=False):
            words_out(laid(f).rearrange("p (c r u) -> p c r u", c=2, u=2), wbank[f], on_vector)

        def v_deal(t):
            vsort[t] = work.tile([P, 4, 512], BF16, name="vsort", align_bytes=64, bufs=1)
            deal(vsort[t][:], vraw[t][:].rearrange("p a k -> p (a k)"))

        def v_turn(t):
            vturn[t] = work.tile([P, 1024], F32, name="vturn", align_bytes=64, bufs=1)
            nc.vector.transpose(out=vturn[t][:], in_=vsort[t][:].rearrange("p s k -> p (s k)").bitcast(F32))

        def v_out(t):
            laid(24 + t)
            words = wg[pair_of(24 + t)[0]][:].rearrange("p i c r t -> p (i c r t)").bitcast(F32)
            nc.vector.tensor_copy(
                out=words.rearrange("p (i c m u) -> p i c m u", i=2, c=2, u=2),
                in_=vturn[t][:].rearrange("p (c u i m) -> p i c m u", c=2, u=2, i=2),
            )

        def w_quant(f, count):
            j, i = pair_of(f)
            if i == 0:
                wc[j] = work.tile([P, 2, 2, P], U32, name="wc", align_bytes=64, bufs=6)
                ws[j] = work.tile([P, 2, 2, P], U8, name="ws", align_bytes=64, bufs=6)
            part = slice(i, i + count)
            nc.vector.quantize_mx(
                out=wc[j][:, part, :, :].rearrange("p i c r -> p (i c r)").bitcast(FP8X4),
                scales=ws[j][:, part, :, :].rearrange("p i c r -> p (i c r)"),
                in_=wg[j][:, part, :, :, :].rearrange("p i c r t -> p (i c r t)"),
            )

        pre, zt, zi, acc = {}, {}, {}, {}

        def encode(f, at, cols=slice(0, T)):
            if f not in pre:
                pre[f] = psum.tile([P, T], F32, name="pre", tag="bank%d" % at)
            j, i = pair_of(f)
            for c in range(2):
                nc.tensor.matmul_mx(
                    out=pre[f][:, cols],
                    lhsT=wc[j][:, i, c, :].bitcast(FP8X4),
                    lhsT_scale=ws[j][:, i, c, :],
                    rhs=xc[:, c, cols].bitcast(FP8X4),
                    rhs_scale=xs[:, c, cols],
                    start=(c == 0),
                    stop=(c == 1),
                )

        def relu_out(f):
            g, t = divmod(f, 4)
            if g not in zt:
                zt[g] = work.tile([P, 4, T], BF16, name="zt", tag="zt", bufs=GROUPS)
            nc.scalar.activation(out=zt[g][:, t, :], in_=pre[f][:], func=ACT.Relu, bias=b_cols[:, g, t : t + 1], scale=1.0)

        def z_lace(g, n, count=1, on_vector=True, into=None):
            first = n if into is None else into
            if (g, first) not in zi:
                zi[g, first] = work.tile([P, (count if into is None else 2) * P, 4], BF16, name="zi", tag="laced", align_bytes=64, bufs=8)
            copy = nc.vector.tensor_copy if on_vector else nc.scalar.copy
            copy(
                out=zi[g, first][:, P * (n - first) : P * (n - first + count), :].rearrange("p (c i) t -> p c t i", i=4),
                in_=zt[g][:, :, P * n : P * (n + count)].rearrange("p t (c i) -> p c t i", i=4),
            )

        def z_quant(g, n, count=1):
            cols = slice(P * n, P * (n + count))
            nc.vector.quantize_mx(
                out=zc[:, g, cols].bitcast(FP8X4),
                scales=zs[:, g, cols],
                in_=zi[g, n][:].rearrange("p n t -> p (n t)"),
            )

        orows = out.rearrange("(p n) k -> n p k", p=P)

        def decode_cols(bank, n, g, lo, width):
            part = g // 4
            at = K * (g - SCALE_PARTS[part][0]) + lo
            nc.tensor.matmul_mx(
                out=bank[:, 0:width],
                lhsT=zc[:, g, P * n : P * (n + 1)].bitcast(FP8X4),
                lhsT_scale=zs[:, g, P * n : P * (n + 1)],
                rhs=dw[:, g, 2 * lo : 2 * (lo + width)].bitcast(FP4X4),
                rhs_scale=dsc[part][:, at : at + width],
                start=(g == 0),
                stop=(g == last),
            )

        def store_cols(bank, n, lo, width):
            o = work.tile([P, width], F32, name="o", tag="zt", bufs=GROUPS)
            cols = slice(lo, lo + width)
            nc.vector.tensor_tensor(out=o[:], in0=bank[:, 0:width], in1=bd[:, cols], op=ALU.add)
            nc.sync.dma_start(out=orows[n][:, cols], in_=o[:])

        def decode(n, g, h, at=None):
            if g == 0:
                acc[n, h] = psum.tile([P, 512], F32, name="acc", tag="bank%d" % at)
            decode_cols(acc[n, h], n, g, 512 * h, 512)

        def store(n, h):
            store_cols(acc[n, h], n, 512 * h, 512)

        nc.scalar.dma_start(out=xsc[:], in_=x_scale.rearrange("(p n) b -> p n b", p=P))
        nc.scalar.activation(out=early[:], in_=warm[:, 0:2], func=ACT.Copy)
        for i in range(2):
            nc.sync.dma_start(out=xin[i][:], in_=xr[i])
        nc.sync.dma_start(out=b_rows[0:GROUPS, :], in_=b_enc.rearrange("(g k) -> g k", g=GROUPS))
        for f in range(0, 22, 2):
            load_w(f, 2)
        load_dec(0)
        load_dec_scales(0)
        load_w(22, 2)
        load_w(24, 2)
        load_w(28, 2)
        load_dec(1, 2)
        load_v(3)
        load_dec(3, 2)
        load_v(2)
        load_dec_scales(1)
        load_dec(5)
        load_dec(6, 2)
        nc.sync.dma_start(out=bd[:], in_=b_dec.partition_broadcast(P))

        for i in range(5):
            warm_up(3 + i)
        b_bank = psum.tile([P, 2, P], F32, name="b_bank", tag="bank4")
        for u in range(2):
            nc.tensor.transpose(b_bank[:, u, :], b_rows[:].bitcast(F32)[:, u : 2 * P : 2], ident[:])
        x_widen(0, True)
        x_widen(1, False)
        x_widen(2, True)
        deal(xw[1][:], flat[1][:])
        w_deal(0)
        x_widen(3, True)
        nc.scalar.copy(out=b_cols[:].bitcast(F32), in_=b_bank[:, :, 0:GROUPS].rearrange("p u g -> p g u"))
        x_turn(0, 0)
        x_out(0)
        x_turn(2, 1)
        x_out(2)
        x_turn(1, 2)
        x_out(1)
        warm_up(5)
        w_turn(0, 6)
        w_turn(1, 7)
        x_turn(3, 3)
        w_deal(2)
        w_turn(2, 4)
        w_turn(3, 5)
        x_quant(0)
        w_out(0)
        w_out(1)
        x_out(3)
        w_quant(0, 1)
        w_quant(1, 1)
        w_out(2)
        w_out(3)
        encode(0, 6, slice(0, HALF))
        encode(1, 7, slice(0, HALF))
        w_deal(4)
        w_turn(4, 0)
        w_turn(5, 1)
        x_quant(1)
        encode(0, 6, slice(HALF, T))
        encode(1, 7, slice(HALF, T))
        w_deal(6)
        w_quant(2, 2)
        w_out(4)
        w_out(5)
        relu_out(0)
        relu_out(1)

        def turns(tiles, banks):
            for f, at in zip(tiles, banks):
                w_turn(f, at)

        def encodes(tiles, banks):
            for f, at in zip(tiles, banks):
                encode(f, at)
                relu_out(f)

        def both(n, g, at=None):
            for h in range(2):
                decode(n, g, h, None if at is None else at[h])

        turns((6, 7), (2, 3))
        w_deal(8)
        w_quant(4, 2)
        w_out(6, True)
        w_out(7)
        w_deal(10)
        w_deal(12)
        encodes(range(2, 6), (4, 5, 0, 1))
        turns(range(8, 12), (6, 7, 2, 4))
        w_deal(14)
        w_quant(6, 2)
        turns(range(12, 16), (3, 0, 5, 1))
        for f in (8, 9, 12):
            w_out(f, True)
        for f in (10, 11, 13, 14, 15):
            w_out(f)
        w_quant(8, 2)
        w_quant(10, 2)
        w_deal(16)
        w_quant(12, 2)
        w_deal(18)
        w_deal(20)
        w_quant(14, 2)
        z_lace(0, 0)
        encodes(range(6, 14), (6, 7, 3, 4, 2, 5, 0, 1))
        turns(range(16, 22), (6, 7, 3, 4, 2, 5))
        z_lace(1, 0)
        z_quant(0, 0)
        for f in range(16, 22):
            w_out(f, f < 18)
        z_quant(1, 0)
        w_quant(16, 2)
        w_deal(22)
        w_deal(24)
        w_quant(18, 2)
        z_lace(2, 0)
        w_deal(28)
        z_quant(2, 0)
        w_quant(20, 2)
        encodes((14, 15), (6, 7))
        both(0, 0, (0, 3))
        encodes(range(16, 20), (1, 2, 4, 5))
        both(0, 1)
        z_lace(0, 1, 2)
        z_lace(3, 0)
        turns((22, 23, 24, 25, 28, 29), (6, 7, 1, 2, 4, 5))
        for f in (22, 23, 24, 25, 28, 29):
            w_out(f, f < 24)
        z_quant(0, 1, 2)
        z_quant(3, 0)
        w_quant(22, 2)
        z_lace(1, 1, 2)
        w_quant(24, 2)
        z_quant(1, 1, 2)
        w_quant(28, 2)
        v_deal(3)
        z_lace(4, 0)
        v_turn(3)
        both(0, 2)
        encodes((20, 21, 22, 23, 24, 25), (6, 1, 7, 4, 2, 5))
        both(0, 3)

        def feature(f, at):
            encode(f, at)
            relu_out(f)

        z_quant(4, 0)
        v_out(3)
        v_deal(2)
        z_lace(2, 1, 2, False)
        w_quant(27, 2)
        z_quant(2, 1, 2)
        v_turn(2)
        both(1, 0, (6, 1))
        both(2, 0, (7, 4))
        feature(28, 2)
        z_lace(3, 1, 1, False, 1)
        both(1, 1)
        feature(29, 5)
        z_lace(3, 2, 1, False, 1)
        z_lace(5, 0, 1, False)
        z_quant(3, 1, 2)
        v_out(2)
        z_quant(5, 0)
        w_quant(26, 2)
        z_lace(4, 1, 2)
        both(2, 1)
        both(0, 4)
        feature(27, 2)
        both(1, 2)
        feature(31, 5)
        z_lace(5, 1, 2, False)
        both(2, 2)
        both(1, 3)
        both(0, 5)
        feature(26, 2)
        feature(30, 5)
        both(2, 3)
        z_lace(0, 3)
        z_quant(4, 1, 2)
        z_lace(1, 3)
        z_quant(5, 1, 2)
        z_lace(6, 0, 2)
        z_lace(7, 0, 2)
        z_quant(6, 0, 2)
        z_lace(6, 2, 2, False)
        z_lace(7, 2, 2, False)
        z_quant(7, 0, 2)
        z_quant(0, 3)
        z_quant(1, 3)
        z_lace(2, 3)
        z_quant(6, 2, 2)
        z_quant(2, 3)
        both(1, 4)
        both(2, 4)
        both(1, 5)
        both(2, 5)
        both(0, 6)
        both(0, 7)
        both(1, 6)
        both(1, 7)
        for g in range(3, 6):
            z_lace(g, 3, 1, False)
        store(0, 0)
        z_quant(7, 2, 2)
        store(0, 1)
        z_quant(3, 3)
        store(1, 0)
        z_quant(4, 3)
        z_quant(5, 3)
        store(1, 1)
        both(2, 6)
        both(2, 7)
        store(2, 0)
        store(2, 1)
        for g in range(GROUPS):
            decode(3, g, 0, 2)
        store(3, 0)
        for lo, width, at in ((512, 256, 5), (768, P, 0), (896, P, 3)):
            piece = psum.tile([P, 512], F32, name="piece", tag="bank%d" % at)
            for g in range(GROUPS):
                decode_cols(piece, 3, g, lo, width)
            store_cols(piece, 3, lo, width)
